import numpy as np, ml_dtypes
CORES = [16,17,18,19,32,33,34,35]
N = 8
BF = ml_dtypes.bfloat16
V, C, S, IT, Q, RO, D = 2560, 256, 128, 3, 6, 2, 2048
P = V + 2 * C * RO
def mesh(rng, m, isb, chain):
    o = rng.permutation(V); x = np.zeros(3 * V, np.int64); sn = np.zeros(2 * S, np.int64); rest = V - 2 * m
    x[2 * V + o[0:2 * m:2]] = o[1:2 * m:2]; x[2 * V + o[1:2 * m:2]] = o[0:2 * m:2]
    up = 2 * V + o[2 * m:]; leg = rng.integers(0, 2, rest) * V + o[:rest] if chain else rng.permutation(2 * V)[:rest]
    left = np.ones(2 * V, bool); left[leg] = False
    jb, jl = np.flatnonzero(isb), np.flatnonzero(~isb); c = rng.permutation(rest); cut, keep = c[:len(jb)], c[len(jb):]
    x[up[keep]] = leg[keep] % V; x[leg[keep]] = up[keep] - 2 * V
    x[up[cut]] = P + jb; sn[jb] = up[cut] - 2 * V
    pool = np.concatenate([rng.permutation(leg[cut]), rng.permutation(np.flatnonzero(left))]); h = rng.permutation(pool[:len(jl)])
    x[h] = P + jl; sn[jl] = h % V
    k = rng.permutation(pool[len(jl):]).reshape(2, -1); x[k[0]] = k[1] % V; x[k[1]] = k[0] % V
    return x.reshape(3, V), sn, o
def meshes(rng, m, chain=False):
    x = rng.choice(4, (N, 8, S), p=[0.35, 0.35, 0.2, 0.1])
    isb = np.concatenate([np.roll((x == 1) | (x == 3), 1, axis=0), (x == 0) | (x == 3)], axis=2)
    z = [[mesh(rng, int(m[a, g]), isb[a, g], chain) for g in range(8)] for a in range(N)]
    return tuple(np.stack([np.stack([u[i] for u in row]) for row in z]) for i in range(3))
def levels(rng):
    return rng.permuted(np.tile(np.array([60, 90, 110, 130, 150, 165, 180, 200]), (N, 1)), axis=1)[:, :, None, None] + rng.integers(-20, 21, (N, 8, 16, 1))
def errors(rng):
    return (256 * (0.25 + 0.75 * rng.random((N, 8, 1, V))) * rng.random((N, 8, 16, V))).astype(np.int64)
def under(rng, th):
    return np.minimum((th * rng.random((N, 8, 16, V))).astype(np.int64), th - 1)
def plant(rng, e, t, x, y, cnt):
    on = np.argsort(rng.random((16, len(x))), axis=0) < cnt[None, :]; one = rng.random(on.shape) < 0.5
    v = np.where(rng.random(on.shape) < 0.5, t, np.minimum(t + (rng.random(on.shape) * (256 - t)).astype(np.int64), 255))
    e[:, x] = np.where(on & one, v, e[:, x]); e[:, y] = np.where(on & ~one, v, e[:, y])
def more(rng):
    return rng.integers(0, 256, (N, 8, 16, D)), rng.integers(0, 256, (N, 8, 16, 1))
def pack(err, p, sn, det, wt, th):
    b = lambda a: np.ascontiguousarray(a.reshape(N, 128, -1)).astype(np.float32).astype(BF)
    i = lambda a: np.ascontiguousarray(a).astype(np.int32)
    return {"err": b(err), "lt": i(p[:, :, 0]), "rt": i(p[:, :, 1]), "bs": i(p[:, :, 2]), "snd": i(sn), "det": b(det), "wt": i(wt.reshape(N, 128, 1)), "th": i(th.reshape(N, 128, 1))}
def setup_inputs(rng):
    p, sn, o = meshes(rng, rng.integers(V // 8, V // 3 + 1, (N, 8))); det, wt = more(rng)
    return pack(errors(rng), p, sn, det, wt, levels(rng))
def setup_inputs_room(rng):
    M = V // 3; p, sn, o = meshes(rng, np.full((N, 8), M)); det, wt = more(rng)
    th = np.repeat(rng.integers(64, 192, (1, 8, 16, 1)), N, axis=0); err = under(rng, th)
    for a in range(N):
        for g in range(8):
            n = (C, C + 1, 0, 1, C - 1, M, C, C + 1)[(a + g) % 8]
            plant(rng, err[a, g], th[a, g], o[a, g, 0:2 * M:2], o[a, g, 1:2 * M:2], np.where(rng.permutation(M) < n, Q, Q - 1))
    return pack(err, p, sn, det, wt, th)
def setup_inputs_chain(rng):
    M = V // (2 * (IT + 3)); p, sn, o = meshes(rng, np.full((N, 8), M), True); det, wt = more(rng)
    th = np.repeat(rng.integers(64, 192, (1, 8, 16, 1)), N, axis=0); err = under(rng, th); far = np.array([0, 1, IT - 1, IT, IT, IT + 1, IT + 1])
    for a in range(N):
        for g in range(8):
            i = 2 * np.arange(M) + 2 * M * rng.permuted(np.resize(far, M))
            plant(rng, err[a, g], th[a, g], o[a, g, i], o[a, g, i + 1], np.where(rng.random(M) < 0.8, Q, Q - 1))
    return pack(err, p, sn, det, wt, th)
def setup_inputs_ties(rng):
    p, sn, o = meshes(rng, rng.integers(V // 8, V // 3 + 1, (N, 8))); det, wt = more(rng)
    th = np.clip(np.array([1, 2, 100, 128, 254, 255, 255, 30])[None, :, None, None] + rng.integers(-1, 2, (N, 8, 16, 1)), 1, 255); th[:, 6] = 255
    err = np.clip(th - 1 + (rng.random((N, 8, 16, V)) < 0.5 * rng.random((N, 8, 1, V))) * rng.integers(1, 3, (N, 8, 16, V)), 0, 255)
    err[:, 6] = np.minimum(err[:, 6], 254); err[:, 7] = 255
    det[:, 1] = 255; det[:, 2] = 0; wt[:, 0] = 0; wt[:, 1] = 255
    return pack(err, p, sn, det, wt, th)
def pools(rng):
    return [[int(z) for z in rng.permutation(V)] for a in range(N)], rng.permutation(S)[:8 * N].reshape(N, 2, 4)
def watch(x, leg, u, v, slot):
    x[leg, u] = P + slot; x[1 - leg, u] = v; x[2, u] = v; x[:, v] = u
def renamed(rng, x, sn, e):
    pool, kk = pools(rng)
    for a in range(N):
        for s in range(2):
            k, k2, kb, kb2 = [int(z) for z in kk[a, s]]; q, z = (a + 2 * s - 1) % N, (a - 2 * s + 1) % N
            t, b = pool[a].pop(), pool[a].pop()
            x[a, 2, t] = b; x[a, 2, b] = t; x[a, 0, t] = P + (1 - s) * S + k2; x[a, 1, t] = P + s * S + k; e[a, :, t] = 255
            sn[a, s * S + k] = t; sn[a, (1 - s) * S + k] = t
            u, v = pool[q].pop(), pool[q].pop(); sn[q, (1 - s) * S + k] = u; watch(x[q], s, u, v, (1 - s) * S + k)
            u, v = pool[z].pop(), pool[z].pop(); sn[z, s * S + k2] = u; watch(x[z], 1 - s, u, v, s * S + k)
            t, b = pool[a].pop(), pool[a].pop()
            x[a, 2, t] = b; x[a, 2, b] = t; x[a, 0, t] = P + s * S + kb2; e[a, :, t] = 255
            x[a, 1, t] = (P + s * S + kb) % (2 * S) + 2 * S * int(rng.integers(0, V // (2 * S))); sn[a, s * S + kb] = t
            u, v = pool[q].pop(), pool[q].pop(); sn[q, (1 - s) * S + kb2] = u; watch(x[q], s, u, v, (1 - s) * S + kb)
def allpairs(rng, x, e):
    for a in range(N):
        pr = np.sort(rng.permutation(V).reshape(-1, 2), axis=1); pr = pr[np.argsort(pr[:, 0])]
        x[a, 0, pr[0::2]] = pr[1::2]; x[a, 0, pr[1::2]] = pr[0::2]
        for i in (1, 2):
            x[a, i, pr[:, 0]] = pr[:, 1]; x[a, i, pr[:, 1]] = pr[:, 0]
        e[a][:, pr[len(pr) - C // 2:].reshape(-1)] = 255
def crowded(rng, x, sn, e):
    pool, kk = pools(rng)
    for a in range(N):
        for s in range(2):
            q = (a + 2 * s - 1) % N
            for i in range(2):
                k, kn = int(kk[a, s, 2 * i]), int(kk[a, s, 2 * i + 1]); many = [pool[a].pop() for z in range(V // 16)]
                x[a, 2, np.array(many)] = P + s * S + kn
                t = max(many) if i == 0 else min(many); e[a, :, t] = 255; sn[a, s * S + k] = t
                u, v = pool[q].pop(), pool[q].pop(); sn[q, (1 - s) * S + kn] = u; watch(x[q], 1 - i, u, v, (1 - s) * S + k)
def newbases(rng, x, sn, e, th):
    pool, kk = pools(rng)
    for a in range(N):
        pr = np.sort(np.array(pool[a][:2 * S]).reshape(S, 2), axis=1); pr = pr[np.argsort(pr[:, 0])]
        x[a, 2, pr[:, 0]] = pr[:, 1]; x[a, 2, pr[:, 1]] = pr[:, 0]
        plant(rng, e[a], th[a], pr[:, 0], pr[:, 1], rng.integers(Q, 17, S))
        for s in range(2):
            q = (a + 2 * s - 1) % N
            for i in range(2):
                k, kn = int(kk[a, s, 2 * i]), int(kk[a, s, 2 * i + 1]); j = (s * S + kn + P - V) % (2 * S)
                y = int(pr[j // 2, j % 2]); w = pool[a].pop()
                x[a, :, w] = y; x[a, 1, y] = w; e[a, :, w] = 255; sn[a, s * S + k] = w
                u, v = pool[q].pop(), pool[q].pop(); sn[q, (1 - s) * S + kn] = u; watch(x[q], i, u, v, (1 - s) * S + k)
def setup_inputs_free(rng):
    p = rng.choice(np.concatenate([np.arange(V), P + np.arange(2 * S)]), (N, 8, 3, V)); sn = rng.integers(0, V, (N, 8, 2 * S)); m = V // 4
    det, wt = more(rng); err = errors(rng); th = levels(rng)
    for a in range(N):
        for g in range(0, 8, 2):
            o = rng.permutation(V); x = p[a, g]; x[2, o[0:2 * m:2]] = o[1:2 * m:2]; x[2, o[1:2 * m:2]] = o[0:2 * m:2]
            v = o[2 * m:]; v = v[x[2, v] < V]; x[rng.integers(0, 2, len(v)), x[2, v]] = v
            x[0, o[:40]] = o[:40]; x[1, o[20:60]] = o[20:60]; x[0, o[100:140]] = x[1, o[100:140]]; x[1, o[200:240:2]] = o[201:240:2]
            j = rng.permutation(2 * S)[:S // 2]; x[1, sn[a, g, j]] = P + j
    for a in range(N):
        for g in range(0, 8, 2):
            for s in range(2):
                q = (a + 2 * s - 1) % N; k = rng.integers(0, S, 32); k2 = rng.integers(0, S, 32)
                p[q, g, 2, sn[q, g, (1 - s) * S + k]] = P + (1 - s) * S + k2
                p[a, g, rng.integers(0, 2, 32), sn[a, g, s * S + k2]] = P + s * S + k
    p[:, 0, 2, 0] = V - 1; p[:, 0, 2, V - 1] = 0; err[:, 0, :, 0] = 255; err[:, 0, :, V - 1] = 255
    n = 16; me = np.arange(V); two, lone = {}, {}
    for a in range(N):
        for g in range(0, 8, 2):
            x = p[a, g]
            b = np.minimum(x[2], V - 1); pair = (x[2] < V) & (x[2, b] == me) & (b != me)
            t = rng.permutation(np.flatnonzero(pair & (me < b) & (me > 0)))
            two[a, g] = rng.permuted(np.stack([t[:2 * n], b[t[:2 * n]]]), axis=0)
            lone[a, g] = rng.permutation(np.flatnonzero(~pair & (me > 0) & (me < V - 1)))[:2 * n]
            cut = t[C - 4 * n:]; x[2, cut] = P + rng.integers(0, 2 * S, len(cut))
    for g in range(0, 8, 2):
        k, k2 = rng.permutation(S)[:2 * n].reshape(2, n)
        for a in range(N):
            for s in range(2):
                q = (a + 2 * s - 1) % N; u, v = two[a, g][:, s * n:(s + 1) * n]; w = lone[q, g][(1 - s) * n:(2 - s) * n]
                sn[a, g, s * S + k2] = u; sn[q, g, (1 - s) * S + k] = w
                x = p[a, g]; x[0, u] = P + s * S + k; x[1, u] = v; x[0, v] = u; x[1, v] = u
                p[q, g, 2, w] = np.where(np.arange(n) < n // 2, P + s * S + k2, (P + k2) % S + S * rng.integers(0, V // S, n))
                e = err[a, g]; c = np.concatenate([u, v]); e[:, c] = np.minimum(e[:, c], th[a, g] - 1)
                plant(rng, err[q, g], th[a, g], w, w, rng.integers(Q, 17, n))
    th[:, 1::2] = rng.integers(20, 121, (N, 4, 16, 1)); err[:, 1::2] = under(rng, th)[:, 1::2]
    p[:, 1::2, 2] = P + rng.integers(0, 2 * S, (N, 4, V)); p[:, 5] = P + rng.integers(0, 2 * S, (N, 3, V))
    sn[:, 5] = rng.choice(np.array([0, V - 1, V // 2, 5]), (N, 2 * S))
    renamed(rng, p[:, 1], sn[:, 1], err[:, 1]); allpairs(rng, p[:, 3], err[:, 3])
    crowded(rng, p[:, 5], sn[:, 5], err[:, 5]); newbases(rng, p[:, 7], sn[:, 7], err[:, 7], th[:, 7])
    return pack(err, p, sn, det, wt, th)
def setup_inputs_spread(rng):
    p, sn, o = meshes(rng, rng.integers(V // 8, V // 3 + 1, (N, 8)))
    err = (np.exp2(8 * rng.random((N, 8, 1, V))) * rng.random((N, 8, 16, V))).astype(np.int64)
    det = (np.exp2(8 * rng.random((N, 8, 1, D))) * rng.random((N, 8, 16, D))).astype(np.int64)
    wt = np.minimum(np.exp2(8 * rng.random((N, 8, 16, 1))).astype(np.int64), 255)
    th = np.clip(np.exp2(3 + 5 * rng.random((N, 8, 1, 1)) + rng.random((N, 8, 16, 1)) - 0.5).astype(np.int64), 1, 255)
    return pack(np.minimum(err, 255), p, sn, np.minimum(det, 255), wt, th)
def check_inputs(d):
    bad = []
    for k in ("err", "det"):
        x = np.asarray(d[k]).astype(np.float32)
        if not np.all((x >= 0) & (x <= 255) & (x == np.floor(x))): bad.append("range of " + k)
    for k in ("lt", "rt", "bs"):
        x = d[k]
        if not np.all(((x >= 0) & (x < V)) | ((x >= P) & (x < P + 2 * S))): bad.append("range of " + k)
    for k, lo, hi in (("snd", 0, V - 1), ("wt", 0, 255), ("th", 1, 255)):
        if np.min(d[k]) < lo or np.max(d[k]) > hi: bad.append("range of " + k)
    return bad
def ghosts(x):
    return np.concatenate([np.roll(x[..., S:], 1, axis=0), np.roll(x[..., :S], -1, axis=0)], axis=-1)
def reference(err, lt, rt, bs, snd, det, wt, th):
    take = np.take_along_axis; me = np.arange(P)
    e = np.zeros((N, 8, 16, P), np.int32); e[..., :V] = err.astype(np.float32).astype(np.int32).reshape(N, 8, 16, V)
    dt = det.astype(np.float32).astype(np.int32).reshape(N, 8, 16, D); wq = wt.astype(np.int32).reshape(N, 8, 16, 1); tq = th.astype(np.int32).reshape(N, 8, 16, 1)
    p = np.zeros((N, 8, 3, P), np.int64) + me
    p[:, :, 0, :V] = lt; p[:, :, 1, :V] = rt; p[:, :, 2, :V] = bs
    sn = snd.astype(np.int64)
    lo = np.repeat(np.array([0, S]), S); off = np.repeat(np.array([-S, S]), S)
    for t in range(RO):
        L, R, B = p[:, :, 0], p[:, :, 1], p[:, :, 2]
        j = ghosts(take(B, sn, 2)) - P + off
        gb = np.where((j >= lo) & (j < lo + S), take(sn, np.clip(j, 0, 2 * S - 1), 2), -1)
        base = np.concatenate([B, gb], axis=2); gl = (take(base, L, 2) == me)[:, :, None]; gr = (take(base, R, 2) == me)[:, :, None]
        W = e
        for it in range(IT):
            A = np.concatenate([W, ghosts(take(W, sn[:, :, None], 3))], axis=3)
            W = np.maximum(W, np.maximum(np.where(gl, take(A, L[:, :, None], 3), 0), np.where(gr, take(A, R[:, :, None], 3), 0)))
        bo = np.minimum(B, P - 1); pair = (B < P) & (take(B, bo, 2) == me) & (me < B)
        rows = np.add.reduce((np.maximum(W, take(W, bo[:, :, None], 3)) >= tq).astype(np.int32), axis=2)
        go = (pair & (rows >= Q)).astype(np.int64); k = np.add.accumulate(go, axis=2) - go
        a, g, x = np.nonzero((go == 1) & (k < C)); y = B[a, g, x]
        new = np.zeros((N, 8, P), np.int64)
        new[a, g, x] = V + 2 * C * t + 2 * k[a, g, x]; new[a, g, y] = new[a, g, x] + 1
        nx = np.concatenate([new, np.zeros((N, 8, 2 * S), np.int64)], axis=2); rx = np.concatenate([R, np.full((N, 8, 2 * S), -1)], axis=2)
        pn = np.stack([np.where((take(nx, T, 2) > 0) & (take(rx, T, 2) == me), take(nx, T, 2), T) for T in (L, R, B)], axis=2)
        sn = np.where((take(new, sn, 2) > 0) & (take(R, sn, 2) == P + np.arange(2 * S)), take(new, sn, 2), sn)
        a = np.concatenate([a, a]); g = np.concatenate([g, g]); s = np.concatenate([x, y]); o = np.concatenate([y, x])
        n, m = new[a, g, s], new[a, g, o]; bl, br = pn[a, g, 0, s], pn[a, g, 1, s]
        pn[a, g, 0, s] = n; pn[a, g, 1, s] = m; pn[a, g, 2, s] = bl
        pn[a, g, 0, n] = o; pn[a, g, 1, n] = s; pn[a, g, 2, n] = br
        p = pn
        es = e[a, g, :, s]; h = np.add.reduce(wq * e, axis=2)[a, g, s]
        for place in (s, n):
            e[a, g, :, place] = (es >> 1) + (dt[a, g, :, (h + place) & (D - 1)] >> 1)
    return {"ye": e.reshape(N, 128, P).astype(np.float32).astype(BF), "yl": p[:, :, 0].astype(np.float32), "yr": p[:, :, 1].astype(np.float32), "yb": p[:, :, 2].astype(np.float32)}

@@ -1,0 +1,645 @@
+import numpy as np
+from concourse.bass import DstId, RemoteDMATransfer
+from concourse.mybir import AluOpType as A, ActivationFunctionType as F
+
+NR, P0, GH = 8, 2560, 3584
+CP = F.Copy
+W0 = 272
+BIG = 16384.0
+_bf = {"hi": 672, "lo": 672, "shi": 16, "slo": 16, "ihi": 224, "ilo": 224, "chi": 224, "clo": 224,
+       "ev": 4112, "eu": 3856, "wa": 3344, "wb": 3344, "tb": 3840, "tc": 3840, "nt0": 3840, "nt1": 3840,
+       "gl": 3072, "gr": 3072, "gb": 3072, "hb": 3072, "ec": 3072, "cv": 3072, "vf": 3072, "ct": 3328, "snf": 272,
+       "zz": 2048, "zb": 2048, "zr": 2048, "zi": 2048, "zl": 2048, "zh": 2048, "bo": 128, "ltm": 128, "dr": 2048, "dh": 2064,
+       "gh1": 256, "gl1": 256, "gi": 256, "zero": 192, "gs": 256, "gsb": 256, "gx": 512, "gt": 256, "gq": 512, "gy": 512, "gn": 512, "gsn": 256,
+       "rl": 192, "rr": 192, "rb": 192, "eq": 192, "hot": 192, "cum": 192, "sel": 192, "n0": 192, "n1": 192, "nchi": 192, "nclo": 192, "sc": 192,
+       "eg": 512, "dg": 1024, "cl": 512, "cr": 512, "x0": 256, "x1": 256, "x2": 256}
+_f32 = {"px": 672, "sn": 16, "df": 2048, "ci": 8, "i8": 8, "mk2": 8, "mk": 16, "i16": 16, "cc": 224, "me": 224, "ix": 224, "ixm": 192,
+        "xs": 16, "gv": 256, "bes": 16, "bel0": 16, "bel1": 16, "gm": 16, "gd": 16, "gm1": 8, "srf": 16, "sw": 16, "xv": 32, "xf": 32,
+        "vl": 192, "lf": 192, "vr": 192, "rf": 192, "bf": 192, "pt": 192, "thr": 192, "k1": 192, "nt": 192, "kn": 192, "dd": 192, "nc": 192,
+        "st": 192, "spl": 192, "no": 192, "nb": 192, "m8": 192, "wq": 192, "wr": 192, "fl": 32, "fo": 32, "tv": 32, "pv": 32, "rq": 32,
+        "rn": 32, "nw": 96, "dq": 64, "scf": 32}
+_i32 = {"xin": 480, "sin": 16, "win": 2, "pid": 4, "di": 64, "da": 64, "e2": 512}
+_u16 = {"lv": 192, "rv": 192, "bv": 192, "lw": 192, "rw": 192, "bw": 192, "snu": 16, "slu": 32, "siu": 16, "gbu": 16, "xlu": 32,
+        "tu16": 16, "tu": 32, "yu": 32, "du": 64, "scu": 32, "pd": 192}
+SCRATCH, AL, _o = {}, {}, 0
+for _k in list(_f32):
+    if _f32[_k] <= 192 and _k not in ("i16", "xs", "bes", "bel0", "bel1"):
+        AL[_k] = (_o, _f32[_k])
+        _o += (_f32.pop(_k) + 3) // 4 * 4
+_f32["pf"] = _o
+for _s, _d in ((_bf, "bfloat16"), (_f32, "float32"), (_i32, "int32"), (_u16, "uint16")):
+    for _k in _s:
+        SCRATCH[_k] = ("sbuf", [128, _s[_k]], _d)
+for _k in range(8):
+    SCRATCH["ps%d" % _k] = ("psum", [128, 512], "float32")
+_KINDS = ["be", "x0", "x1", "x2"]
+NDMA = 110
+SEMAPHORES = ["qv", "qs", "qt", "qg"] + ["a%s%d" % (k, t) for k in _KINDS for t in range(2)] + \
+             ["l%s%d" % (k, t) for k in _KINDS for t in range(2)] + ["d%d" % k for k in range(NDMA)]
+
+
+def tracker(g, T):
+    Q = {"v": g.vector, "s": g.scalar, "t": g.tensor, "g": g, "y": g.sync}
+    acc, known, snap, cnt, top = {}, {q: {} for q in Q}, {}, {q: 0 for q in Q}, {}
+    nd = [0]
+
+    def hit(x, y):
+        if x[1] >= y[2] or y[1] >= x[2]:
+            return False
+        if x[3] > 1 and x[3] == y[3] and (x[1] - y[1]) % x[3]:
+            return False
+        return x[4] is None or y[4] is None or x[4] == y[4]
+
+    def wait(q, sem, val):
+        if known[q].get(sem, 0) >= val:
+            return
+        Q[q].wait_ge(T.sem[sem], val)
+        for s, v in snap.get((sem, val), {}).items():
+            if known[q].get(s, 0) < v:
+                known[q][s] = v
+        known[q][sem] = val
+
+    def deps(q, reads, writes, asyn):
+        need = {}
+        for wr, refs in ((False, reads), (True, writes)):
+            for r in refs:
+                ps = r[0][:2] == "ps"
+                for (x, k, tok) in acc.get(r[0], []):
+                    if ps:
+                        if tok[2] == q and (q == "t" or wr or not k):
+                            continue
+                    elif not (k or wr) or not hit(r, x) or (q == "t" and tok[2] == q):
+                        continue
+                    need[tok[0]] = max(need.get(tok[0], 0), tok[1])
+        for sem, val in sorted(need.items(), key=lambda z: (z[0][0] == "q", -z[1])):
+            wait(q, sem, val)
+
+    def note(q, reads, writes, tok):
+        for wr, refs in ((False, reads), (True, writes)):
+            for r in refs:
+                old = acc.get(r[0], [])
+                if wr:
+                    old = [o for o in old if not (r[3] == 1 and r[1] <= o[0][1] and o[0][2] <= r[2] and (r[4] is None or r[4] == o[0][4]))]
+                else:
+                    old = [o for o in old if not (not o[1] and o[0] == r and o[2][2] == tok[2] and not tok[3] and not o[2][3])]
+                acc[r[0]] = old + [(r, wr, tok)]
+
+    def op(q, reads, writes, fns):
+        deps(q, reads, writes, False)
+        for f in fns[:-1]:
+            f(Q[q])
+        cnt[q] += 1
+        sem = "q" + q
+        fns[-1](Q[q]).then_inc(T.sem[sem], 1)
+        top[sem] = cnt[q]
+        s = dict(known[q]); s[sem] = cnt[q]
+        snap[(sem, cnt[q])] = s
+        note(q, reads, writes, (sem, cnt[q], q, False))
+
+    def dma(q, out, in_, oap, iap):
+        rd, wr = ([in_] if in_ else []), ([out] if out else [])
+        deps(q, rd, wr, True)
+        sem = "d%d" % nd[0]; nd[0] += 1
+        Q[q].dma_start(out=oap, in_=iap).then_inc(T.sem[sem], 16)
+        top[sem] = 16
+        snap[(sem, 16)] = dict(known[q])
+        note(q, rd, wr, (sem, 16, q, True))
+
+    def remote(src, lsem, lval, call):
+        deps("g", [src], [], True)
+        call()
+        top[lsem] = lval
+        note("g", [src], [], (lsem, lval, "g", True))
+
+    def land(refs, sem, val):
+        top[sem] = val
+        for r in refs:
+            acc[r[0]] = [o for o in acc.get(r[0], []) if not hit(r, o[0])] + [(r, True, (sem, val, "-", True))]
+
+    def finish():
+        for sem, val in sorted(top.items()):
+            wait("g", sem, val)
+    return op, dma, remote, land, finish
+
+
+def rank_program(g, core, T, topo):
+    rank = T.rank_of(core)
+    if rank is None:
+        return
+    op, dma, remote, land, finish = tracker(g, T)
+
+    def R(n, a=0, b=None, step=1, row=None):
+        if n in AL:
+            o, w = AL[n]
+            return ("pf", o + a, o + (w if b is None else b), step, row)
+        return (n, a, (SCRATCH[n][1][1] if b is None else b), step, row)
+
+    def ap(r):
+        if r[4] is not None:
+            return T[r[0]][r[4]::16, r[1]:r[2]]
+        return T[r[0]][:, r[1]:r[2]] if r[3] == 1 else T[r[0]][:, r[1]:r[2]:r[3]]
+
+    def ts(out, a, s1, o1, s2=None, o2=None):
+        rd = [a] + [s for s in (s1, s2) if isinstance(s, tuple)]
+        f1 = ap(s1) if isinstance(s1, tuple) else s1
+        f2 = ap(s2) if isinstance(s2, tuple) else s2
+        if o2 is None:
+            op("v", rd, [out], [lambda e: e.tensor_scalar(out=ap(out), in0=ap(a), scalar1=f1, scalar2=None, op0=o1)])
+        else:
+            op("v", rd, [out], [lambda e: e.tensor_scalar(out=ap(out), in0=ap(a), scalar1=f1, scalar2=f2, op0=o1, op1=o2)])
+
+    def tt(out, a, b, o):
+        op("v", [a, b], [out], [lambda e: e.tensor_tensor(out=ap(out), in0=ap(a), in1=ap(b), op=o)])
+
+    def cp(out, a):
+        op("v", [a], [out], [lambda e: e.tensor_copy(out=ap(out), in_=ap(a))])
+
+    def act(out, a, scale=1.0, bias=0.0):
+        rd = [a] + ([scale] if isinstance(scale, tuple) else [])
+        sc = ap(scale) if isinstance(scale, tuple) else scale
+        op("s", rd, [out], [lambda e: e.activation(out=ap(out), in_=ap(a), func=CP, bias=bias, scale=sc)])
+
+    def fill(r, c):
+        op("v", [], [r], [lambda e: e.memset(ap(r), c)])
+
+    def gat(q, out, win, off):
+        if q == "v":
+            op("v", [win, off], [out], [lambda e: e.tensor_copy(out=ap(out), in_=ap(win).indirect(ap(off)))])
+        else:
+            op("s", [win, off], [out], [lambda e: e.activation(out=ap(out), in_=ap(win).indirect(ap(off)), func=CP)])
+
+    def gat2(out, win, off, b, o):
+        op("v", [win, off, b], [out], [lambda e: e.tensor_tensor(out=ap(out), in0=ap(win).indirect(ap(off)), in1=ap(b), op=o)])
+
+    def sca(win, off, a):
+        op("v", [a, off], [win], [lambda e: e.tensor_copy(out=ap(win).indirect(ap(off)), in_=ap(a))])
+
+    def f2p(ps, c0, z, src, a0, n):
+        def mk(i):
+            return lambda e: e.matmul(T[ps][:, c0:c0 + n], T[z][:, 128 * i:128 * i + 128], T[src][:, a0 + i:a0 + 16 * n:16], i == 0, i == 15)
+        op("t", [R(z), R(src, a0, a0 + 16 * n)], [R(ps)], [mk(i) for i in range(16)])
+
+    def p2f(tab, row, col, src, c0, n):
+        out = R(tab, col, col + 16 * n, 1, row)
+        dma("y", out, R(src, c0, c0 + n), ap(out), T[src][:, c0:c0 + n])
+
+    def route(c):
+        r = T.rank_of(c)
+        nb = [T.cores[(r - 1) % NR], T.cores[(r + 1) % NR]]
+        e = [topo.engines(c, d) for d in nb]
+        first = 0 if len(e[0]) <= len(e[1]) else 1
+        for k in (8, 4, 2, 1):
+            x = e[first][:k]
+            y = [z for z in e[1 - first] if z not in x][-k:]
+            if len(x) == k and len(y) == k:
+                return nb, ([x, y] if first == 0 else [y, x]), k
+
+    nb, eng, kk = route(core)
+    arrive = route(nb[0])[2] + route(nb[1])[2]
+
+    def send(kind, t, src, dst, d0, w):
+        tr = []
+        for s in range(2):
+            rid, pid, _se = topo.addr(nb[s])
+            tr.append(RemoteDMATransfer(dst_ids=[DstId(rid=rid, pnc=pid)], dma_engine_mask=sum(1 << z for z in eng[s]),
+                                        remote_sem=T.sem["a%s%d" % (kind, t)], src=T[src][:, s * w:s * w + w],
+                                        dst=T[dst][:, d0 + (1 - s) * w:d0 + (2 - s) * w]))
+        ls = "l%s%d" % (kind, t)
+        remote(R(src), ls, 2 * kk, lambda: g.remote_dma_fused(tr, local_sem=T.sem[ls]))
+
+    def arrived(kind, t, dst, d0, w):
+        land([R(dst, d0, d0 + 2 * w)], "a%s%d" % (kind, t), arrive)
+
+    def load(q, out, src):
+        dma(q, out, None, ap(out), src)
+    load("s", R("xin", 320, 480), T.bs[:, :])
+    load("y", R("xin", 0, 160), T.lt[:, :])
+    load("s", R("xin", 160, 320), T.rt[:, :])
+    for s in range(2):
+        load("y", R("sin", 8 * s, 8 * s + 8), T.snd[:, 128 * s:128 * s + 128])
+    load("y", R("ev", 0, P0), T.err[:, :])
+    load("y", R("win", 0, 1), T.wt[:, :])
+    load("y", R("win", 1, 2), T.th[:, :])
+    load("s", R("dr"), T.det[:, :])
+
+    op("g", [], [R("pid", 0, 1)], [lambda e: e.iota(T.pid[:, 0:1], [[1, 1]], 0, 1)])
+
+    def iof(n, a, b, pat, base):
+        op("g", [], [R(n, a, b)], [lambda e: e.iota(T[n][:, a:b], pat, base, 0, allow_small_or_imprecise_dtypes=True)])
+    fill(R("bo"), 1.0)
+    iof("cc", 0, 224, [[1, 224]], 0)
+    op("g", [R("bo")], [R("bo")], [lambda e: e.affine_select(T.bo[:, :], T.bo[:, :], [[-16, 8], [0, 16]], A.is_ge, 0.0, 0, 1)])
+    op("g", [R("bo")], [R("bo")], [lambda e: e.affine_select(T.bo[:, :], T.bo[:, :], [[16, 8], [0, 16]], A.is_ge, 0.0, 15, -1)])
+    iof("i16", 0, 16, [[1, 16]], 0)
+    iof("ev", P0, 3600, [[0, 1040]], 0)
+    iof("xs", 0, 16, [[128, 2], [1, 8]], GH)
+    iof("gv", 0, 256, [[128, 2], [1, 16], [16, 8]], 16)
+    op("g", [R("bo")], [R("ltm")], [lambda e: e.affine_select(T.ltm[:, :], T.bo[:, :], [[1, 128]], A.is_gt, 0.0, 0, -1)])
+    ts(R("pid", 1, 2), R("pid", 0, 1), 15, A.bitwise_and)
+    fill(R("zz"), 0.0)
+    ts(R("pid", 2, 3), R("pid", 1, 2), 1, A.logical_shift_right)
+    cp(R("ci", 0, 1), R("pid", 1, 2))
+    cp(R("ci", 1, 2), R("pid", 2, 3))
+    fill(R("tb"), 8192.0)
+    I1 = R("ci", 0, 1)
+    ts(R("ci", 6, 7), I1, float(W0), A.add)
+    ts(R("mk2"), R("i16", 0, 8), R("ci", 1, 2), A.is_equal)
+    ts(R("ix"), R("cc"), 16.0, A.mult, R("ci", 6, 7), A.add)
+
+    def halves(src, a, b, h, l, ha, q="v"):
+        if q == "s":
+            act(R(h, ha, ha + b - a), R(src, a, b))
+        else:
+            cp(R(h, ha, ha + b - a), R(src, a, b))
+        tt(R(l, ha, ha + b - a), R(src, a, b), R(h, ha, ha + b - a), A.subtract)
+    OFF = {"l": 0, "r": 224, "b": 448}
+    TROW = {"b": 0, "r": 2, "l": 6}
+
+    def table(x, t, q="v"):
+        o, n = OFF[x], 160 + 32 * t
+        halves("px", o, o + n, "hi", "lo", o, q)
+        for k, src in ((0, "hi"), (1, "lo")):
+            for tab in (("tc", "tb") if t and x == "b" else ("tb",)):
+                p2f(tab, TROW[x] + k, 0, src, o, 160)
+                if t:
+                    p2f(tab, TROW[x] + k, P0, src, o + 160, 32)
+
+    def slots(t):
+        halves("sn", 0, 16, "shi", "slo", 0)
+        for k, src in ((0, "shi"), (1, "slo")):
+            for s in range(2):
+                p2f("snf", k, 128 * s, src, 8 * s, 8)
+
+    def nat(s, i, src):
+        a = 128 * s + 16 * (i & 7) + (i >> 3)
+        return lambda e: e.matmul(T.ps0[:, 8 * s:8 * s + 8], T.zb[:, 128 * i:128 * i + 128], T[src][:, a:a + 15:2], i == 0, i == 15)
+
+    def bases(src, tab):
+        gat("s", R(src), R(tab), R("snu"))
+        for s in range(2):
+            op("t", [R("zb"), R(src)], [R("ps0")], [nat(s, i, src) for i in range(16)])
+
+    def sendbases(t):
+        cp(R("bes"), R("ps0", 0, 16))
+        send("be", t, "bes", "bel%d" % t, 0, 8)
+
+    halves("ix", 0, 224, "ihi", "ilo", 0)
+    for k, src in ((4, "ihi"), (5, "ilo")):
+        p2f("tb", k, 0, src, 0, 160)
+        p2f("tb", k, P0, src, 160, 32)
+    for x, c in (("b", 320), ("l", 0), ("r", 160)):
+        cp(R("px", OFF[x], OFF[x] + 160), R("xin", c, c + 160))
+        table(x, 0, "s")
+    cp(R("sn"), R("sin"))
+    cp(R("snu"), R("sn"))
+    op("v", [R("bo")], [R("zz")], [lambda e, i=i: e.tensor_copy(out=T.zz[:, 129 * i:128 * i + 128:16], in_=T.bo[:, i::16]) for i in range(16)])
+    ts(R("zb"), R("zz"), R("mk2", 0, 1), A.mult)
+    fill(R("snf"), 0.0)
+    slots(0)
+    ts(R("bv", 0, 160), R("px", 448, 608), float(GH - 1), A.min)
+    ts(R("ci", 2, 3), I1, 160.0, A.mult)
+    ts(R("ci", 3, 4), I1, 32.0, A.mult, 2400.0, A.add)
+    ts(R("ci", 4, 5), I1, 32.0, A.mult, 2880.0, A.add)
+    ts(R("ci", 5, 6), I1, 8.0, A.mult)
+    bases("gs", "tb")
+    ts(R("me", 0, 160), R("cc", 0, 160), R("ci", 2, 3), A.add)
+    ts(R("me", 160, 192), R("cc", 160, 192), R("ci", 3, 4), A.add)
+    ts(R("me", 192, 224), R("cc", 192, 224), R("ci", 4, 5), A.add)
+    ts(R("xs"), R("xs"), R("ci", 5, 6), A.add)
+    ts(R("mk"), R("i16"), I1, A.is_equal)
+    ts(R("i8", 1, 2), R("mk2", 0, 1), 4096.0, A.mult)
+    ts(R("snf", 256, 272), R("i16"), 0.0, A.mult, R("i8", 1, 2), A.add)
+    for w in ("eu", "wa", "wb"):
+        fill(R(w, 0, 16), 0.0)
+    sendbases(0)
+    ts(R("zr"), R("zz"), R("mk2", 1, 2), A.mult)
+    ts(R("zl"), R("zz"), R("mk2", 3, 4), A.mult)
+    ts(R("zi"), R("zz"), R("mk2", 2, 3), A.mult)
+    cp(R("gh1"), R("gv"))
+    tt(R("gl1"), R("gv"), R("gh1"), A.subtract)
+    ts(R("gh1"), R("gh1"), R("mk", 4, 5), A.mult)
+    ts(R("gl1"), R("gl1"), R("mk", 5, 6), A.mult)
+    tt(R("gi"), R("gh1"), R("gl1"), A.add)
+    errors = [None]
+
+    for t in range(2):
+        n = 160 + 32 * t
+        NL, base = 16 * n, P0 + 512 * t
+        nw0 = n
+        h = n // 2
+        E = ((0, h), (h, n))
+        NE = [(W0 + 16 * a, W0 + 16 * b) for a, b in E]
+        EC = [R("ec", 16 * a, 16 * b) for a, b in E]
+        ntb = "nt%d" % t
+        PL, PR, PB = R("px", 0, n), R("px", 224, 224 + n), R("px", 448, 448 + n)
+        ME, WIN = R("me", 0, n), R("tb")
+        WE = R("eu", 0, W0 + NL)
+
+        def keep(src, k):
+            act(EC[k], R(src, *NE[k]))
+        if t == 0:
+            gat("s", R("x0"), R("ev", 0, 3600), R("snu"))
+            send("x0", t, "x0", "eu", 16, 128)
+        else:
+            gat("s", R("gs"), WIN, R("snu"))
+        f2p("ps1", 0, "zl", "gs", 0, 16)
+        f2p("ps1", 16, "zr", "gs", 0, 16)
+        f2p("ps1", 32, "zi", "gs", 0, 16)
+        gat("s", R("gb", 0, NL), WIN, R("bv", 0, n))
+        cp(R("slu"), R("ps1", 0, 32))
+        ts(R("siu"), R("ps1", 32, 48), -float(W0), A.add)
+        tt(R("srf"), R("ps1", 16, 32), R("xs"), A.is_equal)
+        f2p("ps2", 0, "zb", "gb", 0, n)
+        f2p("ps3", 0, "zi", "gb", 0, n)
+        f2p("ps4", 0, "zr", "gb", 0, n)
+        cp(R("lv", 0, n), PL)
+        cp(R("rv", 0, n), PR)
+        if t:
+            errors[0]()
+            gat("s", R("x0"), R("eu", W0, W0 + NL), R("siu"))
+            send("x0", t, "x0", "eu", 16, 128)
+            keep("eu", 0)
+            keep("eu", 1)
+        arrived("be", t, "bel%d" % t, 0, 8)
+        bl = "bel%d" % t
+        ts(R("gm"), R(bl), 3712.0, A.is_ge)
+        ts(R("gm1"), R(bl, 8, 16), 3584.0, A.is_ge)
+        ts(R("gd", 0, 8), R(bl, 0, 8), -3968.0, A.add)
+        ts(R("gd", 8, 16), R(bl, 8, 16), -3712.0, A.add)
+        tt(R("gm", 8, 16), R("gm1"), R("gm", 8, 16), A.subtract)
+        tt(R("gd"), R("gd"), R("gm"), A.mult)
+        ts(R("gbu"), R("gd"), 256.0, A.add)
+        gat2(R("tb", GH, 3840), R("snf"), R("gbu"), R("gi"), A.add)
+        for k, (a, b) in enumerate(E):
+            gat("v", R("gl", 16 * a, 16 * b), WIN, R("lv", a, b))
+            if k == 0:
+                gat("s", R("gx"), WIN, R("slu"))
+            gat("s", R("gr", 16 * a, 16 * b), WIN, R("rv", a, b))
+        for k, (a, b) in enumerate(E):
+            f2p("ps5" if k == 0 else "ps7", 0, "zb", "gl", 16 * a, b - a)
+            f2p("ps6" if k == 0 else "ps0", 0, "zi", "gl", 16 * a, b - a)
+            if k == 0:
+                f2p("ps1", 0, "zb", "gx", 0, 32)
+                f2p("ps1", 32, "zi", "gx", 0, 32)
+        if t == 0:
+            op("v", [R("ev", 0, P0)], [R("eu", W0, W0 + P0)],
+               [lambda e, i=i: e.tensor_copy(out=T.eu[:, W0 + i:W0 + P0:16], in_=T.ev[:, 160 * i:160 * i + 160]) for i in range(16)])
+            keep("eu", 0)
+            keep("eu", 1)
+
+        def legs(ps, ps2, a, b, v, f, w):
+            tt(R(v, a, b), R(ps, 0, b - a), R("me", a, b), A.is_equal)
+            tt(R(f, a, b), R(ps2, 0, b - a), R(v, a, b), A.mult)
+            cp(R(w, a, b), R(f, a, b))
+        legs("ps5", "ps6", E[0][0], E[0][1], "vl", "lf", "lw")
+        for x in (0, 16):
+            tt(R("xv", x, x + 16), R("ps1", x, x + 16), R("sn"), A.is_equal)
+        tt(R("xf"), R("ps1", 32, 64), R("xv"), A.mult)
+        cp(R("xlu"), R("xf"))
+        arrived("x0", t, "eu", 16, 128)
+        gat2(R("wa", *NE[0]), WE, R("lw", *E[0]), EC[0], A.max)
+        gat2(R("x1"), WE, R("xlu", 0, 16), R("x0"), A.max)
+        gat2(R("x1"), WE, R("xlu", 16, 32), R("x1"), A.max)
+        send("x1", t, "x1", "wa", 16, 128)
+        if t == 0:
+            iof("cv", 0, 3072, [[0, 3072]], 1)
+        legs("ps7", "ps0", E[1][0], E[1][1], "vl", "lf", "lw")
+        gat2(R("wa", *NE[1]), WE, R("lw", *E[1]), EC[1], A.max)
+        for k, (a, b) in enumerate(E):
+            f2p("ps5" if k == 0 else "ps7", 0, "zb", "gr", 16 * a, b - a)
+            f2p("ps6" if k == 0 else "ps0", 0, "zi", "gr", 16 * a, b - a)
+            legs("ps5" if k == 0 else "ps7", "ps6" if k == 0 else "ps0", a, b, "vr", "rf", "rw")
+            gat2(R("wa", *NE[k]), WE, R("rw", a, b), R("wa", *NE[k]), A.max)
+            keep("wa", k)
+        f2p("ps5", 0, "zr", "gl", 0, n)
+        f2p("ps6", 0, "zr", "gr", 0, n)
+        arrived("x1", t, "wa", 16, 128)
+        WWA, WWB = R("wa", 0, W0 + NL), R("wb", 0, W0 + NL)
+        gat2(R("x2"), WWA, R("xlu", 0, 16), R("x1"), A.max)
+        gat2(R("x2"), WWA, R("xlu", 16, 32), R("x2"), A.max)
+        send("x2", t, "x2", "wb", 16, 128)
+        if t == 0:
+            for tab in ("nt0", "tc", "nt1"):
+                iof(tab, 0, 3840, [[0, 3840]], 0)
+            act(R("df"), R("dr"), 0.5, -0.25)
+            act(R("df"), R("df"), 1.0, 8388608.0)
+
+        def bulk(dst, win):
+            for k in range(2):
+                gat2(R(dst, *NE[k]), win, R("lw", *E[k]), EC[k], A.max)
+            for k in range(2):
+                gat2(R(dst, *NE[k]), win, R("rw", *E[k]), R(dst, *NE[k]), A.max)
+                keep(dst, k)
+        bulk("wb", WWA)
+        tt(R("eq", 0, n), R("ps2", 0, n), ME, A.is_equal)
+        tt(R("pt", 0, n), PB, ME, A.is_gt)
+        tt(R("bf", 0, n), R("ps3", 0, n), R("eq", 0, n), A.mult)
+        tt(R("pt", 0, n), R("pt", 0, n), R("eq", 0, n), A.mult)
+        cp(R("bw", 0, n), R("bf", 0, n))
+        ts(R("thr", 0, n), R("pt", 0, n), -93.0, A.mult, 99.0, A.add)
+        tt(R("rb", 0, n), R("ps4", 0, n), ME, A.is_equal)
+        tt(R("rl", 0, n), R("ps5", 0, n), ME, A.is_equal)
+        tt(R("rr", 0, n), R("ps6", 0, n), ME, A.is_equal)
+        if t == 0:
+            cp(R("ci", 7, 8), R("win", 1, 2))
+            cp(R("i8", 0, 1), R("win", 0, 1))
+            fill(R("zero"), 0.0)
+            fill(R("dh", 2048, 2064), 0.0)
+            ts(R("ixm"), R("ix", 0, 192), -16.0, A.add)
+            halves("me", 0, 224, "chi", "clo", 0, "s")
+            for k, src in ((0, "chi"), (1, "clo")):
+                p2f("cv", k, 0, src, 0, 160)
+                p2f("cv", k, P0, src, 160, 32)
+            for k in range(3):
+                act(R("px", 224 * k + 192, 224 * k + 224), R("me", 192, 224))
+            act(R("dh", 0, 2048), R("df"), 1.0, -8388608.0)
+            act(R("zh"), R("zz"), R("i8", 0, 1))
+        TH = R("ci", 7, 8)
+        fill(R("ct", 0, 256), 0.0)
+        arrived("x2", t, "wb", 16, 128)
+        bulk("wa", WWB)
+        if t == 0:
+            op("s", [R("cv")], [R("vf")],
+               [lambda e, i=i: e.activation(out=T.vf[:, i:P0:16], in_=T.cv[:, 160 * i:160 * i + 160], func=CP) for i in range(16)] +
+               [lambda e, i=i: e.activation(out=T.vf[:, P0 + i:3072:16], in_=T.cv[:, P0 + 32 * i:P0 + 32 * i + 32], func=CP) for i in range(16)])
+        else:
+            op("s", [R("eu", W0, W0 + 3072)], [R("ev", 0, 3072)],
+               [lambda e, i=i: e.activation(out=T.ev[:, 160 * i:160 * i + 160], in_=T.eu[:, W0 + i:W0 + P0:16], func=CP) for i in range(16)] +
+               [lambda e, i=i: e.activation(out=T.ev[:, P0 + 32 * i:P0 + 32 * i + 32], in_=T.eu[:, W0 + P0 + i:W0 + 3072:16], func=CP) for i in range(16)])
+        for k, (a, b) in enumerate(E):
+            gat2(R("hb", 16 * a, 16 * b), WWA, R("bw", a, b), EC[k], A.max)
+            ts(R("hb", 16 * a, 16 * b), R("hb", 16 * a, 16 * b), TH, A.is_ge)
+            f2p("ps4", a, "zz", "hb", 16 * a, b - a)
+        tt(R("hot", 0, n), R("ps4", 0, n), R("thr", 0, n), A.is_ge)
+        segs = [(0, 160)] + ([(160, 192)] if t else [])
+        for a, b in segs:
+            op("v", [R("hot", a, b), R("zero", a, b)], [R("cum", a, b)],
+               [lambda e, a=a, b=b: e.tensor_tensor_scan(T.cum[:, a:b], T.hot[:, a:b], T.zero[:, a:b], 0.0, A.add, A.add)])
+        op("t", [R("ltm"), R("cum", 0, 160)], [R("ps0")], [lambda e: e.matmul(T.ps0[:, 0:1], T.ltm[:, :], T.cum[:, 159:160], True, True)])
+        if t:
+            op("t", [R("ltm"), R("bo"), R("cum")], [R("ps0")],
+               [lambda e: e.matmul(T.ps0[:, 1:2], T.ltm[:, :], T.cum[:, 191:192], True, False),
+                lambda e: e.matmul(T.ps0[:, 1:2], T.bo[:, :], T.cum[:, 159:160], False, True)])
+        for k, (a, b) in enumerate(segs):
+            ts(R("k1", a, b), R("cum", a, b), R("ps0", k, k + 1), A.add)
+        ts(R("sel", 0, n), R("k1", 0, n), 256.0, A.is_le)
+        ts(R("kn", 0, n), R("k1", 0, n), 2.0, A.mult, -2.0, A.add)
+        tt(R("sel", 0, n), R("sel", 0, n), R("hot", 0, n), A.mult)
+        act(R("n1", 0, n), R("sel", 0, n), float(base))
+        act(R("wr", 0, n), R("sel", 0, n), -BIG, BIG - 1.0)
+        tt(R("n0", 0, n), R("kn", 0, n), R("sel", 0, n), A.mult)
+
+        def rows(lst):
+            for row, src in lst:
+                p2f(ntb, row, 0, src, 0, 160)
+                if t:
+                    p2f(ntb, row, P0, src, 160, 32)
+        rows(((1, "n1"), (0, "n0")))
+        gat("s", R("gb", 0, NL), R(ntb), R("bv", 0, n))
+        tt(R("dd", 0, n), R("wr", 0, n), R("k1", 0, n), A.add)
+        tt(R("dd", 0, n), R("dd", 0, n), R("ixm", 0, n), A.min)
+        cp(R("pd", 0, n), R("dd", 0, n))
+        sp = 96 + 16 * t
+        sca(R("ct", 0, 256 + NL), R("pd", 0, sp), R("vf", 0, 16 * sp))
+        f2p("ps1", 0, "zz", "gb", 0, n)
+        tt(R("nc", 0, n), R("ps1", 0, n), R("eq", 0, n), A.mult)
+        ts(R("sc", 0, n), R("nc", 0, n), 1.0, A.min)
+        halves("nc", 0, n, "nchi", "nclo", 0)
+        rows(((4, "sc"), (2, "nchi"), (3, "nclo")))
+        sca(R("ct", 0, 256 + NL), R("pd", sp, n), R("vf", 16 * sp, NL))
+
+        def ctp(ps, c, z):
+            op("t", [R(z), R("ct", 0, 256)], [R(ps)],
+               [lambda e, i=i: e.matmul(T[ps][:, c:c + 16], T[z][:, 128 * i:128 * i + 128], T.ct[:, 16 * i:16 * i + 16], i == 0, i == 15) for i in range(16)])
+        ctp("ps2", 0, "zr")
+        ctp("ps2", 16, "zb")
+        gat("s", R("gb", 0, NL), R(ntb), R("bv", 0, n))
+        tt(R("nt", 0, n), R("n0", 0, n), R("n1", 0, n), A.add)
+        tt(R("nc", 0, n), R("nc", 0, n), R("sc", 0, n), A.add)
+        ts(R("st", 0, n), R("nt", 0, n), 1.0, A.min)
+        tt(R("spl", 0, n), R("st", 0, n), R("sc", 0, n), A.add)
+        for s in range(2):
+            ts(R("fl", s, 32, 2), R("ps2", 0, 16), 0.5, A.mult)
+        ts(R("fo"), R("fl"), -float(GH), A.mult, float(GH), A.add)
+        tt(R("tv", 0, 32, 2), R("ps2", 16, 32), R("fo", 0, 32, 2), A.add)
+        cp(R("tu16"), R("tv", 0, 32, 2))
+        gat("s", R("gt"), WIN, R("tu16"))
+        act(R("m8", 0, n), R("spl", 0, n), 8192.0)
+        f2p("ps3", 0, "zb", "gt", 0, 16)
+        f2p("ps0", 0, "zz", "gb", 0, n)
+        tt(R("no", 0, n), R("nt", 0, n), R("nc", 0, n), A.add)
+        tt(R("tv", 1, 32, 2), R("ps3", 0, 16), R("fl", 0, 32, 2), A.mult)
+        tt(R("tv", 1, 32, 2), R("tv", 1, 32, 2), R("fo", 0, 32, 2), A.add)
+        cp(R("tu"), R("tv"))
+        gat("s", R("gq"), WIN, R("tu"))
+        f2p("ps6", 0, "zr", "gq", 0, 32)
+        if t == 0:
+            f2p("ps6", 32, "zi", "gq", 0, 32)
+        gat("v", R("gl", 0, 16 * h), R(ntb), R("lv", 0, h))
+        cp(R("rq"), R("ps6", 0, 32))
+        cp(R("yu"), R("rq"))
+        gat("s", R("gy"), WIN, R("yu"))
+        gat("s", R("gn"), R(ntb), R("yu"))
+        gat("s", R("eg"), R("ev", 0, 3600), R("tu"))
+        f2p("ps2", 0, "zr", "gy", 0, 32)
+        f2p("ps3", 0, "zz", "gn", 0, 32)
+        f2p("ps7", 0, "zh", "eg", 0, 32)
+        if t == 0:
+            gat("s", R("gsn"), R(ntb), R("snu"))
+            f2p("ps1", 0, "zz", "gsn", 0, 16)
+        tt(R("wq", 0, n), R("ps0", 0, n), R("rb", 0, n), A.mult)
+        gat("v", R("gl", 16 * h, NL), R(ntb), R("lv", h, n))
+        tt(PB, PB, R("wq", 0, n), A.max)
+        tt(R("nb", 0, n), R("no", 0, n), R("st", 0, n), A.add)
+        tt(PB, PB, R("m8", 0, n), A.subtract)
+        tt(R("nb", 0, n), R("nb", 0, n), R("sc", 0, n), A.subtract)
+        dump = 2800.0 if t == 0 else 3328.0
+
+        def detlists():
+            tt(R("di", 0, 32), R("ps7", 0, 32), R("tv"), A.add)
+            tt(R("di", 32, 64), R("ps7", 0, 32), R("me", nw0, nw0 + 32), A.add)
+            ts(R("da"), R("di"), 2047, A.bitwise_and)
+            ts(R("dq"), R("da"), -2048.0, A.add)
+            tt(R("dq", 32, 64), R("dq", 32, 64), R("fl"), A.mult)
+            ts(R("du"), R("dq"), 2048.0, A.add)
+            gat("s", R("dg"), R("dh"), R("du"))
+
+        def places():
+            if t == 0:
+                ts(R("scf"), R("ps6", 32, 64), -(W0 + dump), A.add)
+            else:
+                ts(R("scf"), R("tv"), -dump, A.add)
+            tt(R("scf"), R("scf"), R("ix", 0, 32), A.subtract)
+            tt(R("scf"), R("scf"), R("fl"), A.mult)
+            tt(R("scf"), R("scf"), R("ix", 0, 32), A.add)
+            ts(R("scu"), R("scf"), dump, A.add)
+            ts(R("e2"), R("eg"), 0.5, A.mult, -0.25, A.add)
+
+        def children(t=t):
+            tt(R("cl"), R("e2"), R("dg", 0, 512), A.add)
+            if t == 0:
+                sca(R("eu", W0, 3856), R("scu"), R("cl"))
+                tt(R("eu", W0 + P0, W0 + 3072), R("e2"), R("dg", 512, 1024), A.add)
+            else:
+                sca(R("ev"), R("scu"), R("cl"))
+                tt(R("cr"), R("e2"), R("dg", 512, 1024), A.add)
+                op("v", [R("cr")], [R("ev", 3072, GH)],
+                   [lambda e, i=i: e.tensor_copy(out=T.ev[:, 3072 + 32 * i:3104 + 32 * i], in_=T.cr[:, i::16]) for i in range(16)])
+        if t == 1:
+            detlists()
+            places()
+        gat("s", R("gr", 0, NL), R(ntb), R("rv", 0, n))
+        f2p("ps4", 0, "zz", "gl", 0, n)
+        f2p("ps5", 0, "zz", "gr", 0, n)
+        MN = R("me", nw0, nw0 + 32)
+
+        def newplaces(k, x):
+            o = R("px", 224 * k + nw0, 224 * k + nw0 + 32)
+            w = R("nw", 32 * k, 32 * k + 32)
+            tt(w, R(x), MN, A.subtract)
+            tt(w, w, R("fl"), A.mult)
+            tt(o, w, MN, A.add)
+        tt(R("rn"), R("ps2", 0, 32), R("tv"), A.is_equal)
+        tt(R("rn"), R("ps3", 0, 32), R("rn"), A.mult)
+        tt(R("rn"), R("rn"), R("rq"), A.max)
+        newplaces(2, "rn")
+        tt(R("wq", 0, n), R("ps4", 0, n), R("rl", 0, n), A.mult)
+        tt(PL, PL, R("wq", 0, n), A.max)
+        tt(R("wq", 0, n), PL, R("spl", 0, n), A.mult)
+        tt(PB, PB, R("wq", 0, n), A.max)
+        if t == 0:
+            table("b", 1)
+            tt(R("sw"), R("ps1", 0, 16), R("srf"), A.mult)
+            tt(R("sn"), R("sn"), R("sw"), A.max)
+            cp(R("snu"), R("sn"))
+            bases("gsb", "tc")
+        tt(PL, PL, R("m8", 0, n), A.subtract)
+        cp(R("pv", 0, 32, 2), R("tv", 1, 32, 2))
+        tt(PL, PL, R("no", 0, n), A.max)
+        cp(R("pv", 1, 32, 2), R("tv", 0, 32, 2))
+        newplaces(0, "pv")
+        if t == 0:
+            table("l", 1)
+            slots(1)
+        tt(PR, PR, R("m8", 0, n), A.subtract)
+        newplaces(1, "tv")
+        if t == 1:
+            children()
+            dma("y", None, R("ev", 0, GH), T.ye[:, :], T.ev[:, 0:GH])
+        tt(R("wq", 0, n), R("ps5", 0, n), R("rr", 0, n), A.mult)
+        tt(R("wq", 0, n), R("wq", 0, n), R("m8", 0, n), A.subtract)
+        tt(PR, PR, R("wq", 0, n), A.max)
+        tt(PR, PR, R("nb", 0, n), A.max)
+        if t == 0:
+            table("r", 1)
+            sendbases(1)
+            ts(R("bv"), R("px", 448, 640), float(GH - 1), A.min)
+            detlists()
+            places()
+            errors[0] = children
+
+    for k, y in ((2, T.yb), (0, T.yl), (1, T.yr)):
+        for a, b, c in ((0, P0, 0), (P0, 3072, 160), (3072, GH, 192)):
+            src = R("px", 224 * k + c, 224 * k + c + (b - a) // 16)
+            dma("y", None, src, y[:, a:b], ap(src))
+    finish()

@@ -1,31 +1,33 @@
-import numpy as np
 from concourse.bass import DstId, RemoteDMATransfer
 from concourse.mybir import AluOpType as A, ActivationFunctionType as F
 
 NR, P0, GH = 8, 2560, 3584
-CP = F.Copy
-W0 = 272
+S0 = 16
+GC, M = GH + S0, 3856
 BIG = 16384.0
-_bf = {"hi": 672, "lo": 672, "shi": 16, "slo": 16, "ihi": 224, "ilo": 224, "chi": 224, "clo": 224,
-       "ev": 4112, "eu": 3856, "wa": 3344, "wb": 3344, "tb": 3840, "tc": 3840, "nt0": 3840, "nt1": 3840,
-       "gl": 3072, "gr": 3072, "gb": 3072, "hb": 3072, "ec": 3072, "cv": 3072, "vf": 3072, "ct": 3328, "snf": 272,
-       "zz": 2048, "zb": 2048, "zr": 2048, "zi": 2048, "zl": 2048, "zh": 2048, "bo": 128, "ltm": 128, "dr": 2048, "dh": 2064,
-       "gh1": 256, "gl1": 256, "gi": 256, "zero": 192, "gs": 256, "gsb": 256, "gx": 512, "gt": 256, "gq": 512, "gy": 512, "gn": 512, "gsn": 256,
-       "rl": 192, "rr": 192, "rb": 192, "eq": 192, "hot": 192, "cum": 192, "sel": 192, "n0": 192, "n1": 192, "nchi": 192, "nclo": 192, "sc": 192,
-       "eg": 512, "dg": 1024, "cl": 512, "cr": 512, "x0": 256, "x1": 256, "x2": 256}
-_f32 = {"px": 672, "sn": 16, "df": 2048, "ci": 8, "i8": 8, "mk2": 8, "mk": 16, "i16": 16, "cc": 224, "me": 224, "ix": 224, "ixm": 192,
-        "xs": 16, "gv": 256, "bes": 16, "bel0": 16, "bel1": 16, "gm": 16, "gd": 16, "gm1": 8, "srf": 16, "sw": 16, "xv": 32, "xf": 32,
-        "vl": 192, "lf": 192, "vr": 192, "rf": 192, "bf": 192, "pt": 192, "thr": 192, "k1": 192, "nt": 192, "kn": 192, "dd": 192, "nc": 192,
-        "st": 192, "spl": 192, "no": 192, "nb": 192, "m8": 192, "wq": 192, "wr": 192, "fl": 32, "fo": 32, "tv": 32, "pv": 32, "rq": 32,
-        "rn": 32, "nw": 96, "dq": 64, "scf": 32}
-_i32 = {"xin": 480, "sin": 16, "win": 2, "pid": 4, "di": 64, "da": 64, "e2": 512}
-_u16 = {"lv": 192, "rv": 192, "bv": 192, "lw": 192, "rw": 192, "bw": 192, "snu": 16, "slu": 32, "siu": 16, "gbu": 16, "xlu": 32,
-        "tu16": 16, "tu": 32, "yu": 32, "du": 64, "scu": 32, "pd": 192}
+KB, KR, KL = 4352.0, 8192.0, 12032.0
+RN0 = 3840
+DA = (768, 896)
+CC = (3, 3)
+ZN = ["zz", "zB", "zR", "zL", "zE", "zB16", "zR16", "zL16", "zT16", "zMB", "zN0", "zN1", "zG0", "zG1", "zh", "z16", "d1", "d16", "d256"]
+_bf = {"win": M, "ew": M + 16, "w1": M + 16, "uw": M + 16, "za": 6912, "zb": 6912, "gl": 3328, "gr": 3328, "gb": 3072, "tr": 3072,
+       "hb": 3072, "eo": 1024, "ta": 1024, "nb": M, "rn": 12048, "dr": 2048, "dh": 2064, "dl": 2064, "msk": 2304, "nc0": 512, "nc1": 512,
+       "it": 2048, "z": 144 * len(ZN), "z0": 288, "bo": 128, "ltm": 128, "nid": 128, "snf": 416, "krow": 256, "dm": 192,
+       "hi": 576, "lo": 576, "shi": 16, "slo": 16, "mh": 416, "ml": 416, "gs": 512, "x0": 256, "x1": 256, "x2": 256, "xa": 256,
+       "hot": 192, "m0": 256, "m1": 256, "m2": 256, "g1": 512, "gq": 512, "eg": 512, "gn": 512, "gsn": 512, "e2": 512, "dg": 512,
+       "ek": 576, "kh": 192, "tgh": 192, "tgl": 192, "m8": 192}
+_f32 = {"px0": 576, "px1": 672, "mc": 416, "me": 192, "me16": 192, "mme": 208, "lm": 208, "rm": 208, "dd": 416, "gt": 192, "thr": 192,
+        "cb": 224, "cw1": 224, "cw2": 200, "cs": 16, "tg": 192, "eq": 576, "ns": 192, "sp": 192, "pre": 576, "e1": 192, "e3": 192,
+        "wq": 576, "ci": 16, "mk": 16, "mk2": 8, "zc": 24, "i16": 16, "cc": 192, "sn": 32, "xs": 32, "bt": 80, "srf": 32, "ab": 16,
+        "sw": 32, "kj": 32, "jj": 32, "nj": 64, "dj": 32, "inv": 64, "aj": 32, "tf": 32, "tq": 32, "dq": 64}
+_i32 = {"xin": 480, "sin": 32, "wti": 2, "pid": 4, "di": 64, "da": 64}
+_u16 = {"lv": 208, "rv": 208, "bv": 192, "lw": 208, "rw": 208, "sa": 32, "su": 32, "bes": 16, "bel0": 16, "bel1": 16,
+        "l1": 16, "l2": 16, "td": 32, "tu": 32, "ru": 32, "xu": 32, "du": 64}
 SCRATCH, AL, _o = {}, {}, 0
 for _k in list(_f32):
-    if _f32[_k] <= 192 and _k not in ("i16", "xs", "bes", "bel0", "bel1"):
+    if _f32[_k] <= 80 and _k != "xs":
         AL[_k] = (_o, _f32[_k])
-        _o += (_f32.pop(_k) + 3) // 4 * 4
+        _o += (_f32.pop(_k) + 7) // 8 * 8
 _f32["pf"] = _o
 for _s, _d in ((_bf, "bfloat16"), (_f32, "float32"), (_i32, "int32"), (_u16, "uint16")):
     for _k in _s:
@@ -59,7 +61,7 @@ def tracker(g, T):
                 known[q][s] = v
         known[q][sem] = val
 
-    def deps(q, reads, writes, asyn):
+    def deps(q, reads, writes):
         need = {}
         for wr, refs in ((False, reads), (True, writes)):
             for r in refs:
@@ -85,7 +87,7 @@ def tracker(g, T):
                 acc[r[0]] = old + [(r, wr, tok)]
 
     def op(q, reads, writes, fns):
-        deps(q, reads, writes, False)
+        deps(q, reads, writes)
         for f in fns[:-1]:
             f(Q[q])
         cnt[q] += 1
@@ -98,7 +100,7 @@ def tracker(g, T):
 
     def dma(q, out, in_, oap, iap):
         rd, wr = ([in_] if in_ else []), ([out] if out else [])
-        deps(q, rd, wr, True)
+        deps(q, rd, wr)
         sem = "d%d" % nd[0]; nd[0] += 1
         Q[q].dma_start(out=oap, in_=iap).then_inc(T.sem[sem], 16)
         top[sem] = 16
@@ -106,7 +108,7 @@ def tracker(g, T):
         note(q, rd, wr, (sem, 16, q, True))
 
     def remote(src, lsem, lval, call):
-        deps("g", [src], [], True)
+        deps("g", [src], [])
         call()
         top[lsem] = lval
         note("g", [src], [], (lsem, lval, "g", True))
@@ -154,19 +156,23 @@ def rank_program(g, core, T, topo):
     def cp(out, a):
         op("v", [a], [out], [lambda e: e.tensor_copy(out=ap(out), in_=ap(a))])
 
-    def act(out, a, scale=1.0, bias=0.0):
-        rd = [a] + ([scale] if isinstance(scale, tuple) else [])
+    def act(out, a, scale=1.0, bias=0.0, func=F.Copy):
+        rd = [a] + [s for s in (scale, bias) if isinstance(s, tuple)]
         sc = ap(scale) if isinstance(scale, tuple) else scale
-        op("s", rd, [out], [lambda e: e.activation(out=ap(out), in_=ap(a), func=CP, bias=bias, scale=sc)])
+        bi = ap(bias) if isinstance(bias, tuple) else bias
+        op("s", rd, [out], [lambda e: e.activation(out=ap(out), in_=ap(a), func=func, bias=bi, scale=sc)])
 
     def fill(r, c):
         op("v", [], [r], [lambda e: e.memset(ap(r), c)])
+
+    def scan(out, d0, d1, o0, o1):
+        op("v", [d0, d1], [out], [lambda e: e.tensor_tensor_scan(ap(out), ap(d0), ap(d1), 0.0, o0, o1)])
 
     def gat(q, out, win, off):
         if q == "v":
             op("v", [win, off], [out], [lambda e: e.tensor_copy(out=ap(out), in_=ap(win).indirect(ap(off)))])
         else:
-            op("s", [win, off], [out], [lambda e: e.activation(out=ap(out), in_=ap(win).indirect(ap(off)), func=CP)])
+            op("s", [win, off], [out], [lambda e: e.activation(out=ap(out), in_=ap(win).indirect(ap(off)), func=F.Copy)])
 
     def gat2(out, win, off, b, o):
         op("v", [win, off, b], [out], [lambda e: e.tensor_tensor(out=ap(out), in0=ap(win).indirect(ap(off)), in1=ap(b), op=o)])
@@ -174,14 +180,44 @@ def rank_program(g, core, T, topo):
     def sca(win, off, a):
         op("v", [a, off], [win], [lambda e: e.tensor_copy(out=ap(win).indirect(ap(off)), in_=ap(a))])
 
-    def f2p(ps, c0, z, src, a0, n):
-        def mk(i):
-            return lambda e: e.matmul(T[ps][:, c0:c0 + n], T[z][:, 128 * i:128 * i + 128], T[src][:, a0 + i:a0 + 16 * n:16], i == 0, i == 15)
-        op("t", [R(z), R(src, a0, a0 + 16 * n)], [R(ps)], [mk(i) for i in range(16)])
+    def sca2(win, off, a, b):
+        op("v", [a, b, off], [win], [lambda e: e.tensor_tensor(out=ap(win).indirect(ap(off)), in0=ap(a), in1=ap(b), op=A.add)])
+
+    def iof(n, a, b, pat, base):
+        op("g", [], [R(n, a, b)], [lambda e: e.iota(T[n][:, a:b], pat, base, 0, allow_small_or_imprecise_dtypes=True)])
+
+    def zero(n, a, b):
+        iof(n, a, b, [[0, b - a]], 0)
+
+    def ZR(z):
+        return R("z", 144 * ZN.index(z), 144 * ZN.index(z) + 144)
+
+    def f2p(ps, c0, n, mode, terms, minus=(), first=True, last=True):
+        mm, rd = [], []
+        for z, src, a0 in terms:
+            k = 8 if mode == "d" else 16
+            rd.append(R(src, a0, a0 + k * n))
+            for i in range(k):
+                zi = z[i % 2] if isinstance(z, tuple) else z
+                o = 144 * ZN.index(zi) + 15 - (2 * i if mode == "d" else i)
+                rd.append(ZR(zi))
+                mm.append((T.z[:, o:o + 128], T[src][:, a0 + n * i:a0 + n * i + n] if mode == "c" else T[src][:, a0 + i:a0 + k * n:k]))
+        for r in minus:
+            rd += [r, R("nid")]
+            mm.append((T.nid[:, :], ap(r)))
+        op("t", rd, [R(ps)], [lambda e, k=k, l=l, x=x: e.matmul(T[ps][:, c0:c0 + n], l, x, first and k == 0, last and k == len(mm) - 1)
+                              for k, (l, x) in enumerate(mm)])
 
     def p2f(tab, row, col, src, c0, n):
         out = R(tab, col, col + 16 * n, 1, row)
         dma("y", out, R(src, c0, c0 + n), ap(out), T[src][:, c0:c0 + n])
+
+    def halves(src, a, b, h, l, ha, q="s"):
+        if q == "s":
+            act(R(h, ha, ha + b - a), R(src, a, b))
+        else:
+            cp(R(h, ha, ha + b - a), R(src, a, b))
+        tt(R(l, ha, ha + b - a), R(src, a, b), R(h, ha, ha + b - a), A.subtract)
 
     def route(c):
         r = T.rank_of(c)
@@ -194,13 +230,13 @@ def rank_program(g, core, T, topo):
             if len(x) == k and len(y) == k:
                 return nb, ([x, y] if first == 0 else [y, x]), k
 
-    nb, eng, kk = route(core)
-    arrive = route(nb[0])[2] + route(nb[1])[2]
+    nbr, eng, kk = route(core)
+    arrive = route(nbr[0])[2] + route(nbr[1])[2]
 
     def send(kind, t, src, dst, d0, w):
         tr = []
         for s in range(2):
-            rid, pid, _se = topo.addr(nb[s])
+            rid, pid, _se = topo.addr(nbr[s])
             tr.append(RemoteDMATransfer(dst_ids=[DstId(rid=rid, pnc=pid)], dma_engine_mask=sum(1 << z for z in eng[s]),
                                         remote_sem=T.sem["a%s%d" % (kind, t)], src=T[src][:, s * w:s * w + w],
                                         dst=T[dst][:, d0 + (1 - s) * w:d0 + (2 - s) * w]))
@@ -210,436 +246,454 @@ def rank_program(g, core, T, topo):
     def arrived(kind, t, dst, d0, w):
         land([R(dst, d0, d0 + 2 * w)], "a%s%d" % (kind, t), arrive)
 
+    def sendbases(t, src):
+        ts(R("bes", 0, 8), R(src, 0, 8), -3440.0, A.add, 144.0, A.max)
+        ts(R("bes", 8, 16), R(src, 8, 16), -3712.0, A.add)
+        send("be", t, "bes", "bel%d" % t, 0, 8)
+
     def load(q, out, src):
         dma(q, out, None, ap(out), src)
-    load("s", R("xin", 320, 480), T.bs[:, :])
+    load("y", R("xin", 320, 480), T.bs[:, :])
+    load("s", R("sin", 0, 16), T.snd[:, :])
     load("y", R("xin", 0, 160), T.lt[:, :])
     load("s", R("xin", 160, 320), T.rt[:, :])
     for s in range(2):
-        load("y", R("sin", 8 * s, 8 * s + 8), T.snd[:, 128 * s:128 * s + 128])
-    load("y", R("ev", 0, P0), T.err[:, :])
-    load("y", R("win", 0, 1), T.wt[:, :])
-    load("y", R("win", 1, 2), T.th[:, :])
-    load("s", R("dr"), T.det[:, :])
+        load("s", R("sin", 16 + 8 * s, 24 + 8 * s), T.snd[:, 128 * s:128 * s + 128])
+    load("y", R("ew", S0, S0 + P0), T.err[:, :])
+    load("s", R("wti", 0, 1), T.wt[:, :])
+    load("s", R("wti", 1, 2), T.th[:, :])
+    load("s", R("eo", 0, DA[0]), T.err[:, 0:DA[0]])
 
     op("g", [], [R("pid", 0, 1)], [lambda e: e.iota(T.pid[:, 0:1], [[1, 1]], 0, 1)])
-
-    def iof(n, a, b, pat, base):
-        op("g", [], [R(n, a, b)], [lambda e: e.iota(T[n][:, a:b], pat, base, 0, allow_small_or_imprecise_dtypes=True)])
     fill(R("bo"), 1.0)
-    iof("cc", 0, 224, [[1, 224]], 0)
+    iof("cc", 0, 192, [[1, 192]], 0)
+    fill(R("win"), 1.0)
+    op("g", [R("bo")], [R("nid")], [lambda e: e.affine_select(T.nid[:, :], T.bo[:, :], [[-1, 128]], A.is_equal, 0.0, 0, 1)])
     op("g", [R("bo")], [R("bo")], [lambda e: e.affine_select(T.bo[:, :], T.bo[:, :], [[-16, 8], [0, 16]], A.is_ge, 0.0, 0, 1)])
     op("g", [R("bo")], [R("bo")], [lambda e: e.affine_select(T.bo[:, :], T.bo[:, :], [[16, 8], [0, 16]], A.is_ge, 0.0, 15, -1)])
-    iof("i16", 0, 16, [[1, 16]], 0)
-    iof("ev", P0, 3600, [[0, 1040]], 0)
-    iof("xs", 0, 16, [[128, 2], [1, 8]], GH)
-    iof("gv", 0, 256, [[128, 2], [1, 16], [16, 8]], 16)
-    op("g", [R("bo")], [R("ltm")], [lambda e: e.affine_select(T.ltm[:, :], T.bo[:, :], [[1, 128]], A.is_gt, 0.0, 0, -1)])
+    op("g", [R("bo")], [R("ltm")], [lambda e: e.affine_select(T.ltm[:, :], T.bo[:, :], [[1, 128]], A.is_ge, 0.0, 0, -1)])
     ts(R("pid", 1, 2), R("pid", 0, 1), 15, A.bitwise_and)
-    fill(R("zz"), 0.0)
+    fill(R("z0"), 0.0)
     ts(R("pid", 2, 3), R("pid", 1, 2), 1, A.logical_shift_right)
     cp(R("ci", 0, 1), R("pid", 1, 2))
     cp(R("ci", 1, 2), R("pid", 2, 3))
-    fill(R("tb"), 8192.0)
-    I1 = R("ci", 0, 1)
-    ts(R("ci", 6, 7), I1, float(W0), A.add)
-    ts(R("mk2"), R("i16", 0, 8), R("ci", 1, 2), A.is_equal)
-    ts(R("ix"), R("cc"), 16.0, A.mult, R("ci", 6, 7), A.add)
+    I1, I2 = R("ci", 0, 1), R("ci", 1, 2)
+    for k, (f, b) in enumerate(((160.0, 0.0), (64.0, float(P0)), (192.0, 0.0), (8.0, float(GH))), 2):
+        ts(R("ci", k, k + 1), I1, f, A.mult, b, A.add)
+    MC = (R("mc", 0, 160), R("mc", 224, 416))
+    ts(R("mc", 0, 160), R("cc", 0, 160), R("ci", 2, 3), A.add)
+    ts(R("mc", 160, 224), R("cc", 0, 64), R("ci", 3, 4), A.add)
+    halves("mc", 0, 224, "mh", "ml", 0, "v")
+    W0 = 192
+    ROW = {"l": 4, "r": 2, "b": 0}
+    for x, c, o in (("b", 320, 2), ("l", 0, 0), ("r", 160, 1)):
+        cp(R("px0", W0 * o, W0 * o + 160), R("xin", c, c + 160))
+        halves("px0", W0 * o, W0 * o + 160, "hi", "lo", W0 * o)
+        for k, src in enumerate(("hi", "lo")):
+            p2f("win", ROW[x] + k, S0, src, W0 * o, 160)
+        if x == "b":
+            ts(R("sa"), R("sin"), float(S0), A.add)
+    for k, src in enumerate(("mh", "ml")):
+        p2f("win", 6 + k, S0, src, 0, 160)
+        for row in (0, 2, 4, 6):
+            p2f("win", row + k, S0 + P0, src, 160, 64)
+    ts(R("mk2"), R("cc", 0, 8), I2, A.is_equal)
+    ts(R("mk"), R("cc", 0, 16), I1, A.is_equal)
+    cp(R("z0", 15, 143, 16), R("bo", 0, 128, 16))
+    cp(R("z0", 159, 287, 16), R("bo", 0, 128, 16))
+    cp(R("z0", 160, 288, 16), R("bo", 0, 128, 16))
+    ts(R("ci", 6, 7), R("mk", 15, 16), float(S0), A.mult)
+    ts(R("zc", 0, 5), R("mk2", 0, 5), R("ci", 6, 7), A.add)
+    Z1, Z2 = R("z0", 0, 144), R("z0", 144, 288)
 
-    def halves(src, a, b, h, l, ha, q="v"):
-        if q == "s":
-            act(R(h, ha, ha + b - a), R(src, a, b))
+    def zmat(z, col, f=None, src=Z1):
+        if f is None:
+            ts(ZR(z), src, col, A.mult)
         else:
-            cp(R(h, ha, ha + b - a), R(src, a, b))
-        tt(R(l, ha, ha + b - a), R(src, a, b), R(h, ha, ha + b - a), A.subtract)
-    OFF = {"l": 0, "r": 224, "b": 448}
-    TROW = {"b": 0, "r": 2, "l": 6}
+            ts(ZR(z), src, col, A.mult, f, A.mult)
+    for z, k in (("zB16", 0), ("zR16", 1), ("zL16", 2), ("zT16", 4)):
+        zmat(z, R("zc", k, k + 1))
+    for z, k in (("zE", 3), ("zB", 0), ("zR", 1), ("zL", 2)):
+        zmat(z, R("mk2", k, k + 1))
+    zmat("zMB", R("mk2", 0, 1), float(M))
+    ts(R("ci", 7, 8), R("mk", 0, 1), 3840.0, A.mult)
+    ts(R("snf"), R("win", M - 416, M), 0.0, A.mult, R("ci", 7, 8), A.add)
+    cp(R("sn", 16, 32), R("sin", 16, 32))
+    cp(R("su", 16, 32), R("sa", 16, 32))
 
-    def table(x, t, q="v"):
-        o, n = OFF[x], 160 + 32 * t
-        halves("px", o, o + n, "hi", "lo", o, q)
-        for k, src in ((0, "hi"), (1, "lo")):
-            for tab in (("tc", "tb") if t and x == "b" else ("tb",)):
-                p2f(tab, TROW[x] + k, 0, src, o, 160)
-                if t:
-                    p2f(tab, TROW[x] + k, P0, src, o + 160, 32)
-
-    def slots(t):
-        halves("sn", 0, 16, "shi", "slo", 0)
-        for k, src in ((0, "shi"), (1, "slo")):
+    def slots():
+        halves("sn", 16, 32, "shi", "slo", 0, "v")
+        for k, src in enumerate(("shi", "slo")):
             for s in range(2):
-                p2f("snf", k, 128 * s, src, 8 * s, 8)
+                p2f("snf", k, 16 + 144 * s, src, 8 * s, 8)
+    slots()
+    load("y", R("dr"), T.det[:, :])
+    ts(R("me"), R("cc"), 16.0, A.mult, I1, A.add)
+    ts(R("me16"), R("me"), float(S0), A.add)
+    ts(R("mme", 16, 208), R("me"), float(M), A.mult)
+    for w in ("ew", "w1", "uw"):
+        fill(R(w, 0, S0), 0.0)
+        fill(R(w, S0 + P0, GC), 0.0)
+        fill(R(w, M, M + 16), 0.0)
+    fill(R("msk"), 1.0)
+    fill(R("msk", 0, 2304, 3), 0.0)
+    iof("krow", 0, 256, [[1, 256]], 0)
+    iof("tg", 0, 192, [[0, 12], [1, 16]], 0)
+    iof("xs", 16, 32, [[128, 2], [1, 8]], S0)
+    iof("it", 0, 512, [[32, 16], [0, 32]], P0)
+    iof("it", 512, 1024, [[0, 16], [1, 32]], 0)
+    iof("it", 1024, 1536, [[0, 16], [2, 16], [-1, 2]], 1)
 
-    def nat(s, i, src):
-        a = 128 * s + 16 * (i & 7) + (i >> 3)
-        return lambda e: e.matmul(T.ps0[:, 8 * s:8 * s + 8], T.zb[:, 128 * i:128 * i + 128], T[src][:, a:a + 15:2], i == 0, i == 15)
+    def later():
+        for z, k in (("zN0", 5), ("zN1", 6)):
+            zmat(z, R("mk2", k, k + 1))
+        for z, k in (("zG0", 5), ("zG1", 6)):
+            zmat(z, R("mk2", k, k + 1), 1.0 / KR)
+        cp(R("ci", 8, 10), R("wti"))
+        zmat("zz", 1.0)
+        zmat("z16", 16.0)
+        zmat("zh", R("ci", 8, 9))
+        for z, f in (("d1", 1.0), ("d16", 16.0), ("d256", 256.0)):
+            zmat(z, f, None, Z2)
+        ts(R("ci", 10, 11), R("ci", 9, 10), -1.0, A.mult, 0.5, A.add)
+        ts(R("nid"), R("nid"), -1.0, A.mult)
+        ts(R("dm"), R("tg"), I1, A.is_le, BIG, A.mult)
+        for w in ("cb", "cw1", "cw2"):
+            fill(R(w), BIG)
+        fill(R("cb", 0, 1), 0.0)
+        ts(R("xs", 0, 16), R("me", 0, 16), float(GC), A.add)
+        ts(R("xs", 16, 32), R("xs", 16, 32), R("ci", 5, 6), A.add)
+        ts(R("kj"), R("cc", 0, 32), 8.0, A.mult, I2, A.add)
+        ts(R("dj"), R("me", 0, 32), float(M), A.add)
+        ts(R("mc", 224, 416), R("cc"), R("ci", 4, 5), A.add)
+        halves("mc", 224, 416, "mh", "ml", 224, "v")
+        fill(R("inv"), 0.0)
+        ts(R("dh", 0, 2048), R("dr"), 0.5, A.mult, 127.8, A.add)
+        fill(R("dl", 2048, 2064), -128.0)
+        act(R("dl", 0, 2048), R("dh", 0, 2048), 1.0, -256.0)
 
-    def bases(src, tab):
-        gat("s", R(src), R(tab), R("snu"))
-        for s in range(2):
-            op("t", [R("zb"), R(src)], [R("ps0")], [nat(s, i, src) for i in range(16)])
+    def newrows(t):
+        zero("nc%d" % t, 0, 512)
+        hi = 1536 * t
+        if t:
+            iof("it", hi, hi + 512, [[32, 16], [0, 32]], P0 + 512)
+        for row, c in ((10 + 2 * t, hi), (11 + 2 * t, 512), (2 * t, hi), (2 * t + 1, 1024)):
+            out = R("nc%d" % t, 0, 512, 1, row)
+            dma("y", out, R("it", c, c + 512), ap(out), T.it[0:8, c:c + 512])
 
-    def sendbases(t):
-        cp(R("bes"), R("ps0", 0, 16))
-        send("be", t, "bes", "bel%d" % t, 0, 8)
-
-    halves("ix", 0, 224, "ihi", "ilo", 0)
-    for k, src in ((4, "ihi"), (5, "ilo")):
-        p2f("tb", k, 0, src, 0, 160)
-        p2f("tb", k, P0, src, 160, 32)
-    for x, c in (("b", 320), ("l", 0), ("r", 160)):
-        cp(R("px", OFF[x], OFF[x] + 160), R("xin", c, c + 160))
-        table(x, 0, "s")
-    cp(R("sn"), R("sin"))
-    cp(R("snu"), R("sn"))
-    op("v", [R("bo")], [R("zz")], [lambda e, i=i: e.tensor_copy(out=T.zz[:, 129 * i:128 * i + 128:16], in_=T.bo[:, i::16]) for i in range(16)])
-    ts(R("zb"), R("zz"), R("mk2", 0, 1), A.mult)
-    fill(R("snf"), 0.0)
-    slots(0)
-    ts(R("bv", 0, 160), R("px", 448, 608), float(GH - 1), A.min)
-    ts(R("ci", 2, 3), I1, 160.0, A.mult)
-    ts(R("ci", 3, 4), I1, 32.0, A.mult, 2400.0, A.add)
-    ts(R("ci", 4, 5), I1, 32.0, A.mult, 2880.0, A.add)
-    ts(R("ci", 5, 6), I1, 8.0, A.mult)
-    bases("gs", "tb")
-    ts(R("me", 0, 160), R("cc", 0, 160), R("ci", 2, 3), A.add)
-    ts(R("me", 160, 192), R("cc", 160, 192), R("ci", 3, 4), A.add)
-    ts(R("me", 192, 224), R("cc", 192, 224), R("ci", 4, 5), A.add)
-    ts(R("xs"), R("xs"), R("ci", 5, 6), A.add)
-    ts(R("mk"), R("i16"), I1, A.is_equal)
-    ts(R("i8", 1, 2), R("mk2", 0, 1), 4096.0, A.mult)
-    ts(R("snf", 256, 272), R("i16"), 0.0, A.mult, R("i8", 1, 2), A.add)
-    for w in ("eu", "wa", "wb"):
-        fill(R(w, 0, 16), 0.0)
-    sendbases(0)
-    ts(R("zr"), R("zz"), R("mk2", 1, 2), A.mult)
-    ts(R("zl"), R("zz"), R("mk2", 3, 4), A.mult)
-    ts(R("zi"), R("zz"), R("mk2", 2, 3), A.mult)
-    cp(R("gh1"), R("gv"))
-    tt(R("gl1"), R("gv"), R("gh1"), A.subtract)
-    ts(R("gh1"), R("gh1"), R("mk", 4, 5), A.mult)
-    ts(R("gl1"), R("gl1"), R("mk", 5, 6), A.mult)
-    tt(R("gi"), R("gh1"), R("gl1"), A.add)
-    errors = [None]
-
+    WIN = R("win")
     for t in range(2):
-        n = 160 + 32 * t
-        NL, base = 16 * n, P0 + 512 * t
-        nw0 = n
-        h = n // 2
-        E = ((0, h), (h, n))
-        NE = [(W0 + 16 * a, W0 + 16 * b) for a, b in E]
-        EC = [R("ec", 16 * a, 16 * b) for a, b in E]
-        ntb = "nt%d" % t
-        PL, PR, PB = R("px", 0, n), R("px", 224, 224 + n), R("px", 448, 448 + n)
-        ME, WIN = R("me", 0, n), R("tb")
-        WE = R("eu", 0, W0 + NL)
+        m = 160 + 32 * t
+        n, w = 16 * m, m + 32
+        base, d, nsb = n, DA[t], m // 16
+        px = "px%d" % t
+        PL, PR, PB = R(px, 0, m), R(px, w, w + m), R(px, 2 * w, 2 * w + m)
+        cut = [d // 16 + (m - d // 16) * k // CC[t] // 2 * 2 for k in range(CC[t] + 1)]
+        CH = list(zip(cut[:-1], cut[1:]))
+        PC = [(0, 16 + d // 16)] + [(16 + a, 16 + b) for a, b in CH]
+        EW, W1, UW = R("ew"), R("w1"), R("uw")
 
-        def keep(src, k):
-            act(EC[k], R(src, *NE[k]))
+        def sl(buf, a, b, k):
+            return R(buf, 3 * (16 * a - d) + k, 3 * (16 * b - d), 3)
+
+        def L(x, a, b):
+            return R(x, 16 + a, 16 + b)
+
+        def col(buf, a, b):
+            return R(buf, S0 + 16 * a, S0 + 16 * b)
         if t == 0:
-            gat("s", R("x0"), R("ev", 0, 3600), R("snu"))
-            send("x0", t, "x0", "eu", 16, 128)
+            gat("s", R("gs"), WIN, R("sa"))
+            f2p("ps3", 0, 16, "c", [("zB16", "gs", 0)])
+            f2p("ps2", 0, m, "i", [("zB16", "win", S0)])
+            sendbases(0, "ps3")
+            cp(R("bt", 0, 16), R("ps3", 0, 16))
+            f2p("ps4", 0, 16, "c", [("zE", "gs", 0)])
+            ts(R("bv", 0, m), R("ps2", 0, m), float(GC - 1), A.min)
+            ts(R("su", 0, 16), R("ps4", 0, 16), float(S0), A.add)
+            cp(R("sn", 0, 16), R("ps4", 0, 16))
+            gat("s", R("x0"), R("ew", 0, GC), R("su", 0, 16))
+            send("x0", 0, "x0", "ew", GC, 128)
+            act(R("mme", 0, 16), R("sn", 0, 16), float(M))
+            for ps, z in (("ps0", "zL16"), ("ps1", "zR16")):
+                f2p(ps, 0, 16, "c", [(z, "gs", 0)])
+                f2p(ps, 16, m, "i", [(z, "win", S0)])
+            f2p("ps4", 16, 16, "i", [("zR16", "gs", 256)])
+            hb2 = m // 2
+            gat("s", R("gb", 16 * hb2, n), WIN, R("bv", hb2, m))
+            tt(R("gt", 0, m), R("ps2", 0, m), R("me16", 0, m), A.is_gt)
+            gat("v", R("gb", 0, 16 * hb2), WIN, R("bv", 0, hb2))
+            zero("nb", 0, M)
         else:
-            gat("s", R("gs"), WIN, R("snu"))
-        f2p("ps1", 0, "zl", "gs", 0, 16)
-        f2p("ps1", 16, "zr", "gs", 0, 16)
-        f2p("ps1", 32, "zi", "gs", 0, 16)
-        gat("s", R("gb", 0, NL), WIN, R("bv", 0, n))
-        cp(R("slu"), R("ps1", 0, 32))
-        ts(R("siu"), R("ps1", 32, 48), -float(W0), A.add)
-        tt(R("srf"), R("ps1", 16, 32), R("xs"), A.is_equal)
-        f2p("ps2", 0, "zb", "gb", 0, n)
-        f2p("ps3", 0, "zi", "gb", 0, n)
-        f2p("ps4", 0, "zr", "gb", 0, n)
-        cp(R("lv", 0, n), PL)
-        cp(R("rv", 0, n), PR)
-        if t:
-            errors[0]()
-            gat("s", R("x0"), R("eu", W0, W0 + NL), R("siu"))
-            send("x0", t, "x0", "eu", 16, 128)
-            keep("eu", 0)
-            keep("eu", 1)
-        arrived("be", t, "bel%d" % t, 0, 8)
-        bl = "bel%d" % t
-        ts(R("gm"), R(bl), 3712.0, A.is_ge)
-        ts(R("gm1"), R(bl, 8, 16), 3584.0, A.is_ge)
-        ts(R("gd", 0, 8), R(bl, 0, 8), -3968.0, A.add)
-        ts(R("gd", 8, 16), R(bl, 8, 16), -3712.0, A.add)
-        tt(R("gm", 8, 16), R("gm1"), R("gm", 8, 16), A.subtract)
-        tt(R("gd"), R("gd"), R("gm"), A.mult)
-        ts(R("gbu"), R("gd"), 256.0, A.add)
-        gat2(R("tb", GH, 3840), R("snf"), R("gbu"), R("gi"), A.add)
-        for k, (a, b) in enumerate(E):
+            gat("s", R("gs", 0, 256), WIN, R("su", 0, 16))
+            for ps, z in (("ps0", "zL16"), ("ps1", "zR16")):
+                f2p(ps, 16, m, "i", [(z, "win", S0)])
+                f2p(ps, 0, 16, "i", [(z, "gs", 0)])
+            f2p("ps2", 0, m, "i", [("zB16", "win", S0)])
+        for ps, v, x in (("ps0", "lv", "lm"), ("ps1", "rv", "rm")):
+            cp(R(v, 0, 16 + m), R(ps, 0, 16 + m))
+            tt(R(x, 0, 16 + m), R(ps, 0, 16 + m), R("mme", 0, 16 + m), A.subtract)
+        if t == 0:
+            cp(R("bt", 64, 80), R("ps4", 16, 32))
+            for a, b in CH:
+                cp(sl("za", a, b, 2), col("ew", a, b))
+            arrived("be", 0, "bel0", 0, 8)
+            gat("v", R("win", GC, M), R("snf"), R("bel0"))
+        VB = ("ps4", "ps5", "ps6", "ps7")
+
+        def legs(k, x):
+            a, b = PC[k]
+            ps = VB[(2 * k + (x == "r")) % 4]
+            f2p(ps, 0, b - a, "i", [("zMB", "g" + x, 16 * a)])
+            o = 208 * (x == "r")
+            tt(R("dd", o + a, o + b), R(ps, 0, b - a), R(x + "m", a, b), A.add)
+            ts(R(x + "w", a, b), R("dd", o + a, o + b), float(M), A.min)
+        for k, (a, b) in enumerate(PC):
             gat("v", R("gl", 16 * a, 16 * b), WIN, R("lv", a, b))
-            if k == 0:
-                gat("s", R("gx"), WIN, R("slu"))
             gat("s", R("gr", 16 * a, 16 * b), WIN, R("rv", a, b))
-        for k, (a, b) in enumerate(E):
-            f2p("ps5" if k == 0 else "ps7", 0, "zb", "gl", 16 * a, b - a)
-            f2p("ps6" if k == 0 else "ps0", 0, "zi", "gl", 16 * a, b - a)
+            if k == 0 and t:
+                ts(R("bv", 0, m), R("ps2", 0, m), float(GC - 1), A.min)
+                tt(R("gt", 0, m), R("ps2", 0, m), R("me16", 0, m), A.is_gt)
+            if k:
+                legs(k - 1, "l")
+                legs(k - 1, "r")
+        XL, XR = R("lw", 0, 16), R("rw", 0, 16)
+
+        def three(win, own, slots_, out, dst, side):
+            for k, (a, b) in enumerate(CH):
+                gat("s", sl(slots_, a, b, 0), win, L("lw", a, b))
+                gat("s", sl(slots_, a, b, 1), win, L("rw", a, b))
+            side(0)
+            gat2(R("ta", 0, d), win, L("lw", 0, d // 16), own, A.max)
+            side(1)
+            gat2(col(dst, 0, d // 16), win, L("rw", 0, d // 16), R("ta", 0, d), A.max)
+            side(2)
+            for k, (a, b) in enumerate(CH):
+                u, v = 3 * (16 * a - d), 3 * (16 * b - d)
+                scan(R(out, u, v), R("msk", 0, v - u), R(slots_, u, v), A.mult, A.max)
+                cp(col(dst, a, b), sl(out, a, b, 2))
+                side(3 + k)
+
+        arrived("x0", t, "ew", GC, 128)
+        legs(len(PC) - 1, "l")
+
+        def side1(k):
             if k == 0:
-                f2p("ps1", 0, "zb", "gx", 0, 32)
-                f2p("ps1", 32, "zi", "gx", 0, 32)
-        if t == 0:
-            op("v", [R("ev", 0, P0)], [R("eu", W0, W0 + P0)],
-               [lambda e, i=i: e.tensor_copy(out=T.eu[:, W0 + i:W0 + P0:16], in_=T.ev[:, 160 * i:160 * i + 160]) for i in range(16)])
-            keep("eu", 0)
-            keep("eu", 1)
-
-        def legs(ps, ps2, a, b, v, f, w):
-            tt(R(v, a, b), R(ps, 0, b - a), R("me", a, b), A.is_equal)
-            tt(R(f, a, b), R(ps2, 0, b - a), R(v, a, b), A.mult)
-            cp(R(w, a, b), R(f, a, b))
-        legs("ps5", "ps6", E[0][0], E[0][1], "vl", "lf", "lw")
-        for x in (0, 16):
-            tt(R("xv", x, x + 16), R("ps1", x, x + 16), R("sn"), A.is_equal)
-        tt(R("xf"), R("ps1", 32, 64), R("xv"), A.mult)
-        cp(R("xlu"), R("xf"))
-        arrived("x0", t, "eu", 16, 128)
-        gat2(R("wa", *NE[0]), WE, R("lw", *E[0]), EC[0], A.max)
-        gat2(R("x1"), WE, R("xlu", 0, 16), R("x0"), A.max)
-        gat2(R("x1"), WE, R("xlu", 16, 32), R("x1"), A.max)
-        send("x1", t, "x1", "wa", 16, 128)
-        if t == 0:
-            iof("cv", 0, 3072, [[0, 3072]], 1)
-        legs("ps7", "ps0", E[1][0], E[1][1], "vl", "lf", "lw")
-        gat2(R("wa", *NE[1]), WE, R("lw", *E[1]), EC[1], A.max)
-        for k, (a, b) in enumerate(E):
-            f2p("ps5" if k == 0 else "ps7", 0, "zb", "gr", 16 * a, b - a)
-            f2p("ps6" if k == 0 else "ps0", 0, "zi", "gr", 16 * a, b - a)
-            legs("ps5" if k == 0 else "ps7", "ps6" if k == 0 else "ps0", a, b, "vr", "rf", "rw")
-            gat2(R("wa", *NE[k]), WE, R("rw", a, b), R("wa", *NE[k]), A.max)
-            keep("wa", k)
-        f2p("ps5", 0, "zr", "gl", 0, n)
-        f2p("ps6", 0, "zr", "gr", 0, n)
-        arrived("x1", t, "wa", 16, 128)
-        WWA, WWB = R("wa", 0, W0 + NL), R("wb", 0, W0 + NL)
-        gat2(R("x2"), WWA, R("xlu", 0, 16), R("x1"), A.max)
-        gat2(R("x2"), WWA, R("xlu", 16, 32), R("x2"), A.max)
-        send("x2", t, "x2", "wb", 16, 128)
-        if t == 0:
-            for tab in ("nt0", "tc", "nt1"):
-                iof(tab, 0, 3840, [[0, 3840]], 0)
-            act(R("df"), R("dr"), 0.5, -0.25)
-            act(R("df"), R("df"), 1.0, 8388608.0)
-
-        def bulk(dst, win):
-            for k in range(2):
-                gat2(R(dst, *NE[k]), win, R("lw", *E[k]), EC[k], A.max)
-            for k in range(2):
-                gat2(R(dst, *NE[k]), win, R("rw", *E[k]), R(dst, *NE[k]), A.max)
-                keep(dst, k)
-        bulk("wb", WWA)
-        tt(R("eq", 0, n), R("ps2", 0, n), ME, A.is_equal)
-        tt(R("pt", 0, n), PB, ME, A.is_gt)
-        tt(R("bf", 0, n), R("ps3", 0, n), R("eq", 0, n), A.mult)
-        tt(R("pt", 0, n), R("pt", 0, n), R("eq", 0, n), A.mult)
-        cp(R("bw", 0, n), R("bf", 0, n))
-        ts(R("thr", 0, n), R("pt", 0, n), -93.0, A.mult, 99.0, A.add)
-        tt(R("rb", 0, n), R("ps4", 0, n), ME, A.is_equal)
-        tt(R("rl", 0, n), R("ps5", 0, n), ME, A.is_equal)
-        tt(R("rr", 0, n), R("ps6", 0, n), ME, A.is_equal)
-        if t == 0:
-            cp(R("ci", 7, 8), R("win", 1, 2))
-            cp(R("i8", 0, 1), R("win", 0, 1))
-            fill(R("zero"), 0.0)
-            fill(R("dh", 2048, 2064), 0.0)
-            ts(R("ixm"), R("ix", 0, 192), -16.0, A.add)
-            halves("me", 0, 224, "chi", "clo", 0, "s")
-            for k, src in ((0, "chi"), (1, "clo")):
-                p2f("cv", k, 0, src, 0, 160)
-                p2f("cv", k, P0, src, 160, 32)
-            for k in range(3):
-                act(R("px", 224 * k + 192, 224 * k + 224), R("me", 192, 224))
-            act(R("dh", 0, 2048), R("df"), 1.0, -8388608.0)
-            act(R("zh"), R("zz"), R("i8", 0, 1))
-        TH = R("ci", 7, 8)
-        fill(R("ct", 0, 256), 0.0)
-        arrived("x2", t, "wb", 16, 128)
-        bulk("wa", WWB)
-        if t == 0:
-            op("s", [R("cv")], [R("vf")],
-               [lambda e, i=i: e.activation(out=T.vf[:, i:P0:16], in_=T.cv[:, 160 * i:160 * i + 160], func=CP) for i in range(16)] +
-               [lambda e, i=i: e.activation(out=T.vf[:, P0 + i:3072:16], in_=T.cv[:, P0 + 32 * i:P0 + 32 * i + 32], func=CP) for i in range(16)])
-        else:
-            op("s", [R("eu", W0, W0 + 3072)], [R("ev", 0, 3072)],
-               [lambda e, i=i: e.activation(out=T.ev[:, 160 * i:160 * i + 160], in_=T.eu[:, W0 + i:W0 + P0:16], func=CP) for i in range(16)] +
-               [lambda e, i=i: e.activation(out=T.ev[:, P0 + 32 * i:P0 + 32 * i + 32], in_=T.eu[:, W0 + P0 + i:W0 + 3072:16], func=CP) for i in range(16)])
-        for k, (a, b) in enumerate(E):
-            gat2(R("hb", 16 * a, 16 * b), WWA, R("bw", a, b), EC[k], A.max)
-            ts(R("hb", 16 * a, 16 * b), R("hb", 16 * a, 16 * b), TH, A.is_ge)
-            f2p("ps4", a, "zz", "hb", 16 * a, b - a)
-        tt(R("hot", 0, n), R("ps4", 0, n), R("thr", 0, n), A.is_ge)
-        segs = [(0, 160)] + ([(160, 192)] if t else [])
-        for a, b in segs:
-            op("v", [R("hot", a, b), R("zero", a, b)], [R("cum", a, b)],
-               [lambda e, a=a, b=b: e.tensor_tensor_scan(T.cum[:, a:b], T.hot[:, a:b], T.zero[:, a:b], 0.0, A.add, A.add)])
-        op("t", [R("ltm"), R("cum", 0, 160)], [R("ps0")], [lambda e: e.matmul(T.ps0[:, 0:1], T.ltm[:, :], T.cum[:, 159:160], True, True)])
+                gat2(R("xa"), EW, XL, R("x0"), A.max)
+                gat2(R("x1"), EW, XR, R("xa"), A.max)
+                send("x1", t, "x1", "w1", GC, 128)
+                if t == 0:
+                    zero("rn", int(KL) - RN0 + S0, int(KL) - RN0 + S0 + 3072)
+        legs(len(PC) - 1, "r")
+        three(EW, R("eo", 0, d), "za", "zb", "w1", side1)
         if t:
-            op("t", [R("ltm"), R("bo"), R("cum")], [R("ps0")],
-               [lambda e: e.matmul(T.ps0[:, 1:2], T.ltm[:, :], T.cum[:, 191:192], True, False),
-                lambda e: e.matmul(T.ps0[:, 1:2], T.bo[:, :], T.cum[:, 159:160], False, True)])
-        for k, (a, b) in enumerate(segs):
-            ts(R("k1", a, b), R("cum", a, b), R("ps0", k, k + 1), A.add)
-        ts(R("sel", 0, n), R("k1", 0, n), 256.0, A.is_le)
-        ts(R("kn", 0, n), R("k1", 0, n), 2.0, A.mult, -2.0, A.add)
-        tt(R("sel", 0, n), R("sel", 0, n), R("hot", 0, n), A.mult)
-        act(R("n1", 0, n), R("sel", 0, n), float(base))
-        act(R("wr", 0, n), R("sel", 0, n), -BIG, BIG - 1.0)
-        tt(R("n0", 0, n), R("kn", 0, n), R("sel", 0, n), A.mult)
+            for k, z in enumerate(("zL", "zR", "zB")):
+                f2p("ps%d" % k, 0, m, "c", [(z, "win", S0)])
+                act(R(px, w * k, w * k + m), R("ps%d" % k, 0, m))
+        mh, ml = R("mh", 224 * t, 224 * t + m), R("ml", 224 * t, 224 * t + m)
+        if t == 0:
+            later()
+        g3 = [m * k // 3 // 2 * 2 for k in range(4)]
 
-        def rows(lst):
-            for row, src in lst:
-                p2f(ntb, row, 0, src, 0, 160)
-                if t:
-                    p2f(ntb, row, P0, src, 160, 32)
-        rows(((1, "n1"), (0, "n0")))
-        gat("s", R("gb", 0, NL), R(ntb), R("bv", 0, n))
-        tt(R("dd", 0, n), R("wr", 0, n), R("k1", 0, n), A.add)
-        tt(R("dd", 0, n), R("dd", 0, n), R("ixm", 0, n), A.min)
-        cp(R("pd", 0, n), R("dd", 0, n))
-        sp = 96 + 16 * t
-        sca(R("ct", 0, 256 + NL), R("pd", 0, sp), R("vf", 0, 16 * sp))
-        f2p("ps1", 0, "zz", "gb", 0, n)
-        tt(R("nc", 0, n), R("ps1", 0, n), R("eq", 0, n), A.mult)
-        ts(R("sc", 0, n), R("nc", 0, n), 1.0, A.min)
-        halves("nc", 0, n, "nchi", "nclo", 0)
-        rows(((4, "sc"), (2, "nchi"), (3, "nclo")))
-        sca(R("ct", 0, 256 + NL), R("pd", sp, n), R("vf", 16 * sp, NL))
+        def bases(k):
+            if t:
+                gat("s", R("gb", 16 * g3[k], 16 * g3[k + 1]), WIN, R("bv", g3[k], g3[k + 1]))
+        bases(0)
+        for k, z in enumerate(("zL", "zR", "zB")):
+            f2p("ps%d" % (4 + k), 0, m, "c", [(z, "gr", 256)], (mh, ml))
+        arrived("x1", t, "w1", GC, 128)
+        gat("v", R("xa"), W1, XL)
+        gat2(R("x2"), W1, XR, R("xa"), A.max)
+        send("x2", t, "x2", "uw", GC, 128)
+        if t == 0:
+            for k in (KR, KB):
+                zero("rn", int(k) - RN0 + S0, int(k) - RN0 + S0 + 3072)
+            newrows(0)
+            newrows(1)
+        c2 = [0, m // 8, 3 * m // 8, 11 * m // 16, m]
+        c2 = [x // 2 * 2 for x in c2]
+        for k, (a, b) in enumerate(zip(c2[:-1], c2[1:])):
+            gat("s", R("tr", 16 * a, 16 * b), W1, L("rw", a, b))
+            gat2(col("uw", a, b), W1, L("lw", a, b), R("tr", 16 * a, 16 * b), A.max)
+        bases(1)
+        arrived("x2", t, "uw", GC, 128)
 
-        def ctp(ps, c, z):
-            op("t", [R(z), R("ct", 0, 256)], [R(ps)],
-               [lambda e, i=i: e.matmul(T[ps][:, c:c + 16], T[z][:, 128 * i:128 * i + 128], T.ct[:, 16 * i:16 * i + 16], i == 0, i == 15) for i in range(16)])
-        ctp("ps2", 0, "zr")
-        ctp("ps2", 16, "zb")
-        gat("s", R("gb", 0, NL), R(ntb), R("bv", 0, n))
-        tt(R("nt", 0, n), R("n0", 0, n), R("n1", 0, n), A.add)
-        tt(R("nc", 0, n), R("nc", 0, n), R("sc", 0, n), A.add)
-        ts(R("st", 0, n), R("nt", 0, n), 1.0, A.min)
-        tt(R("spl", 0, n), R("st", 0, n), R("sc", 0, n), A.add)
-        for s in range(2):
-            ts(R("fl", s, 32, 2), R("ps2", 0, 16), 0.5, A.mult)
-        ts(R("fo"), R("fl"), -float(GH), A.mult, float(GH), A.add)
-        tt(R("tv", 0, 32, 2), R("ps2", 16, 32), R("fo", 0, 32, 2), A.add)
-        cp(R("tu16"), R("tv", 0, 32, 2))
-        gat("s", R("gt"), WIN, R("tu16"))
-        act(R("m8", 0, n), R("spl", 0, n), 8192.0)
-        f2p("ps3", 0, "zb", "gt", 0, 16)
-        f2p("ps0", 0, "zz", "gb", 0, n)
-        tt(R("no", 0, n), R("nt", 0, n), R("nc", 0, n), A.add)
-        tt(R("tv", 1, 32, 2), R("ps3", 0, 16), R("fl", 0, 32, 2), A.mult)
-        tt(R("tv", 1, 32, 2), R("tv", 1, 32, 2), R("fo", 0, 32, 2), A.add)
-        cp(R("tu"), R("tv"))
+        def side3(k):
+            if k == 1:
+                for j, kf in enumerate((KL, KR, KB)):
+                    ts(R("ek", 192 * j, 192 * j + m), R("ps%d" % (4 + j), 0, m), 0.0, A.is_equal, kf, A.mult)
+            if k == 2:
+                tt(R("kh", 0, m), R("ek", 0, m), R("ek", 192, 192 + m), A.max)
+                tt(R("eq", 0, m), PL, PR, A.is_equal)
+                tt(R("kh", 0, m), R("kh", 0, m), R("ek", 384, 384 + m), A.max)
+                tt(R("eq", 192, 192 + m), PL, PB, A.is_equal)
+                tt(R("tg", 0, m), R("kh", 0, m), PR, A.add)
+                tt(R("eq", 384, 384 + m), PR, PB, A.is_equal)
+        three(UW, col("w1", 0, d // 16), "zb", "za", "w1", side3)
+        bases(2)
+        act(R("eo", 0, d), col("w1", 0, d // 16))
+        f2p("ps3", 0, m, "i", [("zB", "gb", 0)])
+        halves("tg", 0, m, "tgh", "tgl", 0)
+        for row, src, c in ((8, "tgh", 0), (9, "tgl", 0), (10 + 2 * t, "ek", 192), (11 + 2 * t, "ek", 192)):
+            p2f("win", row, S0, src, c, m)
+        HC = CH + [(0, d // 32), (d // 32, d // 16)]
+        for k, (a, b) in enumerate(HC):
+            own = sl("za", a, b, 2) if k < len(CH) else R("eo", 16 * a, 16 * b)
+            gat2(R("hb", 16 * a, 16 * b), R("w1", 0, GC), R("bv", a, b), own, A.max)
+            act(R("hb", 16 * a, 16 * b), R("hb", 16 * a, 16 * b), 1.0, R("ci", 10, 11), F.Sign)
+            f2p(VB[k % 4], 0, b - a, "i", [("zz", "hb", 16 * a)])
+            if k == 0:
+                tt(R("wq", 0, m), R("ps3", 0, m), R("me", 0, m), A.is_equal)
+                tt(R("gt", 0, m), R("gt", 0, m), R("wq", 0, m), A.mult)
+                act(R("thr", 0, m), R("gt", 0, m), -103.0, 99.0)
+            if k >= 2:
+                u, v = HC[k - 2]
+                tt(R("hot", u, v), R(VB[(k - 2) % 4], 0, v - u), R("thr", u, v), A.is_ge)
+        for k in (len(HC) - 2, len(HC) - 1):
+            u, v = HC[k]
+            tt(R("hot", u, v), R(VB[k % 4], 0, v - u), R("thr", u, v), A.is_ge)
+        op("t", [R("bo"), R("hot", 0, m)], [R("ps1")], [lambda e: e.matmul(T.ps1[:, 0:m], T.bo[:, :], T.hot[:, 0:m], True, True)])
+        op("t", [R("ltm"), R("hot", 0, m)], [R("ps0")], [lambda e: e.matmul(T.ps0[:, 0:m], T.ltm[:, :], T.hot[:, 0:m], True, True)])
+        scan(R("cb", 1, m + 1), R("ps1", 0, m), R("msk", 1, 3 * m, 3), A.add, A.mult)
+        scan(R("cs", 0, nsb + 1), R("dm", 0, nsb + 1), R("cb", 16, m + 17, 16), A.add, A.min)
+        ts(R("m0"), R("krow"), R("cs", nsb, nsb + 1), A.is_ge)
+        f2p("ps2", 0, 16, "i", [("z16", "m0", 0)])
+        f2p("ps3", 0, 16, "i", [("z16", "m0", 0)], last=False)
+        f2p("ps4", 0, 32, "d", [("d256", "m0", 0)], last=False)
+        scan(R("cw1", 1, m + 1), R("dm", 0, m), R("cb", 1, m + 1), A.add, A.min)
+        tt(R("cw2", 0, m), R("ps0", 0, m), R("cb", 0, m), A.add)
+        cp(R("l1"), R("ps2", 0, 16))
+        gat2(R("m1"), R("cw1", 16, 224), R("l1"), R("krow"), A.is_le)
+        f2p("ps3", 0, 16, "i", [("zz", "m1", 0)], first=False)
+        f2p("ps4", 0, 32, "d", [("d16", "m1", 0)], first=False, last=False)
+        ts(R("inv", 32, 64), R("kj"), R("cb", m, m + 1), A.is_ge)
+        ts(R("nj", 32, 64), R("me", 0, 32), float(base), A.add)
+        tt(R("aj"), R("inv", 32, 64), R("me", 0, 32), A.mult)
+        cp(R("l2"), R("ps3", 0, 16))
+        gat2(R("m2"), R("cw2"), R("l2"), R("krow"), A.is_le)
+        f2p("ps4", 0, 32, "d", [("d1", "m2", 0)], first=False)
+        ts(R("inv", 32, 64), R("inv", 32, 64), 4096.0, A.mult)
+        tt(R("tq"), R("ps4", 0, 32), R("aj"), A.add)
+        ts(R("td"), R("tq"), float(S0), A.add)
+        gat("v", R("g1"), WIN, R("td"))
+        f2p("ps5", 0, 32, "i", [(("zE", "zB"), "g1", 0)])
+        ts(R("tu"), R("ps5", 0, 32), float(S0), A.add)
+        nc, zn = R("nc%d" % t), "zN%d" % t
         gat("s", R("gq"), WIN, R("tu"))
-        f2p("ps6", 0, "zr", "gq", 0, 32)
+        gat("s", R("eg"), R("ew", 0, GC), R("tu"))
+        sca(R("nb"), R("tu"), nc)
+        f2p("ps6", 0, 32, "i", [("zT16", "gq", 0)])
+        f2p("ps6", 32, 32, "i", [("zR16", "gq", 0)])
+        f2p("ps0", 0, m, "c", [(zn, "nb", S0)])
+        cp(R("nj", 0, 32), R("ps5", 0, 32))
+        tt(R("tq"), R("ps6", 0, 32), R("dj"), A.max)
+        ts(R("ru"), R("tq"), -float(RN0), A.add)
+        cp(R("xu"), R("ps6", 32, 64))
         if t == 0:
-            f2p("ps6", 32, "zi", "gq", 0, 32)
-        gat("v", R("gl", 0, 16 * h), R(ntb), R("lv", 0, h))
-        cp(R("rq"), R("ps6", 0, 32))
-        cp(R("yu"), R("rq"))
-        gat("s", R("gy"), WIN, R("yu"))
-        gat("s", R("gn"), R(ntb), R("yu"))
-        gat("s", R("eg"), R("ev", 0, 3600), R("tu"))
-        f2p("ps2", 0, "zr", "gy", 0, 32)
-        f2p("ps3", 0, "zz", "gn", 0, 32)
-        f2p("ps7", 0, "zh", "eg", 0, 32)
+            gat("s", R("gsn"), R("nb"), R("su"))
+        sca(R("rn"), R("ru"), nc)
+        f2p("ps1", 0, m, "c", [(("zB", "zR")[t], "nb", S0)])
+        f2p("ps5", 0, 32, "i", [("zh", "eg", 0)])
+        act(R("ns", 0, m), R("ps0", 0, m), -1.0, 1.0, F.Relu)
+        act(R("sp", 0, m), R("ps0", 0, m), 1.0, 0.0, F.Sign)
+        act(R("m8", 0, m), R("sp", 0, m), 8192.0)
+        act(R("e2"), R("eg"), 0.5, 127.8)
+        for k, z in enumerate(("zB", "zE", "zR")):
+            f2p("ps7", 32 * k, 32, "c", [(z, "gq", 0)])
+        M8 = (R("m8", 0, m),)
+
+        def blk(k):
+            return int(k) - RN0 + S0
         if t == 0:
-            gat("s", R("gsn"), R(ntb), R("snu"))
-            f2p("ps1", 0, "zz", "gsn", 0, 16)
-        tt(R("wq", 0, n), R("ps0", 0, n), R("rb", 0, n), A.mult)
-        gat("v", R("gl", 16 * h, NL), R(ntb), R("lv", h, n))
-        tt(PB, PB, R("wq", 0, n), A.max)
-        tt(R("nb", 0, n), R("no", 0, n), R("st", 0, n), A.add)
-        tt(PB, PB, R("m8", 0, n), A.subtract)
-        tt(R("nb", 0, n), R("nb", 0, n), R("sc", 0, n), A.subtract)
-        dump = 2800.0 if t == 0 else 3328.0
+            f2p("ps6", 64, 32, "i", [(zn, "gsn", 0)])
+        f2p("ps2", 0, m, "c", [(zn, "rn", blk(KL))])
+        f2p("ps3", 0, m, "c", [(zn, "rn", blk(KR))], M8)
+        f2p("ps4", 0, m, "c", [(zn, "rn", blk(KB))], M8)
+        for k in range(3):
+            act(R(px, w * k + m, w * k + w), R("ps7", 32 * k, 32 * k + 32))
 
         def detlists():
-            tt(R("di", 0, 32), R("ps7", 0, 32), R("tv"), A.add)
-            tt(R("di", 32, 64), R("ps7", 0, 32), R("me", nw0, nw0 + 32), A.add)
+            for k in range(2):
+                tt(R("di", 32 * k, 32 * k + 32), R("ps5", 0, 32), R("nj", 32 * k, 32 * k + 32), A.add)
             ts(R("da"), R("di"), 2047, A.bitwise_and)
-            ts(R("dq"), R("da"), -2048.0, A.add)
-            tt(R("dq", 32, 64), R("dq", 32, 64), R("fl"), A.mult)
-            ts(R("du"), R("dq"), 2048.0, A.add)
-            gat("s", R("dg"), R("dh"), R("du"))
+            tt(R("dq"), R("da"), R("inv"), A.add)
+            ts(R("du"), R("dq"), 2048.0, A.min)
+            gat("s", R("dg"), R("dl"), R("du", 0, 32))
 
-        def places():
-            if t == 0:
-                ts(R("scf"), R("ps6", 32, 64), -(W0 + dump), A.add)
-            else:
-                ts(R("scf"), R("tv"), -dump, A.add)
-            tt(R("scf"), R("scf"), R("ix", 0, 32), A.subtract)
-            tt(R("scf"), R("scf"), R("fl"), A.mult)
-            tt(R("scf"), R("scf"), R("ix", 0, 32), A.add)
-            ts(R("scu"), R("scf"), dump, A.add)
-            ts(R("e2"), R("eg"), 0.5, A.mult, -0.25, A.add)
-
-        def children(t=t):
-            tt(R("cl"), R("e2"), R("dg", 0, 512), A.add)
-            if t == 0:
-                sca(R("eu", W0, 3856), R("scu"), R("cl"))
-                tt(R("eu", W0 + P0, W0 + 3072), R("e2"), R("dg", 512, 1024), A.add)
-            else:
-                sca(R("ev"), R("scu"), R("cl"))
-                tt(R("cr"), R("e2"), R("dg", 512, 1024), A.add)
-                op("v", [R("cr")], [R("ev", 3072, GH)],
-                   [lambda e, i=i: e.tensor_copy(out=T.ev[:, 3072 + 32 * i:3104 + 32 * i], in_=T.cr[:, i::16]) for i in range(16)])
-        if t == 1:
+        def children():
+            sca2(R("ew", 0, GC), R("tu"), R("e2"), R("dg"))
+            gat2(R("ew", S0 + base, S0 + base + 512), R("dl"), R("du", 32, 64), R("e2"), A.add)
+        if t == 0:
+            cp(R("bt", 32, 48), R("lv", 0, 16))
+            cp(R("bt", 48, 64), R("rv", 0, 16))
+            tt(R("srf"), R("bt", 48, 80), R("xs"), A.is_equal)
+            tt(R("ab"), R("bt", 48, 64), R("bt", 32, 48), A.subtract)
+            tt(R("bt", 32, 48), R("bt", 32, 48), R("bt", 0, 16), A.subtract)
+            tt(R("ab"), R("ab"), R("srf", 0, 16), A.mult)
+            ts(R("sw", 0, 16), R("ps6", 64, 80), 1.0, A.min)
+            tt(R("ab"), R("ab"), R("bt", 32, 48), A.add)
+            tt(R("srf"), R("ps6", 64, 96), R("srf"), A.mult)
+            tt(R("ab"), R("ab"), R("sw", 0, 16), A.mult)
+            tt(R("sn"), R("sn"), R("srf"), A.max)
+            tt(R("bt", 0, 16), R("bt", 0, 16), R("ab"), A.add)
+            sendbases(1, "bt")
+            slots()
+            ts(R("su", 0, 16), R("sn", 0, 16), float(S0), A.add)
+            act(R("mme", 0, 16), R("sn", 0, 16), float(M))
+        else:
             detlists()
-            places()
-        gat("s", R("gr", 0, NL), R(ntb), R("rv", 0, n))
-        f2p("ps4", 0, "zz", "gl", 0, n)
-        f2p("ps5", 0, "zz", "gr", 0, n)
-        MN = R("me", nw0, nw0 + 32)
-
-        def newplaces(k, x):
-            o = R("px", 224 * k + nw0, 224 * k + nw0 + 32)
-            w = R("nw", 32 * k, 32 * k + 32)
-            tt(w, R(x), MN, A.subtract)
-            tt(w, w, R("fl"), A.mult)
-            tt(o, w, MN, A.add)
-        tt(R("rn"), R("ps2", 0, 32), R("tv"), A.is_equal)
-        tt(R("rn"), R("ps3", 0, 32), R("rn"), A.mult)
-        tt(R("rn"), R("rn"), R("rq"), A.max)
-        newplaces(2, "rn")
-        tt(R("wq", 0, n), R("ps4", 0, n), R("rl", 0, n), A.mult)
-        tt(PL, PL, R("wq", 0, n), A.max)
-        tt(R("wq", 0, n), PL, R("spl", 0, n), A.mult)
-        tt(PB, PB, R("wq", 0, n), A.max)
-        if t == 0:
-            table("b", 1)
-            tt(R("sw"), R("ps1", 0, 16), R("srf"), A.mult)
-            tt(R("sn"), R("sn"), R("sw"), A.max)
-            cp(R("snu"), R("sn"))
-            bases("gsb", "tc")
-        tt(PL, PL, R("m8", 0, n), A.subtract)
-        cp(R("pv", 0, 32, 2), R("tv", 1, 32, 2))
-        tt(PL, PL, R("no", 0, n), A.max)
-        cp(R("pv", 1, 32, 2), R("tv", 0, 32, 2))
-        newplaces(0, "pv")
-        if t == 0:
-            table("l", 1)
-            slots(1)
-        tt(PR, PR, R("m8", 0, n), A.subtract)
-        newplaces(1, "tv")
-        if t == 1:
+        gat2(R("gn"), R("nb"), R("xu"), R("gq"), A.mult)
+        f2p("ps7", 128, 32, "c", [("zG%d" % t, "gn", 0)])
+        NS, SP = R("ns", 0, m), R("sp", 0, m)
+        q0, q1, q2 = (R("pre", 192 * k, 192 * k + m) for k in range(3))
+        u0, u1, u2 = (R("wq", 192 * k, 192 * k + m) for k in range(3))
+        tt(q0, PL, NS, A.mult)
+        tt(q1, PR, NS, A.mult)
+        tt(q2, PB, NS, A.mult)
+        tt(u0, PL, SP, A.mult)
+        tt(q0, R("ps0", 0, m), q0, A.add)
+        tt(q1, R("ps1", 0, m), q1, A.add)
+        tt(q2, q2, u0, A.add)
+        tt(R("e1", 0, m), R("eq", 0, m), NS, A.mult)
+        tt(R("e3", 0, m), R("eq", 192, 192 + m), SP, A.max)
+        if t:
             children()
-            dma("y", None, R("ev", 0, GH), T.ye[:, :], T.ev[:, 0:GH])
-        tt(R("wq", 0, n), R("ps5", 0, n), R("rr", 0, n), A.mult)
-        tt(R("wq", 0, n), R("wq", 0, n), R("m8", 0, n), A.subtract)
-        tt(PR, PR, R("wq", 0, n), A.max)
-        tt(PR, PR, R("nb", 0, n), A.max)
-        if t == 0:
-            table("r", 1)
-            sendbases(1)
-            ts(R("bv"), R("px", 448, 640), float(GH - 1), A.min)
-            detlists()
-            places()
-            errors[0] = children
+            dma("y", None, R("ew", S0, GC), T.ye[:, :], T.ew[:, S0:GC])
 
-    for k, y in ((2, T.yb), (0, T.yl), (1, T.yr)):
-        for a, b, c in ((0, P0, 0), (P0, 3072, 160), (3072, GH, 192)):
-            src = R("px", 224 * k + c, 224 * k + c + (b - a) // 16)
-            dma("y", None, src, y[:, a:b], ap(src))
+        def done(x, k):
+            if t == 0:
+                halves(px, w * k, w * k + w, "hi", "lo", w * k)
+                for j, src in enumerate(("hi", "lo")):
+                    p2f("win", ROW[x] + j, S0, src, w * k, m)
+                    p2f("win", ROW[x] + j, S0 + n, src, w * k + m, 32)
+            else:
+                y = {"l": T.yl, "r": T.yr, "b": T.yb}[x]
+                for a, b, c in ((0, n, 0), (n, GH, m)):
+                    src = R(px, w * k + c, w * k + c + (b - a) // 16)
+                    dma("y", None, src, y[:, a:b], ap(src))
+        NL, NRm, NBm = R("ps2", 0, m), R("ps3", 0, m), R("ps4", 0, m)
+        tt(u0, NL, NS, A.mult)
+        tt(u1, NL, R("e1", 0, m), A.mult)
+        tt(u2, NL, R("e3", 0, m), A.mult)
+        tt(PL, q0, u0, A.max)
+        tt(q1, q1, u1, A.max)
+        tt(q2, q2, u2, A.max)
+        done("l", 0)
+        tt(PR, NRm, q1, A.max)
+        tt(u2, NRm, R("eq", 384, 384 + m), A.mult)
+        BN = R(px, 2 * w + m, 3 * w)
+        tt(BN, R("ps7", 128, 160), BN, A.max)
+        tt(q2, q2, u2, A.max)
+        done("r", 1)
+        tt(PB, NBm, q2, A.max)
+        done("b", 2)
+        if t == 0:
+            detlists()
+            arrived("be", 1, "bel1", 0, 8)
+            gat("v", R("win", GC, M), R("snf"), R("bel1"))
+            children()
+            gat("s", R("x0"), R("ew", 0, GC), R("su", 0, 16))
+            send("x0", 1, "x0", "ew", GC, 128)
+            d1, m1 = DA[1], 192
+            act(R("eo", 0, d1), R("ew", S0, S0 + d1))
+            cp(R("za", 2, 3 * (16 * m1 - d1), 3), R("ew", S0 + d1, S0 + 16 * m1))
     finish()

@@ -9,19 +9,20 @@ KB, KR, KL = 4352.0, 8192.0, 12032.0
 RN0 = 3840
 DA = (768, 896)
 CC = (3, 3)
+GB0, HL = 64, 16
 ZN = ["zz", "zB", "zR", "zL", "zE", "zB16", "zR16", "zL16", "zT16", "zMB", "zN0", "zN1", "zG0", "zG1", "zh", "z16", "d1", "d16", "d256"]
 _bf = {"win": M, "ew": M + 16, "w1": M + 16, "uw": M + 16, "za": 6912, "zb": 6912, "gl": 3328, "gr": 3328, "gb": 3072, "tr": 3072,
        "hb": 3072, "eo": 1024, "ta": 1024, "nb": M, "rn": 12048, "dr": 2048, "dh": 2064, "dl": 2064, "msk": 2304, "nc0": 512, "nc1": 512,
        "it": 2048, "z": 144 * len(ZN), "z0": 288, "bo": 128, "ltm": 128, "nid": 128, "snf": 416, "krow": 256, "dm": 192,
-       "hi": 576, "lo": 576, "shi": 16, "slo": 16, "mh": 416, "ml": 416, "gs": 512, "x0": 256, "x1": 256, "x2": 256, "xa": 256,
+       "hi": 576, "lo": 576, "shi": 16, "slo": 16, "mh": 416, "ml": 416, "gs": 512, "x0": 256, "x1": 256, "x2": 256, "xa": 256, "gi": 256,
        "hot": 192, "m0": 256, "m1": 256, "m2": 256, "g1": 512, "gq": 512, "eg": 512, "gn": 512, "gsn": 512, "e2": 512, "dg": 512,
        "ek": 576, "kh": 192, "tgh": 192, "tgl": 192, "m8": 192}
 _f32 = {"px0": 576, "px1": 672, "mc": 416, "me": 192, "me16": 192, "mme": 208, "lm": 208, "rm": 208, "dd": 416, "gt": 192, "thr": 192,
         "cb": 224, "cw1": 224, "cw2": 200, "cs": 16, "tg": 192, "eq": 576, "ns": 192, "sp": 192, "pre": 576, "e1": 192, "e3": 192,
-        "wq": 576, "ci": 16, "mk": 16, "mk2": 8, "zc": 24, "i16": 16, "cc": 192, "sn": 32, "xs": 32, "bt": 80, "srf": 32, "ab": 16,
+        "wq": 576, "ci": 16, "mk": 16, "mk2": 8, "zc": 24, "i16": 16, "cc": 192, "sn": 16, "xs": 32, "bt": 80, "srf": 32, "ab": 16,
         "sw": 32, "kj": 32, "jj": 32, "nj": 64, "dj": 32, "inv": 64, "aj": 32, "tf": 32, "tq": 32, "dq": 64}
 _i32 = {"xin": 480, "sin": 32, "wti": 2, "pid": 4, "di": 64, "da": 64}
-_u16 = {"lv": 208, "rv": 208, "bv": 192, "lw": 208, "rw": 208, "sa": 32, "su": 32, "bes": 16, "bel0": 16, "bel1": 16,
+_u16 = {"lv": 208, "rv": 208, "bv": 192, "lw": 208, "rw": 208, "sa": 32, "su": 16, "bes": 16, "bel0": 16, "bel1": 16,
         "l1": 16, "l2": 16, "td": 32, "tu": 32, "ru": 32, "xu": 32, "du": 64}
 SCRATCH, AL, _o = {}, {}, 0
 for _k in list(_f32):
@@ -254,129 +255,131 @@ def rank_program(g, core, T, topo):
     def load(q, out, src):
         dma(q, out, None, ap(out), src)
     load("y", R("xin", 320, 480), T.bs[:, :])
-    load("s", R("sin", 0, 16), T.snd[:, :])
-    load("y", R("xin", 0, 160), T.lt[:, :])
-    load("s", R("xin", 160, 320), T.rt[:, :])
+    load("s", R("xin", 0, 160), T.lt[:, :])
+    load("y", R("xin", 160, 320), T.rt[:, :])
     for s in range(2):
         load("s", R("sin", 16 + 8 * s, 24 + 8 * s), T.snd[:, 128 * s:128 * s + 128])
+    load("y", R("sin", 0, 16), T.snd[:, :])
     load("y", R("ew", S0, S0 + P0), T.err[:, :])
-    load("s", R("wti", 0, 1), T.wt[:, :])
-    load("s", R("wti", 1, 2), T.th[:, :])
-    load("s", R("eo", 0, DA[0]), T.err[:, 0:DA[0]])
 
     op("g", [], [R("pid", 0, 1)], [lambda e: e.iota(T.pid[:, 0:1], [[1, 1]], 0, 1)])
     fill(R("bo"), 1.0)
     iof("cc", 0, 192, [[1, 192]], 0)
-    fill(R("win"), 1.0)
-    op("g", [R("bo")], [R("nid")], [lambda e: e.affine_select(T.nid[:, :], T.bo[:, :], [[-1, 128]], A.is_equal, 0.0, 0, 1)])
+    fill(R("nid"), -1.0)
+    fill(R("win"), 0.25)
     op("g", [R("bo")], [R("bo")], [lambda e: e.affine_select(T.bo[:, :], T.bo[:, :], [[-16, 8], [0, 16]], A.is_ge, 0.0, 0, 1)])
     op("g", [R("bo")], [R("bo")], [lambda e: e.affine_select(T.bo[:, :], T.bo[:, :], [[16, 8], [0, 16]], A.is_ge, 0.0, 15, -1)])
-    op("g", [R("bo")], [R("ltm")], [lambda e: e.affine_select(T.ltm[:, :], T.bo[:, :], [[1, 128]], A.is_ge, 0.0, 0, -1)])
+    iof("gi", 0, 256, [[0, 2], [-7, 16], [15, 8]], 0)
     ts(R("pid", 1, 2), R("pid", 0, 1), 15, A.bitwise_and)
     fill(R("z0"), 0.0)
     ts(R("pid", 2, 3), R("pid", 1, 2), 1, A.logical_shift_right)
     cp(R("ci", 0, 1), R("pid", 1, 2))
     cp(R("ci", 1, 2), R("pid", 2, 3))
     I1, I2 = R("ci", 0, 1), R("ci", 1, 2)
-    for k, (f, b) in enumerate(((160.0, 0.0), (64.0, float(P0)), (192.0, 0.0), (8.0, float(GH))), 2):
-        ts(R("ci", k, k + 1), I1, f, A.mult, b, A.add)
-    MC = (R("mc", 0, 160), R("mc", 224, 416))
-    ts(R("mc", 0, 160), R("cc", 0, 160), R("ci", 2, 3), A.add)
-    ts(R("mc", 160, 224), R("cc", 0, 64), R("ci", 3, 4), A.add)
-    halves("mc", 0, 224, "mh", "ml", 0, "v")
+    fill(R("ew", 0, S0), 0.0)
+    ts(R("mk"), R("cc", 0, 16), I1, A.is_equal)
+    ts(R("mk2"), R("cc", 0, 8), I2, A.is_equal)
+    cp(R("z0", 15, 143, 16), R("bo", 0, 128, 16))
+    ts(R("ci", 6, 7), R("mk", 15, 16), 4.0 * S0, A.mult)
     W0 = 192
     ROW = {"l": 4, "r": 2, "b": 0}
     for x, c, o in (("b", 320, 2), ("l", 0, 0), ("r", 160, 1)):
-        cp(R("px0", W0 * o, W0 * o + 160), R("xin", c, c + 160))
-        halves("px0", W0 * o, W0 * o + 160, "hi", "lo", W0 * o)
+        halves("xin", c, c + 160, "hi", "lo", W0 * o, "v")
         for k, src in enumerate(("hi", "lo")):
             p2f("win", ROW[x] + k, S0, src, W0 * o, 160)
-        if x == "b":
-            ts(R("sa"), R("sin"), float(S0), A.add)
-    for k, src in enumerate(("mh", "ml")):
-        p2f("win", 6 + k, S0, src, 0, 160)
-        for row in (0, 2, 4, 6):
-            p2f("win", row + k, S0 + P0, src, 160, 64)
-    ts(R("mk2"), R("cc", 0, 8), I2, A.is_equal)
-    ts(R("mk"), R("cc", 0, 16), I1, A.is_equal)
-    cp(R("z0", 15, 143, 16), R("bo", 0, 128, 16))
-    cp(R("z0", 159, 287, 16), R("bo", 0, 128, 16))
-    cp(R("z0", 160, 288, 16), R("bo", 0, 128, 16))
-    ts(R("ci", 6, 7), R("mk", 15, 16), float(S0), A.mult)
+    ts(R("sa"), R("sin"), float(S0), A.add)
+    cp(R("su"), R("sa", 16, 32))
+    gat("s", R("x0"), R("ew", 0, S0 + P0), R("su"))
+    send("x0", 0, "x0", "ew", GC, 128)
     ts(R("zc", 0, 5), R("mk2", 0, 5), R("ci", 6, 7), A.add)
     Z1, Z2 = R("z0", 0, 144), R("z0", 144, 288)
 
-    def zmat(z, col, f=None, src=Z1):
-        if f is None:
-            ts(ZR(z), src, col, A.mult)
+    def zmat(z, col, src=Z1, q="s"):
+        if q == "s":
+            act(ZR(z), src, col)
         else:
-            ts(ZR(z), src, col, A.mult, f, A.mult)
-    for z, k in (("zB16", 0), ("zR16", 1), ("zL16", 2), ("zT16", 4)):
-        zmat(z, R("zc", k, k + 1))
-    for z, k in (("zE", 3), ("zB", 0), ("zR", 1), ("zL", 2)):
-        zmat(z, R("mk2", k, k + 1))
-    zmat("zMB", R("mk2", 0, 1), float(M))
+            ts(ZR(z), src, col, A.mult)
+    for z, k in (("zB16", 0), ("zL16", 2), ("zR16", 1)):
+        zmat(z, R("zc", k, k + 1), Z1, "v")
     ts(R("ci", 7, 8), R("mk", 0, 1), 3840.0, A.mult)
+    cp(R("sn"), R("sin", 16, 32))
     ts(R("snf"), R("win", M - 416, M), 0.0, A.mult, R("ci", 7, 8), A.add)
-    cp(R("sn", 16, 32), R("sin", 16, 32))
-    cp(R("su", 16, 32), R("sa", 16, 32))
 
     def slots():
-        halves("sn", 16, 32, "shi", "slo", 0, "v")
+        halves("sn", 0, 16, "shi", "slo", 0, "v")
         for k, src in enumerate(("shi", "slo")):
             for s in range(2):
                 p2f("snf", k, 16 + 144 * s, src, 8 * s, 8)
     slots()
-    load("y", R("dr"), T.det[:, :])
+    load("y", R("wti", 0, 1), T.wt[:, :])
+    load("y", R("wti", 1, 2), T.th[:, :])
+    load("y", R("eo", 0, DA[0]), T.err[:, 0:DA[0]])
     ts(R("me"), R("cc"), 16.0, A.mult, I1, A.add)
-    ts(R("me16"), R("me"), float(S0), A.add)
+    tt(R("zc", 8, 9), R("mk", 14, 15), R("mk", 15, 16), A.subtract)
     ts(R("mme", 16, 208), R("me"), float(M), A.mult)
-    for w in ("ew", "w1", "uw"):
-        fill(R(w, 0, S0), 0.0)
-        fill(R(w, S0 + P0, GC), 0.0)
-        fill(R(w, M, M + 16), 0.0)
+    ts(R("zc", 8, 9), R("mk2", 0, 1), float(M), A.mult, R("zc", 8, 9), A.add)
+    ts(R("mme", 0, 16), R("sn"), float(M), A.mult)
+    ts(R("gi"), R("gi"), R("mk", 14, 15), A.mult)
+    zmat("zMB", R("zc", 8, 9), Z1, "v")
+    for k, (f, b) in enumerate(((160.0, 0.0), (64.0, float(P0)), (192.0, 0.0), (8.0, float(GH))), 2):
+        ts(R("ci", k, k + 1), I1, f, A.mult, b, A.add)
+    cp(R("z0", 159, 287, 16), R("bo", 0, 128, 16))
+    cp(R("z0", 160, 288, 16), R("bo", 0, 128, 16))
+    ts(R("zc", 5, 7), R("mk2", 5, 7), 1.0 / KR, A.mult)
+    act(R("me16"), R("me"), 1.0, float(S0))
     fill(R("msk"), 1.0)
     fill(R("msk", 0, 2304, 3), 0.0)
-    iof("krow", 0, 256, [[1, 256]], 0)
-    iof("tg", 0, 192, [[0, 12], [1, 16]], 0)
-    iof("xs", 16, 32, [[128, 2], [1, 8]], S0)
-    iof("it", 0, 512, [[32, 16], [0, 32]], P0)
-    iof("it", 512, 1024, [[0, 16], [1, 32]], 0)
-    iof("it", 1024, 1536, [[0, 16], [2, 16], [-1, 2]], 1)
 
-    def later():
-        for z, k in (("zN0", 5), ("zN1", 6)):
+    def early():
+        for z, k in (("zL", 2), ("zR", 1), ("zB", 0), ("zE", 3), ("zN0", 5), ("zN1", 6)):
             zmat(z, R("mk2", k, k + 1))
-        for z, k in (("zG0", 5), ("zG1", 6)):
-            zmat(z, R("mk2", k, k + 1), 1.0 / KR)
-        cp(R("ci", 8, 10), R("wti"))
+        for z, k in (("zT16", 4), ("zG0", 5), ("zG1", 6)):
+            zmat(z, R("zc", k, k + 1))
         zmat("zz", 1.0)
         zmat("z16", 16.0)
-        zmat("zh", R("ci", 8, 9))
         for z, f in (("d1", 1.0), ("d16", 16.0), ("d256", 256.0)):
-            zmat(z, f, None, Z2)
+            zmat(z, f, Z2)
+        for o, c in enumerate((0, 160, 320)):
+            cp(R("px0", W0 * o, W0 * o + 160), R("xin", c, c + 160))
+        fill(R("ew", S0 + P0, GC), 0.0)
+        for w in ("ew", "w1", "uw"):
+            fill(R(w, M, M + 16), 0.0)
+        for w in ("w1", "uw"):
+            fill(R(w, 0, S0), 0.0)
+        ts(R("mc", 0, 160), R("cc", 0, 160), R("ci", 2, 3), A.add)
+        ts(R("mc", 160, 224), R("cc", 0, 64), R("ci", 3, 4), A.add)
+        ts(R("mc", 224, 416), R("cc"), R("ci", 4, 5), A.add)
+        cp(R("ci", 8, 10), R("wti"))
+        halves("mc", 0, 416, "mh", "ml", 0, "v")
         ts(R("ci", 10, 11), R("ci", 9, 10), -1.0, A.mult, 0.5, A.add)
-        ts(R("nid"), R("nid"), -1.0, A.mult)
+        zmat("zh", R("ci", 8, 9))
+        op("g", [R("nid")], [R("nid")], [lambda e: e.affine_select(T.nid[:, :], T.nid[:, :], [[-1, 128]], A.is_equal, 0.0, 0, 1)])
+        op("g", [R("bo")], [R("ltm")], [lambda e: e.affine_select(T.ltm[:, :], T.bo[:, :], [[1, 128]], A.is_ge, 0.0, 0, -1)])
+        for w in ("w1", "uw"):
+            zero(w, S0 + P0, GC)
+        iof("krow", 0, 256, [[1, 256]], 0)
+        iof("tg", 0, 192, [[0, 12], [1, 16]], 0)
+        iof("xs", 16, 32, [[128, 2], [1, 8]], S0)
+
+    def later():
         ts(R("dm"), R("tg"), I1, A.is_le, BIG, A.mult)
         for w in ("cb", "cw1", "cw2"):
-            fill(R(w), BIG)
-        fill(R("cb", 0, 1), 0.0)
-        ts(R("xs", 0, 16), R("me", 0, 16), float(GC), A.add)
-        ts(R("xs", 16, 32), R("xs", 16, 32), R("ci", 5, 6), A.add)
-        ts(R("kj"), R("cc", 0, 32), 8.0, A.mult, I2, A.add)
-        ts(R("dj"), R("me", 0, 32), float(M), A.add)
-        ts(R("mc", 224, 416), R("cc"), R("ci", 4, 5), A.add)
-        halves("mc", 224, 416, "mh", "ml", 224, "v")
-        fill(R("inv"), 0.0)
-        ts(R("dh", 0, 2048), R("dr"), 0.5, A.mult, 127.8, A.add)
-        fill(R("dl", 2048, 2064), -128.0)
-        act(R("dl", 0, 2048), R("dh", 0, 2048), 1.0, -256.0)
+            act(R(w), R("mc", 0, SCRATCH[w][1][1]), 0.0, BIG)
+        act(R("cb", 0, 1), R("cc", 0, 1), 0.0)
+        act(R("xs", 0, 16), R("me", 0, 16), 1.0, float(GC))
+        act(R("xs", 16, 32), R("xs", 16, 32), 1.0, R("ci", 5, 6), F.Identity)
+        act(R("kj"), R("cc", 0, 32), 8.0, I2, F.Identity)
+        act(R("dj"), R("me", 0, 32), 1.0, float(M))
+        act(R("inv"), R("cc", 0, 64), 0.0)
+        act(R("dl", 2048, 2064), R("cc", 0, 16), 0.0, -128.0)
 
     def newrows(t):
         zero("nc%d" % t, 0, 512)
         hi = 1536 * t
-        if t:
-            iof("it", hi, hi + 512, [[32, 16], [0, 32]], P0 + 512)
+        iof("it", hi, hi + 512, [[32, 16], [0, 32]], P0 + 512 * t)
+        if t == 0:
+            iof("it", 512, 1024, [[0, 16], [1, 32]], 0)
+            iof("it", 1024, 1536, [[0, 16], [2, 16], [-1, 2]], 1)
         for row, c in ((10 + 2 * t, hi), (11 + 2 * t, 512), (2 * t, hi), (2 * t + 1, 1024)):
             out = R("nc%d" % t, 0, 512, 1, row)
             dma("y", out, R("it", c, c + 512), ap(out), T.it[0:8, c:c + 512])
@@ -402,29 +405,26 @@ def rank_program(g, core, T, topo):
         def col(buf, a, b):
             return R(buf, S0 + 16 * a, S0 + 16 * b)
         if t == 0:
-            gat("s", R("gs"), WIN, R("sa"))
+            gat("v", R("gs", 0, 256), WIN, R("sa", 0, 16))
+            gat("s", R("gs", 256, 512), WIN, R("su"))
             f2p("ps3", 0, 16, "c", [("zB16", "gs", 0)])
             f2p("ps2", 0, m, "i", [("zB16", "win", S0)])
             sendbases(0, "ps3")
             cp(R("bt", 0, 16), R("ps3", 0, 16))
-            f2p("ps4", 0, 16, "c", [("zE", "gs", 0)])
+            cp(sl("za", d // 16, m, 2), col("ew", d // 16, m))
             ts(R("bv", 0, m), R("ps2", 0, m), float(GC - 1), A.min)
-            ts(R("su", 0, 16), R("ps4", 0, 16), float(S0), A.add)
-            cp(R("sn", 0, 16), R("ps4", 0, 16))
-            gat("s", R("x0"), R("ew", 0, GC), R("su", 0, 16))
-            send("x0", 0, "x0", "ew", GC, 128)
-            act(R("mme", 0, 16), R("sn", 0, 16), float(M))
             for ps, z in (("ps0", "zL16"), ("ps1", "zR16")):
-                f2p(ps, 0, 16, "c", [(z, "gs", 0)])
+                f2p(ps, 0, 16, "i", [(z, "gs", 256)])
                 f2p(ps, 16, m, "i", [(z, "win", S0)])
-            f2p("ps4", 16, 16, "i", [("zR16", "gs", 256)])
-            hb2 = m // 2
+            for k, z in enumerate(("zL16", "zR16")):
+                f2p("ps3", 32 + 16 * k, 16, "c", [(z, "gs", 0)])
+            hb2 = GB0
             gat("s", R("gb", 16 * hb2, n), WIN, R("bv", hb2, m))
             tt(R("gt", 0, m), R("ps2", 0, m), R("me16", 0, m), A.is_gt)
             gat("v", R("gb", 0, 16 * hb2), WIN, R("bv", 0, hb2))
-            zero("nb", 0, M)
+            load("y", R("dr"), T.det[:, :])
         else:
-            gat("s", R("gs", 0, 256), WIN, R("su", 0, 16))
+            gat("s", R("gs", 0, 256), WIN, R("su"))
             for ps, z in (("ps0", "zL16"), ("ps1", "zR16")):
                 f2p(ps, 16, m, "i", [(z, "win", S0)])
                 f2p(ps, 0, 16, "i", [(z, "gs", 0)])
@@ -433,11 +433,12 @@ def rank_program(g, core, T, topo):
             cp(R(v, 0, 16 + m), R(ps, 0, 16 + m))
             tt(R(x, 0, 16 + m), R(ps, 0, 16 + m), R("mme", 0, 16 + m), A.subtract)
         if t == 0:
-            cp(R("bt", 64, 80), R("ps4", 16, 32))
-            for a, b in CH:
-                cp(sl("za", a, b, 2), col("ew", a, b))
+            early()
+            cp(R("bt", 32, 64), R("ps3", 32, 64))
+            cp(R("bt", 64, 80), R("rv", 0, 16))
+            zero("nb", 0, 1536)
             arrived("be", 0, "bel0", 0, 8)
-            gat("v", R("win", GC, M), R("snf"), R("bel0"))
+            gat2(R("win", GC, M), R("snf"), R("bel0"), R("gi"), A.add)
         VB = ("ps4", "ps5", "ps6", "ps7")
 
         def legs(k, x):
@@ -473,25 +474,26 @@ def rank_program(g, core, T, topo):
                 cp(col(dst, a, b), sl(out, a, b, 2))
                 side(3 + k)
 
+        def blk(k):
+            return int(k) - RN0 + S0
         arrived("x0", t, "ew", GC, 128)
+        gat2(R("xa"), EW, XL, R("x0"), A.max)
+        gat2(R("x1"), EW, XR, R("xa"), A.max)
+        send("x1", t, "x1", "w1", GC, 128)
         legs(len(PC) - 1, "l")
-
-        def side1(k):
-            if k == 0:
-                gat2(R("xa"), EW, XL, R("x0"), A.max)
-                gat2(R("x1"), EW, XR, R("xa"), A.max)
-                send("x1", t, "x1", "w1", GC, 128)
-                if t == 0:
-                    zero("rn", int(KL) - RN0 + S0, int(KL) - RN0 + S0 + 3072)
         legs(len(PC) - 1, "r")
-        three(EW, R("eo", 0, d), "za", "zb", "w1", side1)
+        if t == 0:
+            zero("nb", 1536, M)
+            for k, src in enumerate(("mh", "ml")):
+                p2f("win", 6 + k, S0, src, 0, 160)
+                for row in (0, 2, 4, 6):
+                    p2f("win", row + k, S0 + P0, src, 160, 64)
+        three(EW, R("eo", 0, d), "za", "zb", "w1", lambda k: None)
         if t:
             for k, z in enumerate(("zL", "zR", "zB")):
                 f2p("ps%d" % k, 0, m, "c", [(z, "win", S0)])
                 act(R(px, w * k, w * k + m), R("ps%d" % k, 0, m))
         mh, ml = R("mh", 224 * t, 224 * t + m), R("ml", 224 * t, 224 * t + m)
-        if t == 0:
-            later()
         g3 = [m * k // 3 // 2 * 2 for k in range(4)]
 
         def bases(k):
@@ -505,10 +507,9 @@ def rank_program(g, core, T, topo):
         gat2(R("x2"), W1, XR, R("xa"), A.max)
         send("x2", t, "x2", "uw", GC, 128)
         if t == 0:
-            for k in (KR, KB):
-                zero("rn", int(k) - RN0 + S0, int(k) - RN0 + S0 + 3072)
             newrows(0)
-            newrows(1)
+            for k in (KL, KR, KB):
+                zero("rn", blk(k), blk(k) + P0)
         c2 = [0, m // 8, 3 * m // 8, 11 * m // 16, m]
         c2 = [x // 2 * 2 for x in c2]
         for k, (a, b) in enumerate(zip(c2[:-1], c2[1:])):
@@ -518,33 +519,44 @@ def rank_program(g, core, T, topo):
         arrived("x2", t, "uw", GC, 128)
 
         def side3(k):
+            pl, pr, pb = (R("ps%d" % j, 0, m) for j in (4, 5, 6))
             if k == 1:
-                for j, kf in enumerate((KL, KR, KB)):
-                    ts(R("ek", 192 * j, 192 * j + m), R("ps%d" % (4 + j), 0, m), 0.0, A.is_equal, kf, A.mult)
+                ts(R("ek", 0, m), pr, 0.0, A.is_equal, KR, A.mult)
+                ts(pl, pl, 0.0, A.is_equal, KL, A.mult)
+                ts(pb, pb, 0.0, A.is_equal, KB, A.mult)
             if k == 2:
-                tt(R("kh", 0, m), R("ek", 0, m), R("ek", 192, 192 + m), A.max)
-                tt(R("eq", 0, m), PL, PR, A.is_equal)
-                tt(R("kh", 0, m), R("kh", 0, m), R("ek", 384, 384 + m), A.max)
-                tt(R("eq", 192, 192 + m), PL, PB, A.is_equal)
-                tt(R("tg", 0, m), R("kh", 0, m), PR, A.add)
-                tt(R("eq", 384, 384 + m), PR, PB, A.is_equal)
+                tt(R("kh", 0, m), pl, R("ek", 0, m), A.max)
+            if k == 3:
+                tt(pb, pb, R("kh", 0, m), A.max)
+            if k == 4:
+                tt(pb, pb, PR, A.add)
         three(UW, col("w1", 0, d // 16), "zb", "za", "w1", side3)
         bases(2)
+        act(R("tgh", 0, m), R("ps6", 0, m))
         act(R("eo", 0, d), col("w1", 0, d // 16))
         f2p("ps3", 0, m, "i", [("zB", "gb", 0)])
-        halves("tg", 0, m, "tgh", "tgl", 0)
-        for row, src, c in ((8, "tgh", 0), (9, "tgl", 0), (10 + 2 * t, "ek", 192), (11 + 2 * t, "ek", 192)):
-            p2f("win", row, S0, src, c, m)
-        HC = CH + [(0, d // 32), (d // 32, d // 16)]
+        e16 = d // 16 - HL
+        HC = CH + [(0, e16), (e16, d // 16)]
         for k, (a, b) in enumerate(HC):
             own = sl("za", a, b, 2) if k < len(CH) else R("eo", 16 * a, 16 * b)
-            gat2(R("hb", 16 * a, 16 * b), R("w1", 0, GC), R("bv", a, b), own, A.max)
-            act(R("hb", 16 * a, 16 * b), R("hb", 16 * a, 16 * b), 1.0, R("ci", 10, 11), F.Sign)
-            f2p(VB[k % 4], 0, b - a, "i", [("zz", "hb", 16 * a)])
+            hb = R("hb", 16 * a, 16 * b)
+            gat2(hb, R("w1", 0, GC), R("bv", a, b), own, A.max)
             if k == 0:
-                tt(R("wq", 0, m), R("ps3", 0, m), R("me", 0, m), A.is_equal)
-                tt(R("gt", 0, m), R("gt", 0, m), R("wq", 0, m), A.mult)
+                tt(R("tgl", 0, m), R("ps6", 0, m), R("tgh", 0, m), A.subtract)
+                for row, src in ((8, "tgh"), (9, "tgl"), (10 + 2 * t, "ek"), (11 + 2 * t, "ek")):
+                    p2f("win", row, S0, src, 0, m)
+                tt(R("ps3", 0, m), R("ps3", 0, m), R("me", 0, m), A.is_equal)
+            if k < len(HC) - 1:
+                act(hb, hb, 1.0, R("ci", 10, 11), F.Sign)
+            else:
+                ts(hb, hb, R("ci", 9, 10), A.is_ge, 2.0, A.mult)
+            f2p(VB[k % 4], 0, b - a, "i", [("zz", "hb", 16 * a)])
+            if k == 1:
+                tt(R("gt", 0, m), R("ps3", 0, m), R("gt", 0, m), A.mult)
                 act(R("thr", 0, m), R("gt", 0, m), -103.0, 99.0)
+                act(R("thr", e16, d // 16), R("gt", e16, d // 16), -87.0, 99.0)
+            if k == 2 and t == 0:
+                later()
             if k >= 2:
                 u, v = HC[k - 2]
                 tt(R("hot", u, v), R(VB[(k - 2) % 4], 0, v - u), R("thr", u, v), A.is_ge)
@@ -561,6 +573,10 @@ def rank_program(g, core, T, topo):
         f2p("ps4", 0, 32, "d", [("d256", "m0", 0)], last=False)
         scan(R("cw1", 1, m + 1), R("dm", 0, m), R("cb", 1, m + 1), A.add, A.min)
         tt(R("cw2", 0, m), R("ps0", 0, m), R("cb", 0, m), A.add)
+        if t == 0:
+            act(R("dh", 0, 2048), R("dr"), 0.5, 127.8)
+            act(R("dl", 0, 2048), R("dh", 0, 2048), 1.0, -256.0)
+        tt(R("eq", 0, m), PL, PR, A.is_equal)
         cp(R("l1"), R("ps2", 0, 16))
         gat2(R("m1"), R("cw1", 16, 224), R("l1"), R("krow"), A.is_le)
         f2p("ps3", 0, 16, "i", [("zz", "m1", 0)], first=False)
@@ -568,14 +584,23 @@ def rank_program(g, core, T, topo):
         ts(R("inv", 32, 64), R("kj"), R("cb", m, m + 1), A.is_ge)
         ts(R("nj", 32, 64), R("me", 0, 32), float(base), A.add)
         tt(R("aj"), R("inv", 32, 64), R("me", 0, 32), A.mult)
+        tt(R("eq", 192, 192 + m), PL, PB, A.is_equal)
         cp(R("l2"), R("ps3", 0, 16))
         gat2(R("m2"), R("cw2"), R("l2"), R("krow"), A.is_le)
         f2p("ps4", 0, 32, "d", [("d1", "m2", 0)], first=False)
         ts(R("inv", 32, 64), R("inv", 32, 64), 4096.0, A.mult)
+        if t == 0:
+            tt(R("srf"), R("bt", 48, 80), R("xs"), A.is_equal)
+            tt(R("ab"), R("bt", 48, 64), R("bt", 32, 48), A.subtract)
+            tt(R("bt", 32, 48), R("bt", 32, 48), R("bt", 0, 16), A.subtract)
         tt(R("tq"), R("ps4", 0, 32), R("aj"), A.add)
         ts(R("td"), R("tq"), float(S0), A.add)
         gat("v", R("g1"), WIN, R("td"))
         f2p("ps5", 0, 32, "i", [(("zE", "zB"), "g1", 0)])
+        tt(R("eq", 384, 384 + m), PR, PB, A.is_equal)
+        if t == 0:
+            tt(R("ab"), R("ab"), R("srf", 0, 16), A.mult)
+            tt(R("ab"), R("ab"), R("bt", 32, 48), A.add)
         ts(R("tu"), R("ps5", 0, 32), float(S0), A.add)
         nc, zn = R("nc%d" % t), "zN%d" % t
         gat("s", R("gq"), WIN, R("tu"))
@@ -589,31 +614,24 @@ def rank_program(g, core, T, topo):
         ts(R("ru"), R("tq"), -float(RN0), A.add)
         cp(R("xu"), R("ps6", 32, 64))
         if t == 0:
-            gat("s", R("gsn"), R("nb"), R("su"))
+            gat("s", R("gsn"), R("nb"), R("sa"))
         sca(R("rn"), R("ru"), nc)
-        f2p("ps1", 0, m, "c", [(("zB", "zR")[t], "nb", S0)])
-        f2p("ps5", 0, 32, "i", [("zh", "eg", 0)])
-        act(R("ns", 0, m), R("ps0", 0, m), -1.0, 1.0, F.Relu)
-        act(R("sp", 0, m), R("ps0", 0, m), 1.0, 0.0, F.Sign)
-        act(R("m8", 0, m), R("sp", 0, m), 8192.0)
+        NS, SP, E1 = R("ps6", 64, 64 + m), R("ps6", 256, 256 + m), R("ps5", 64, 64 + m)
+        N0 = R("ps0", 0, m)
+        act(NS, N0, -1.0, 1.0, F.Relu)
+        act(SP, N0, 1.0, 0.0, F.Sign)
+        act(R("m8", 0, m), SP, 8192.0)
         act(R("e2"), R("eg"), 0.5, 127.8)
-        for k, z in enumerate(("zB", "zE", "zR")):
-            f2p("ps7", 32 * k, 32, "c", [(z, "gq", 0)])
         M8 = (R("m8", 0, m),)
 
-        def blk(k):
-            return int(k) - RN0 + S0
-        if t == 0:
-            f2p("ps6", 64, 32, "i", [(zn, "gsn", 0)])
-        f2p("ps2", 0, m, "c", [(zn, "rn", blk(KL))])
-        f2p("ps3", 0, m, "c", [(zn, "rn", blk(KR))], M8)
-        f2p("ps4", 0, m, "c", [(zn, "rn", blk(KB))], M8)
-        for k in range(3):
+        def child(k):
+            f2p("ps7", 32 * k, 32, "c", [(("zB", "zE", "zR")[k], "gq", 0)])
             act(R(px, w * k + m, w * k + w), R("ps7", 32 * k, 32 * k + 32))
 
         def detlists():
+            f2p("ps7", 192, 32, "i", [("zh", "eg", 0)])
             for k in range(2):
-                tt(R("di", 32 * k, 32 * k + 32), R("ps5", 0, 32), R("nj", 32 * k, 32 * k + 32), A.add)
+                tt(R("di", 32 * k, 32 * k + 32), R("ps7", 192, 224), R("nj", 32 * k, 32 * k + 32), A.add)
             ts(R("da"), R("di"), 2047, A.bitwise_and)
             tt(R("dq"), R("da"), R("inv"), A.add)
             ts(R("du"), R("dq"), 2048.0, A.min)
@@ -623,38 +641,33 @@ def rank_program(g, core, T, topo):
             sca2(R("ew", 0, GC), R("tu"), R("e2"), R("dg"))
             gat2(R("ew", S0 + base, S0 + base + 512), R("dl"), R("du", 32, 64), R("e2"), A.add)
         if t == 0:
-            cp(R("bt", 32, 48), R("lv", 0, 16))
-            cp(R("bt", 48, 64), R("rv", 0, 16))
-            tt(R("srf"), R("bt", 48, 80), R("xs"), A.is_equal)
-            tt(R("ab"), R("bt", 48, 64), R("bt", 32, 48), A.subtract)
-            tt(R("bt", 32, 48), R("bt", 32, 48), R("bt", 0, 16), A.subtract)
-            tt(R("ab"), R("ab"), R("srf", 0, 16), A.mult)
-            ts(R("sw", 0, 16), R("ps6", 64, 80), 1.0, A.min)
-            tt(R("ab"), R("ab"), R("bt", 32, 48), A.add)
-            tt(R("srf"), R("ps6", 64, 96), R("srf"), A.mult)
+            f2p("ps7", 160, 16, "c", [(zn, "gsn", 0)])
+            f2p("ps7", 176, 16, "i", [(zn, "gsn", 256)])
+            ts(R("sw", 0, 16), R("ps7", 160, 176), 1.0, A.min)
+            tt(R("sw", 16, 32), R("ps7", 176, 192), R("srf", 16, 32), A.mult)
             tt(R("ab"), R("ab"), R("sw", 0, 16), A.mult)
-            tt(R("sn"), R("sn"), R("srf"), A.max)
+            tt(R("sn"), R("sn"), R("sw", 16, 32), A.max)
             tt(R("bt", 0, 16), R("bt", 0, 16), R("ab"), A.add)
             sendbases(1, "bt")
-            slots()
-            ts(R("su", 0, 16), R("sn", 0, 16), float(S0), A.add)
-            act(R("mme", 0, 16), R("sn", 0, 16), float(M))
+            newrows(1)
+            for k in (KL, KR, KB):
+                zero("rn", blk(k) + P0, blk(k) + P0 + 512)
         else:
             detlists()
+        f2p("ps2", 0, m, "c", [(zn, "rn", blk(KL))])
+        child(0)
+        f2p("ps1", 0, m, "c", [(("zB", "zR")[t], "nb", S0)])
+        child(1)
         gat2(R("gn"), R("nb"), R("xu"), R("gq"), A.mult)
+        f2p("ps3", 0, m, "c", [(zn, "rn", blk(KR))], M8)
+        child(2)
         f2p("ps7", 128, 32, "c", [("zG%d" % t, "gn", 0)])
-        NS, SP = R("ns", 0, m), R("sp", 0, m)
+        f2p("ps4", 0, m, "c", [(zn, "rn", blk(KB))], M8)
         q0, q1, q2 = (R("pre", 192 * k, 192 * k + m) for k in range(3))
-        u0, u1, u2 = (R("wq", 192 * k, 192 * k + m) for k in range(3))
-        tt(q0, PL, NS, A.mult)
-        tt(q1, PR, NS, A.mult)
-        tt(q2, PB, NS, A.mult)
-        tt(u0, PL, SP, A.mult)
-        tt(q0, R("ps0", 0, m), q0, A.add)
-        tt(q1, R("ps1", 0, m), q1, A.add)
-        tt(q2, q2, u0, A.add)
-        tt(R("e1", 0, m), R("eq", 0, m), NS, A.mult)
-        tt(R("e3", 0, m), R("eq", 192, 192 + m), SP, A.max)
+        tt(q1, NS, PR, A.mult)
+        tt(q2, NS, PB, A.mult)
+        tt(E1, NS, R("eq", 0, m), A.mult)
+        tt(SP, SP, R("eq", 192, 192 + m), A.max)
         if t:
             children()
             dma("y", None, R("ew", S0, GC), T.ye[:, :], T.ew[:, S0:GC])
@@ -671,27 +684,33 @@ def rank_program(g, core, T, topo):
                     src = R(px, w * k + c, w * k + c + (b - a) // 16)
                     dma("y", None, src, y[:, a:b], ap(src))
         NL, NRm, NBm = R("ps2", 0, m), R("ps3", 0, m), R("ps4", 0, m)
-        tt(u0, NL, NS, A.mult)
-        tt(u1, NL, R("e1", 0, m), A.mult)
-        tt(u2, NL, R("e3", 0, m), A.mult)
-        tt(PL, q0, u0, A.max)
-        tt(q1, q1, u1, A.max)
-        tt(q2, q2, u2, A.max)
+        tt(PL, NL, PL, A.max)
+        tt(q0, NS, PL, A.mult)
+        tt(E1, E1, PL, A.mult)
+        tt(SP, SP, PL, A.mult)
+        tt(PL, N0, q0, A.add)
+        tt(q1, E1, q1, A.max)
+        tt(q2, SP, q2, A.max)
         done("l", 0)
+        tt(q1, R("ps1", 0, m), q1, A.add)
+        if t == 0:
+            slots()
+            ts(R("su"), R("sn"), float(S0), A.add)
+            act(R("mme", 0, 16), R("sn"), float(M))
+        tt(E1, NRm, R("eq", 384, 384 + m), A.mult)
         tt(PR, NRm, q1, A.max)
-        tt(u2, NRm, R("eq", 384, 384 + m), A.mult)
+        tt(q2, E1, q2, A.max)
+        done("r", 1)
         BN = R(px, 2 * w + m, 3 * w)
         tt(BN, R("ps7", 128, 160), BN, A.max)
-        tt(q2, q2, u2, A.max)
-        done("r", 1)
         tt(PB, NBm, q2, A.max)
         done("b", 2)
         if t == 0:
             detlists()
             arrived("be", 1, "bel1", 0, 8)
-            gat("v", R("win", GC, M), R("snf"), R("bel1"))
+            gat2(R("win", GC, M), R("snf"), R("bel1"), R("gi"), A.add)
             children()
-            gat("s", R("x0"), R("ew", 0, GC), R("su", 0, 16))
+            gat("s", R("x0"), R("ew", 0, GC), R("su"))
             send("x0", 1, "x0", "ew", GC, 128)
             d1, m1 = DA[1], 192
             act(R("eo", 0, d1), R("ew", S0, S0 + d1))

@@ -9,18 +9,20 @@ KB, KR, KL = 4352.0, 8192.0, 12032.0
 RN0 = 3840
 DA = (768, 896)
 CC = (3, 3)
-GB0, HL = 64, 16
-ZN = ["zz", "zB", "zR", "zL", "zE", "zB16", "zR16", "zL16", "zT16", "zMB", "zN0", "zN1", "zG0", "zG1", "zh", "z16", "d1", "d16", "d256"]
+PCK = (2, 2)
+G3 = ((90, 160), (64, 128))
+HL = 24
+ZN = ["zz", "zB", "zR", "zL", "zE", "zB16", "zR16", "zL16", "zT16", "zMB", "zN0", "zN1", "zG0", "zG1", "zh", "q1", "q16", "d1", "d16", "d256"]
 _bf = {"win": M, "ew": M + 16, "w1": M + 16, "uw": M + 16, "za": 6912, "zb": 6912, "gl": 3328, "gr": 3328, "gb": 3072, "tr": 3072,
        "hb": 3072, "eo": 1024, "ta": 1024, "nb": M, "rn": 12048, "dr": 2048, "dh": 2064, "dl": 2064, "msk": 2304, "nc0": 512, "nc1": 512,
-       "it": 2048, "z": 144 * len(ZN), "z0": 288, "bo": 128, "ltm": 128, "nid": 128, "snf": 416, "krow": 256, "dm": 192,
+       "it": 3072, "z": 144 * len(ZN), "z0": 432, "bo": 128, "ltm": 128, "nid": 128, "snf": 416, "krow": 256, "dm": 256,
        "hi": 576, "lo": 576, "shi": 16, "slo": 16, "mh": 416, "ml": 416, "gs": 512, "x0": 256, "x1": 256, "x2": 256, "xa": 256, "gi": 256,
        "hot": 192, "m0": 256, "m1": 256, "m2": 256, "g1": 512, "gq": 512, "eg": 512, "gn": 512, "gsn": 512, "e2": 512, "dg": 512,
        "ek": 576, "kh": 192, "tgh": 192, "tgl": 192, "m8": 192}
 _f32 = {"px0": 576, "px1": 672, "mc": 416, "me": 192, "me16": 192, "mme": 208, "lm": 208, "rm": 208, "dd": 416, "gt": 192, "thr": 192,
-        "cb": 224, "cw1": 224, "cw2": 200, "cs": 16, "tg": 192, "eq": 576, "ns": 192, "sp": 192, "pre": 576, "e1": 192, "e3": 192,
+        "cb": 224, "cw1": 224, "cw2": 200, "cs": 16, "tg": 256, "eq": 576, "ns": 192, "sp": 192, "pre": 576, "e1": 192, "e3": 192,
         "wq": 576, "ci": 16, "mk": 16, "mk2": 8, "zc": 24, "i16": 16, "cc": 192, "sn": 16, "xs": 32, "bt": 80, "srf": 32, "ab": 16,
-        "sw": 32, "kj": 32, "jj": 32, "nj": 64, "dj": 32, "inv": 64, "aj": 32, "tf": 32, "tq": 32, "dq": 64}
+        "sw": 32, "kj": 32, "jj": 32, "nj": 64, "dj": 32, "inv": 64, "aj": 32, "pk": 64, "tq": 32, "dq": 64}
 _i32 = {"xin": 480, "sin": 32, "wti": 2, "pid": 4, "di": 64, "da": 64}
 _u16 = {"lv": 208, "rv": 208, "bv": 192, "lw": 208, "rw": 208, "sa": 32, "su": 16, "bes": 16, "bel0": 16, "bel1": 16,
         "l1": 16, "l2": 16, "td": 32, "tu": 32, "ru": 32, "xu": 32, "du": 64}
@@ -184,8 +186,9 @@ def rank_program(g, core, T, topo):
     def sca2(win, off, a, b):
         op("v", [a, b, off], [win], [lambda e: e.tensor_tensor(out=ap(win).indirect(ap(off)), in0=ap(a), in1=ap(b), op=A.add)])
 
-    def iof(n, a, b, pat, base):
-        op("g", [], [R(n, a, b)], [lambda e: e.iota(T[n][:, a:b], pat, base, 0, allow_small_or_imprecise_dtypes=True)])
+    def iof(n, a, b, pat, base, step=1):
+        r = R(n, a, b, step)
+        op("g", [], [r], [lambda e: e.iota(ap(r), pat, base, 0, allow_small_or_imprecise_dtypes=True)])
 
     def zero(n, a, b):
         iof(n, a, b, [[0, b - a]], 0)
@@ -196,7 +199,7 @@ def rank_program(g, core, T, topo):
     def f2p(ps, c0, n, mode, terms, minus=(), first=True, last=True):
         mm, rd = [], []
         for z, src, a0 in terms:
-            k = 8 if mode == "d" else 16
+            k = {"d": 8, "q": 4}.get(mode, 16)
             rd.append(R(src, a0, a0 + k * n))
             for i in range(k):
                 zi = z[i % 2] if isinstance(z, tuple) else z
@@ -270,6 +273,7 @@ def rank_program(g, core, T, topo):
     op("g", [R("bo")], [R("bo")], [lambda e: e.affine_select(T.bo[:, :], T.bo[:, :], [[-16, 8], [0, 16]], A.is_ge, 0.0, 0, 1)])
     op("g", [R("bo")], [R("bo")], [lambda e: e.affine_select(T.bo[:, :], T.bo[:, :], [[16, 8], [0, 16]], A.is_ge, 0.0, 15, -1)])
     iof("gi", 0, 256, [[0, 2], [-7, 16], [15, 8]], 0)
+    iof("xs", 16, 32, [[128, 2], [1, 8]], S0)
     ts(R("pid", 1, 2), R("pid", 0, 1), 15, A.bitwise_and)
     fill(R("z0"), 0.0)
     ts(R("pid", 2, 3), R("pid", 1, 2), 1, A.logical_shift_right)
@@ -281,6 +285,19 @@ def rank_program(g, core, T, topo):
     ts(R("mk2"), R("cc", 0, 8), I2, A.is_equal)
     cp(R("z0", 15, 143, 16), R("bo", 0, 128, 16))
     ts(R("ci", 6, 7), R("mk", 15, 16), 4.0 * S0, A.mult)
+    cp(R("z0", 159, 287, 16), R("bo", 0, 128, 16))
+    cp(R("z0", 160, 288, 16), R("bo", 0, 128, 16))
+    cp(R("z0", 303, 431, 4), R("bo", 0, 128, 4))
+    ts(R("zc", 0, 5), R("mk2", 0, 5), R("ci", 6, 7), A.add)
+    ts(R("zc", 5, 7), R("mk2", 5, 7), 1.0 / KR, A.mult)
+    for k, (f, b) in enumerate(((160.0, 0.0), (64.0, float(P0)), (192.0, 0.0), (8.0, float(GH))), 2):
+        ts(R("ci", k, k + 1), I1, f, A.mult, b, A.add)
+    Z1, Z2, Z4 = R("z0", 0, 144), R("z0", 144, 288), R("z0", 288, 432)
+
+    def zmat(z, col, src=Z1):
+        act(ZR(z), src, col)
+    for z, k in (("zB16", 0), ("zL16", 2), ("zR16", 1), ("zT16", 4), ("zG0", 5), ("zG1", 6)):
+        zmat(z, R("zc", k, k + 1))
     W0 = 192
     ROW = {"l": 4, "r": 2, "b": 0}
     for x, c, o in (("b", 320, 2), ("l", 0, 0), ("r", 160, 1)):
@@ -291,16 +308,8 @@ def rank_program(g, core, T, topo):
     cp(R("su"), R("sa", 16, 32))
     gat("s", R("x0"), R("ew", 0, S0 + P0), R("su"))
     send("x0", 0, "x0", "ew", GC, 128)
-    ts(R("zc", 0, 5), R("mk2", 0, 5), R("ci", 6, 7), A.add)
-    Z1, Z2 = R("z0", 0, 144), R("z0", 144, 288)
-
-    def zmat(z, col, src=Z1, q="s"):
-        if q == "s":
-            act(ZR(z), src, col)
-        else:
-            ts(ZR(z), src, col, A.mult)
-    for z, k in (("zB16", 0), ("zL16", 2), ("zR16", 1)):
-        zmat(z, R("zc", k, k + 1), Z1, "v")
+    for z, k in (("zL", 2), ("zR", 1), ("zB", 0), ("zE", 3), ("zN0", 5), ("zN1", 6)):
+        zmat(z, R("mk2", k, k + 1))
     ts(R("ci", 7, 8), R("mk", 0, 1), 3840.0, A.mult)
     cp(R("sn"), R("sin", 16, 32))
     ts(R("snf"), R("win", M - 416, M), 0.0, A.mult, R("ci", 7, 8), A.add)
@@ -320,69 +329,68 @@ def rank_program(g, core, T, topo):
     ts(R("zc", 8, 9), R("mk2", 0, 1), float(M), A.mult, R("zc", 8, 9), A.add)
     ts(R("mme", 0, 16), R("sn"), float(M), A.mult)
     ts(R("gi"), R("gi"), R("mk", 14, 15), A.mult)
-    zmat("zMB", R("zc", 8, 9), Z1, "v")
-    for k, (f, b) in enumerate(((160.0, 0.0), (64.0, float(P0)), (192.0, 0.0), (8.0, float(GH))), 2):
-        ts(R("ci", k, k + 1), I1, f, A.mult, b, A.add)
-    cp(R("z0", 159, 287, 16), R("bo", 0, 128, 16))
-    cp(R("z0", 160, 288, 16), R("bo", 0, 128, 16))
-    ts(R("zc", 5, 7), R("mk2", 5, 7), 1.0 / KR, A.mult)
+    zmat("zMB", R("zc", 8, 9))
     act(R("me16"), R("me"), 1.0, float(S0))
-    fill(R("msk"), 1.0)
-    fill(R("msk", 0, 2304, 3), 0.0)
+    ts(R("mc", 0, 160), R("cc", 0, 160), R("ci", 2, 3), A.add)
+    ts(R("mc", 160, 224), R("cc", 0, 64), R("ci", 3, 4), A.add)
+    ts(R("mc", 224, 416), R("cc"), R("ci", 4, 5), A.add)
 
-    def early():
-        for z, k in (("zL", 2), ("zR", 1), ("zB", 0), ("zE", 3), ("zN0", 5), ("zN1", 6)):
-            zmat(z, R("mk2", k, k + 1))
-        for z, k in (("zT16", 4), ("zG0", 5), ("zG1", 6)):
-            zmat(z, R("zc", k, k + 1))
-        zmat("zz", 1.0)
-        zmat("z16", 16.0)
-        for z, f in (("d1", 1.0), ("d16", 16.0), ("d256", 256.0)):
-            zmat(z, f, Z2)
-        for o, c in enumerate((0, 160, 320)):
-            cp(R("px0", W0 * o, W0 * o + 160), R("xin", c, c + 160))
-        fill(R("ew", S0 + P0, GC), 0.0)
-        for w in ("ew", "w1", "uw"):
-            fill(R(w, M, M + 16), 0.0)
-        for w in ("w1", "uw"):
-            fill(R(w, 0, S0), 0.0)
-        ts(R("mc", 0, 160), R("cc", 0, 160), R("ci", 2, 3), A.add)
-        ts(R("mc", 160, 224), R("cc", 0, 64), R("ci", 3, 4), A.add)
-        ts(R("mc", 224, 416), R("cc"), R("ci", 4, 5), A.add)
-        cp(R("ci", 8, 10), R("wti"))
-        halves("mc", 0, 416, "mh", "ml", 0, "v")
-        ts(R("ci", 10, 11), R("ci", 9, 10), -1.0, A.mult, 0.5, A.add)
-        zmat("zh", R("ci", 8, 9))
-        op("g", [R("nid")], [R("nid")], [lambda e: e.affine_select(T.nid[:, :], T.nid[:, :], [[-1, 128]], A.is_equal, 0.0, 0, 1)])
-        op("g", [R("bo")], [R("ltm")], [lambda e: e.affine_select(T.ltm[:, :], T.bo[:, :], [[1, 128]], A.is_ge, 0.0, 0, -1)])
-        for w in ("w1", "uw"):
-            zero(w, S0 + P0, GC)
-        iof("krow", 0, 256, [[1, 256]], 0)
-        iof("tg", 0, 192, [[0, 12], [1, 16]], 0)
-        iof("xs", 16, 32, [[128, 2], [1, 8]], S0)
+    def early(k):
+        if k == 0:
+            halves("mc", 0, 416, "mh", "ml", 0, "v")
+            iof("msk", 0, 2304, [[0, 768], [256, 3]], 0)
+            op("g", [R("nid")], [R("nid")], [lambda e: e.affine_select(T.nid[:, :], T.nid[:, :], [[-1, 128]], A.is_equal, 0.0, 0, 1)])
+            op("g", [R("bo")], [R("ltm")], [lambda e: e.affine_select(T.ltm[:, :], T.bo[:, :], [[1, 128]], A.is_ge, 0.0, 0, -1)])
+            iof("krow", 0, 256, [[1, 256]], 0)
+            iof("tg", 0, 256, [[0, 16], [1, 16]], 0)
+        if k == 1:
+            for w in ("ew", "w1", "uw"):
+                fill(R(w, S0 + P0, GC), 0.0)
+                fill(R(w, M, M + 16), 0.0)
+            for w in ("w1", "uw"):
+                fill(R(w, 0, S0), 0.0)
+        if k == 2:
+            for o, c in enumerate((0, 160, 320)):
+                cp(R("px0", W0 * o, W0 * o + 160), R("xin", c, c + 160))
+            cp(R("ci", 8, 10), R("wti"))
+            ts(R("ci", 10, 11), R("ci", 9, 10), -1.0, A.mult, 0.5, A.add)
 
-    def later():
-        ts(R("dm"), R("tg"), I1, A.is_le, BIG, A.mult)
-        for w in ("cb", "cw1", "cw2"):
-            act(R(w), R("mc", 0, SCRATCH[w][1][1]), 0.0, BIG)
-        act(R("cb", 0, 1), R("cc", 0, 1), 0.0)
-        act(R("xs", 0, 16), R("me", 0, 16), 1.0, float(GC))
-        act(R("xs", 16, 32), R("xs", 16, 32), 1.0, R("ci", 5, 6), F.Identity)
-        act(R("kj"), R("cc", 0, 32), 8.0, I2, F.Identity)
-        act(R("dj"), R("me", 0, 32), 1.0, float(M))
-        act(R("inv"), R("cc", 0, 64), 0.0)
-        act(R("dl", 2048, 2064), R("cc", 0, 16), 0.0, -128.0)
+    def later(k):
+        if k == 0:
+            zmat("zz", 1.0)
+            for z, f, src in (("q1", 1.0, Z4), ("q16", 16.0, Z4), ("d1", 1.0, Z2), ("d16", 16.0, Z2), ("d256", 256.0, Z2)):
+                zmat(z, f, src)
+            for w in ("cb", "cw1", "cw2"):
+                act(R(w), R("mc", 0, SCRATCH[w][1][1]), 0.0, BIG)
+            act(R("cb", 0, 1), R("cc", 0, 1), 0.0)
+            act(R("kj"), R("cc", 0, 32), 8.0, I2, F.Identity)
+            act(R("inv"), R("cc", 0, 64), 0.0)
+            act(R("xs", 0, 16), R("me", 0, 16), 1.0, float(GC))
+            act(R("xs", 16, 32), R("xs", 16, 32), 1.0, R("ci", 5, 6), F.Identity)
+            act(R("nj", 32, 64), R("me", 0, 32), 1.0, float(P0))
+        else:
+            zmat("zh", R("ci", 8, 9))
+            act(R("dj"), R("me", 0, 32), 1.0, float(M))
+            act(R("dl", 2048, 2064), R("cc", 0, 16), 0.0, -128.0)
+            act(R("dh", 0, 2048), R("dr"), 0.5, 127.8)
+            act(R("dl", 0, 2048), R("dh", 0, 2048), 1.0, -256.0)
 
     def newrows(t):
         zero("nc%d" % t, 0, 512)
-        hi = 1536 * t
-        iof("it", hi, hi + 512, [[32, 16], [0, 32]], P0 + 512 * t)
+        hi, b = 1024 + 1024 * t, P0 + 512 * t
+        iof("it", hi, hi + 512, [[32, 16], [0, 32]], b)
+        iof("it", hi + 512, hi + 1024, [[32, 16], [0, 16]], b, 2)
+        iof("it", hi + 513, hi + 1024, [[-32, 16], [0, 16]], -b, 2)
         if t == 0:
-            iof("it", 512, 1024, [[0, 16], [1, 32]], 0)
-            iof("it", 1024, 1536, [[0, 16], [2, 16], [-1, 2]], 1)
-        for row, c in ((10 + 2 * t, hi), (11 + 2 * t, 512), (2 * t, hi), (2 * t + 1, 1024)):
+            iof("it", 0, 512, [[0, 16], [1, 32]], 0)
+            iof("it", 512, 1024, [[0, 16], [2, 16]], 0, 2)
+            iof("it", 513, 1024, [[0, 16], [-2, 16]], -1, 2)
+        for row, c in ((10 + 2 * t, hi), (11 + 2 * t, 0), (2 * t, hi + 512), (2 * t + 1, 512)):
             out = R("nc%d" % t, 0, 512, 1, row)
             dma("y", out, R("it", c, c + 512), ap(out), T.it[0:8, c:c + 512])
+
+    def blk(k):
+        return int(k) - RN0 + S0
 
     WIN = R("win")
     for t in range(2):
@@ -393,7 +401,8 @@ def rank_program(g, core, T, topo):
         PL, PR, PB = R(px, 0, m), R(px, w, w + m), R(px, 2 * w, 2 * w + m)
         cut = [d // 16 + (m - d // 16) * k // CC[t] // 2 * 2 for k in range(CC[t] + 1)]
         CH = list(zip(cut[:-1], cut[1:]))
-        PC = [(0, 16 + d // 16)] + [(16 + a, 16 + b) for a, b in CH]
+        PC = [0] + [16 + x for x in (cut[0], cut[PCK[t]], m)]
+        PC = list(zip(PC[:-1], PC[1:]))
         EW, W1, UW = R("ew"), R("w1"), R("uw")
 
         def sl(buf, a, b, k):
@@ -405,40 +414,47 @@ def rank_program(g, core, T, topo):
         def col(buf, a, b):
             return R(buf, S0 + 16 * a, S0 + 16 * b)
         if t == 0:
-            gat("v", R("gs", 0, 256), WIN, R("sa", 0, 16))
+            gat("s", R("gs", 0, 256), WIN, R("sa", 0, 16))
             gat("s", R("gs", 256, 512), WIN, R("su"))
             f2p("ps3", 0, 16, "c", [("zB16", "gs", 0)])
-            f2p("ps2", 0, m, "i", [("zB16", "win", S0)])
+            cp(sl("za", d // 16, m, 2), col("ew", d // 16, m))
             sendbases(0, "ps3")
             cp(R("bt", 0, 16), R("ps3", 0, 16))
-            cp(sl("za", d // 16, m, 2), col("ew", d // 16, m))
-            ts(R("bv", 0, m), R("ps2", 0, m), float(GC - 1), A.min)
+            early(0)
             for ps, z in (("ps0", "zL16"), ("ps1", "zR16")):
-                f2p(ps, 0, 16, "i", [(z, "gs", 256)])
                 f2p(ps, 16, m, "i", [(z, "win", S0)])
+                f2p(ps, 0, 16, "i", [(z, "gs", 256)])
+            f2p("ps2", 0, m, "i", [("zB16", "win", S0)])
             for k, z in enumerate(("zL16", "zR16")):
                 f2p("ps3", 32 + 16 * k, 16, "c", [(z, "gs", 0)])
-            hb2 = GB0
-            gat("s", R("gb", 16 * hb2, n), WIN, R("bv", hb2, m))
-            tt(R("gt", 0, m), R("ps2", 0, m), R("me16", 0, m), A.is_gt)
-            gat("v", R("gb", 0, 16 * hb2), WIN, R("bv", 0, hb2))
+            later(0)
             load("y", R("dr"), T.det[:, :])
         else:
-            gat("s", R("gs", 0, 256), WIN, R("su"))
             for ps, z in (("ps0", "zL16"), ("ps1", "zR16")):
                 f2p(ps, 16, m, "i", [(z, "win", S0)])
                 f2p(ps, 0, 16, "i", [(z, "gs", 0)])
             f2p("ps2", 0, m, "i", [("zB16", "win", S0)])
+            gat("s", R("x0"), R("ew", 0, GC), R("su"))
+            send("x0", 1, "x0", "ew", GC, 128)
+            newrows(1)
+            for k in (KL, KR, KB):
+                zero("rn", blk(k) + P0, blk(k) + P0 + 512)
+            act(R("eo", 0, d), col("ew", 0, d // 16))
+
+        def ghosts():
+            arrived("be", t, "bel%d" % t, 0, 8)
+            gat2(R("win", GC, M), R("snf"), R("bel%d" % t), R("gi"), A.add)
         for ps, v, x in (("ps0", "lv", "lm"), ("ps1", "rv", "rm")):
             cp(R(v, 0, 16 + m), R(ps, 0, 16 + m))
             tt(R(x, 0, 16 + m), R(ps, 0, 16 + m), R("mme", 0, 16 + m), A.subtract)
+            if t == 0:
+                early(1 + (x == "rm"))
+            elif x == "lm":
+                ghosts()
+                cp(sl("za", d // 16, m, 2), col("ew", d // 16, m))
         if t == 0:
-            early()
-            cp(R("bt", 32, 64), R("ps3", 32, 64))
-            cp(R("bt", 64, 80), R("rv", 0, 16))
-            zero("nb", 0, 1536)
-            arrived("be", 0, "bel0", 0, 8)
-            gat2(R("win", GC, M), R("snf"), R("bel0"), R("gi"), A.add)
+            zero("nb", 0, 1024)
+            ghosts()
         VB = ("ps4", "ps5", "ps6", "ps7")
 
         def legs(k, x):
@@ -451,7 +467,7 @@ def rank_program(g, core, T, topo):
         for k, (a, b) in enumerate(PC):
             gat("v", R("gl", 16 * a, 16 * b), WIN, R("lv", a, b))
             gat("s", R("gr", 16 * a, 16 * b), WIN, R("rv", a, b))
-            if k == 0 and t:
+            if k == 0:
                 ts(R("bv", 0, m), R("ps2", 0, m), float(GC - 1), A.min)
                 tt(R("gt", 0, m), R("ps2", 0, m), R("me16", 0, m), A.is_gt)
             if k:
@@ -470,12 +486,10 @@ def rank_program(g, core, T, topo):
             side(2)
             for k, (a, b) in enumerate(CH):
                 u, v = 3 * (16 * a - d), 3 * (16 * b - d)
-                scan(R(out, u, v), R("msk", 0, v - u), R(slots_, u, v), A.mult, A.max)
+                scan(R(out, u, v), R("msk", 0, v - u), R(slots_, u, v), A.min, A.max)
                 cp(col(dst, a, b), sl(out, a, b, 2))
                 side(3 + k)
 
-        def blk(k):
-            return int(k) - RN0 + S0
         arrived("x0", t, "ew", GC, 128)
         gat2(R("xa"), EW, XL, R("x0"), A.max)
         gat2(R("x1"), EW, XR, R("xa"), A.max)
@@ -483,21 +497,17 @@ def rank_program(g, core, T, topo):
         legs(len(PC) - 1, "l")
         legs(len(PC) - 1, "r")
         if t == 0:
-            zero("nb", 1536, M)
-            for k, src in enumerate(("mh", "ml")):
-                p2f("win", 6 + k, S0, src, 0, 160)
-                for row in (0, 2, 4, 6):
-                    p2f("win", row + k, S0 + P0, src, 160, 64)
+            zero("nb", 1024, M)
         three(EW, R("eo", 0, d), "za", "zb", "w1", lambda k: None)
         if t:
             for k, z in enumerate(("zL", "zR", "zB")):
                 f2p("ps%d" % k, 0, m, "c", [(z, "win", S0)])
                 act(R(px, w * k, w * k + m), R("ps%d" % k, 0, m))
         mh, ml = R("mh", 224 * t, 224 * t + m), R("ml", 224 * t, 224 * t + m)
-        g3 = [m * k // 3 // 2 * 2 for k in range(4)]
+        g3 = (0,) + G3[t] + (m,)
 
         def bases(k):
-            if t:
+            if g3[k] < g3[k + 1]:
                 gat("s", R("gb", 16 * g3[k], 16 * g3[k + 1]), WIN, R("bv", g3[k], g3[k + 1]))
         bases(0)
         for k, z in enumerate(("zL", "zR", "zB")):
@@ -516,20 +526,33 @@ def rank_program(g, core, T, topo):
             gat("s", R("tr", 16 * a, 16 * b), W1, L("rw", a, b))
             gat2(col("uw", a, b), W1, L("lw", a, b), R("tr", 16 * a, 16 * b), A.max)
         bases(1)
+        pl, pr, pb = (R("ps%d" % j, 0, m) for j in (4, 5, 6))
+        ts(R("ek", 0, m), pr, 0.0, A.is_equal, KR, A.mult)
+        ts(pl, pl, 0.0, A.is_equal, KL, A.mult)
+        ts(pb, pb, 0.0, A.is_equal, KB, A.mult)
+        tt(R("kh", 0, m), pl, R("ek", 0, m), A.max)
+        if t == 0:
+            for k, src in enumerate(("mh", "ml")):
+                p2f("win", 6 + k, S0, src, 0, 160)
+                for row in (0, 2, 4, 6):
+                    p2f("win", row + k, S0 + P0, src, 160, 64)
+            ts(R("dm"), R("tg"), I1, A.is_le, BIG, A.mult)
+            cp(R("bt", 32, 64), R("ps3", 32, 64))
+            cp(R("bt", 64, 80), R("rv", 0, 16))
+        tt(pb, pb, R("kh", 0, m), A.max)
         arrived("x2", t, "uw", GC, 128)
 
         def side3(k):
-            pl, pr, pb = (R("ps%d" % j, 0, m) for j in (4, 5, 6))
             if k == 1:
-                ts(R("ek", 0, m), pr, 0.0, A.is_equal, KR, A.mult)
-                ts(pl, pl, 0.0, A.is_equal, KL, A.mult)
-                ts(pb, pb, 0.0, A.is_equal, KB, A.mult)
-            if k == 2:
-                tt(R("kh", 0, m), pl, R("ek", 0, m), A.max)
-            if k == 3:
-                tt(pb, pb, R("kh", 0, m), A.max)
-            if k == 4:
                 tt(pb, pb, PR, A.add)
+            if t == 0 and k == 1:
+                tt(R("srf"), R("bt", 48, 80), R("xs"), A.is_equal)
+                tt(R("ab"), R("bt", 48, 64), R("bt", 32, 48), A.subtract)
+                tt(R("bt", 32, 48), R("bt", 32, 48), R("bt", 0, 16), A.subtract)
+            if t == 0 and k == 2:
+                tt(R("ab"), R("ab"), R("srf", 0, 16), A.mult)
+            if t == 0 and k == 3:
+                tt(R("ab"), R("ab"), R("bt", 32, 48), A.add)
         three(UW, col("w1", 0, d // 16), "zb", "za", "w1", side3)
         bases(2)
         act(R("tgh", 0, m), R("ps6", 0, m))
@@ -555,8 +578,6 @@ def rank_program(g, core, T, topo):
                 tt(R("gt", 0, m), R("ps3", 0, m), R("gt", 0, m), A.mult)
                 act(R("thr", 0, m), R("gt", 0, m), -103.0, 99.0)
                 act(R("thr", e16, d // 16), R("gt", e16, d // 16), -87.0, 99.0)
-            if k == 2 and t == 0:
-                later()
             if k >= 2:
                 u, v = HC[k - 2]
                 tt(R("hot", u, v), R(VB[(k - 2) % 4], 0, v - u), R("thr", u, v), A.is_ge)
@@ -565,42 +586,39 @@ def rank_program(g, core, T, topo):
             tt(R("hot", u, v), R(VB[k % 4], 0, v - u), R("thr", u, v), A.is_ge)
         op("t", [R("bo"), R("hot", 0, m)], [R("ps1")], [lambda e: e.matmul(T.ps1[:, 0:m], T.bo[:, :], T.hot[:, 0:m], True, True)])
         op("t", [R("ltm"), R("hot", 0, m)], [R("ps0")], [lambda e: e.matmul(T.ps0[:, 0:m], T.ltm[:, :], T.hot[:, 0:m], True, True)])
-        scan(R("cb", 1, m + 1), R("ps1", 0, m), R("msk", 1, 3 * m, 3), A.add, A.mult)
+        scan(R("cb", 1, m + 1), R("ps1", 0, m), R("msk", 0, 3 * m, 3), A.add, A.max)
         scan(R("cs", 0, nsb + 1), R("dm", 0, nsb + 1), R("cb", 16, m + 17, 16), A.add, A.min)
         ts(R("m0"), R("krow"), R("cs", nsb, nsb + 1), A.is_ge)
-        f2p("ps2", 0, 16, "i", [("z16", "m0", 0)])
-        f2p("ps3", 0, 16, "i", [("z16", "m0", 0)], last=False)
+        f2p("ps2", 0, 64, "q", [("q16", "m0", 0)])
+        f2p("ps3", 0, 64, "q", [("q16", "m0", 0)], last=False)
         f2p("ps4", 0, 32, "d", [("d256", "m0", 0)], last=False)
         scan(R("cw1", 1, m + 1), R("dm", 0, m), R("cb", 1, m + 1), A.add, A.min)
-        tt(R("cw2", 0, m), R("ps0", 0, m), R("cb", 0, m), A.add)
+        act(R("pre", 192, 192 + m), PR, 1.0, -1.0)
         if t == 0:
-            act(R("dh", 0, 2048), R("dr"), 0.5, 127.8)
-            act(R("dl", 0, 2048), R("dh", 0, 2048), 1.0, -256.0)
-        tt(R("eq", 0, m), PL, PR, A.is_equal)
-        cp(R("l1"), R("ps2", 0, 16))
+            later(1)
+        else:
+            act(R("nj", 32, 64), R("me", 0, 32), 1.0, float(base))
+
+        def pick(lst, ps):
+            scan(R("pk"), R("dm", 0, 256, 4), R(ps, 0, 64), A.add, A.min)
+            cp(R(lst), R("pk", 3, 64, 4))
+        pick("l1", "ps2")
         gat2(R("m1"), R("cw1", 16, 224), R("l1"), R("krow"), A.is_le)
-        f2p("ps3", 0, 16, "i", [("zz", "m1", 0)], first=False)
+        f2p("ps3", 0, 64, "q", [("q1", "m1", 0)], first=False)
         f2p("ps4", 0, 32, "d", [("d16", "m1", 0)], first=False, last=False)
+        tt(R("cw2", 0, m), R("ps0", 0, m), R("cb", 0, m), A.add)
         ts(R("inv", 32, 64), R("kj"), R("cb", m, m + 1), A.is_ge)
-        ts(R("nj", 32, 64), R("me", 0, 32), float(base), A.add)
-        tt(R("aj"), R("inv", 32, 64), R("me", 0, 32), A.mult)
-        tt(R("eq", 192, 192 + m), PL, PB, A.is_equal)
-        cp(R("l2"), R("ps3", 0, 16))
+        pick("l2", "ps3")
         gat2(R("m2"), R("cw2"), R("l2"), R("krow"), A.is_le)
         f2p("ps4", 0, 32, "d", [("d1", "m2", 0)], first=False)
-        ts(R("inv", 32, 64), R("inv", 32, 64), 4096.0, A.mult)
-        if t == 0:
-            tt(R("srf"), R("bt", 48, 80), R("xs"), A.is_equal)
-            tt(R("ab"), R("bt", 48, 64), R("bt", 32, 48), A.subtract)
-            tt(R("bt", 32, 48), R("bt", 32, 48), R("bt", 0, 16), A.subtract)
+        tt(R("aj"), R("inv", 32, 64), R("me", 0, 32), A.mult)
+        act(R("inv", 32, 64), R("inv", 32, 64), 4096.0)
         tt(R("tq"), R("ps4", 0, 32), R("aj"), A.add)
         ts(R("td"), R("tq"), float(S0), A.add)
         gat("v", R("g1"), WIN, R("td"))
         f2p("ps5", 0, 32, "i", [(("zE", "zB"), "g1", 0)])
-        tt(R("eq", 384, 384 + m), PR, PB, A.is_equal)
-        if t == 0:
-            tt(R("ab"), R("ab"), R("srf", 0, 16), A.mult)
-            tt(R("ab"), R("ab"), R("bt", 32, 48), A.add)
+        tt(R("eq", 0, m), PL, PR, A.is_equal)
+        tt(R("eq", 192, 192 + m), PL, PB, A.is_equal)
         ts(R("tu"), R("ps5", 0, 32), float(S0), A.add)
         nc, zn = R("nc%d" % t), "zN%d" % t
         gat("s", R("gq"), WIN, R("tu"))
@@ -608,7 +626,8 @@ def rank_program(g, core, T, topo):
         sca(R("nb"), R("tu"), nc)
         f2p("ps6", 0, 32, "i", [("zT16", "gq", 0)])
         f2p("ps6", 32, 32, "i", [("zR16", "gq", 0)])
-        f2p("ps0", 0, m, "c", [(zn, "nb", S0)])
+        f2p("ps0", 0, m, "c", [(("zB", "zR")[t], "nb", S0)])
+        tt(R("eq", 384, 384 + m), PR, PB, A.is_equal)
         cp(R("nj", 0, 32), R("ps5", 0, 32))
         tt(R("tq"), R("ps6", 0, 32), R("dj"), A.max)
         ts(R("ru"), R("tq"), -float(RN0), A.add)
@@ -617,16 +636,20 @@ def rank_program(g, core, T, topo):
             gat("s", R("gsn"), R("nb"), R("sa"))
         sca(R("rn"), R("ru"), nc)
         NS, SP, E1 = R("ps6", 64, 64 + m), R("ps6", 256, 256 + m), R("ps5", 64, 64 + m)
-        N0 = R("ps0", 0, m)
+        N0, NP = R("ps1", 0, m), R("ps1", 256, 256 + m)
+        act(N0, R("ps0", 0, m), 1.0, 0.0, F.Abs)
         act(NS, N0, -1.0, 1.0, F.Relu)
         act(SP, N0, 1.0, 0.0, F.Sign)
+        act(NP, R("ps0", 0, m), 1.0, 1.0, F.Abs)
         act(R("m8", 0, m), SP, 8192.0)
         act(R("e2"), R("eg"), 0.5, 127.8)
         M8 = (R("m8", 0, m),)
 
         def child(k):
-            f2p("ps7", 32 * k, 32, "c", [(("zB", "zE", "zR")[k], "gq", 0)])
-            act(R(px, w * k + m, w * k + w), R("ps7", 32 * k, 32 * k + 32))
+            f2p(("ps7", "ps0")[k % 2], 32 * k, 32, "c", [(("zB", "zE", "zR")[k], "gq", 0)])
+
+        def childto(k):
+            act(R(px, w * k + m, w * k + w), R(("ps7", "ps0")[k % 2], 32 * k, 32 * k + 32))
 
         def detlists():
             f2p("ps7", 192, 32, "i", [("zh", "eg", 0)])
@@ -639,8 +662,12 @@ def rank_program(g, core, T, topo):
 
         def children():
             sca2(R("ew", 0, GC), R("tu"), R("e2"), R("dg"))
+            if t:
+                dma("y", None, R("ew", S0, S0 + n), T.ye[:, 0:n], T.ew[:, S0:S0 + n])
             gat2(R("ew", S0 + base, S0 + base + 512), R("dl"), R("du", 32, 64), R("e2"), A.add)
-        if t == 0:
+            if t:
+                dma("y", None, R("ew", S0 + n, GC), T.ye[:, n:GH], T.ew[:, S0 + n:GC])
+        def border():
             f2p("ps7", 160, 16, "c", [(zn, "gsn", 0)])
             f2p("ps7", 176, 16, "i", [(zn, "gsn", 256)])
             ts(R("sw", 0, 16), R("ps7", 160, 176), 1.0, A.min)
@@ -649,14 +676,14 @@ def rank_program(g, core, T, topo):
             tt(R("sn"), R("sn"), R("sw", 16, 32), A.max)
             tt(R("bt", 0, 16), R("bt", 0, 16), R("ab"), A.add)
             sendbases(1, "bt")
-            newrows(1)
-            for k in (KL, KR, KB):
-                zero("rn", blk(k) + P0, blk(k) + P0 + 512)
-        else:
+            slots()
+            ts(R("su"), R("sn"), float(S0), A.add)
+            act(R("mme", 0, 16), R("sn"), float(M))
+        if t:
             detlists()
-        f2p("ps2", 0, m, "c", [(zn, "rn", blk(KL))])
         child(0)
-        f2p("ps1", 0, m, "c", [(("zB", "zR")[t], "nb", S0)])
+        f2p("ps2", 0, m, "c", [(zn, "rn", blk(KL))])
+        childto(0)
         child(1)
         gat2(R("gn"), R("nb"), R("xu"), R("gq"), A.mult)
         f2p("ps3", 0, m, "c", [(zn, "rn", blk(KR))], M8)
@@ -664,13 +691,13 @@ def rank_program(g, core, T, topo):
         f2p("ps7", 128, 32, "c", [("zG%d" % t, "gn", 0)])
         f2p("ps4", 0, m, "c", [(zn, "rn", blk(KB))], M8)
         q0, q1, q2 = (R("pre", 192 * k, 192 * k + m) for k in range(3))
-        tt(q1, NS, PR, A.mult)
+        tt(q1, NS, q1, A.mult)
         tt(q2, NS, PB, A.mult)
         tt(E1, NS, R("eq", 0, m), A.mult)
         tt(SP, SP, R("eq", 192, 192 + m), A.max)
+        tt(q1, NP, q1, A.add)
         if t:
             children()
-            dma("y", None, R("ew", S0, GC), T.ye[:, :], T.ew[:, S0:GC])
 
         def done(x, k):
             if t == 0:
@@ -692,27 +719,19 @@ def rank_program(g, core, T, topo):
         tt(q1, E1, q1, A.max)
         tt(q2, SP, q2, A.max)
         done("l", 0)
-        tt(q1, R("ps1", 0, m), q1, A.add)
-        if t == 0:
-            slots()
-            ts(R("su"), R("sn"), float(S0), A.add)
-            act(R("mme", 0, 16), R("sn"), float(M))
-        tt(E1, NRm, R("eq", 384, 384 + m), A.mult)
+        childto(1)
         tt(PR, NRm, q1, A.max)
-        tt(q2, E1, q2, A.max)
+        tt(E1, NRm, R("eq", 384, 384 + m), A.mult)
         done("r", 1)
+        childto(2)
+        tt(q2, E1, q2, A.max)
         BN = R(px, 2 * w + m, 3 * w)
         tt(BN, R("ps7", 128, 160), BN, A.max)
         tt(PB, NBm, q2, A.max)
         done("b", 2)
         if t == 0:
+            border()
             detlists()
-            arrived("be", 1, "bel1", 0, 8)
-            gat2(R("win", GC, M), R("snf"), R("bel1"), R("gi"), A.add)
+            gat("s", R("gs", 0, 256), R("win", 0, GC), R("su"))
             children()
-            gat("s", R("x0"), R("ew", 0, GC), R("su"))
-            send("x0", 1, "x0", "ew", GC, 128)
-            d1, m1 = DA[1], 192
-            act(R("eo", 0, d1), R("ew", S0, S0 + d1))
-            cp(R("za", 2, 3 * (16 * m1 - d1), 3), R("ew", S0 + d1, S0 + 16 * m1))
     finish()

@@ -5,23 +5,26 @@ NR, P0, GH = 8, 2560, 3584
 S0 = 16
 GC, M = GH + S0, 3856
 BIG = 16384.0
-KB, KR, KL = 4352.0, 8192.0, 12032.0
+KB, KR, KL = 4352.0, 10368.0, 14336.0
+ZB = 6528
+TLR = ("w1", "uw")
 RN0 = 3840
-DA = (768, 896)
+DA = (768, 1024)
 CC = (3, 3)
 PCK = (2, 2)
-G3 = ((90, 160), (64, 128))
+G3 = ((70, 140), (80, 140))
+C2 = ((20, 60, 110), (24, 72, 132))
 HL = 24
-ZN = ["zz", "zB", "zR", "zL", "zE", "zB16", "zR16", "zL16", "zT16", "zMB", "zN0", "zN1", "zG0", "zG1", "zh", "q1", "q16", "d1", "d16", "d256"]
-_bf = {"win": M, "ew": M + 16, "w1": M + 16, "uw": M + 16, "za": 6912, "zb": 6912, "gl": 3328, "gr": 3328, "gb": 3072, "tr": 3072,
-       "hb": 3072, "eo": 1024, "ta": 1024, "nb": M, "rn": 12048, "dr": 2048, "dh": 2064, "dl": 2064, "msk": 2304, "nc0": 512, "nc1": 512,
+ZN = ["zz", "zB", "zR", "zL", "zE", "zB16", "zR16", "zL16", "zT16", "zMB", "zN0", "zN1", "zX", "zh", "q1", "q16", "d1", "d16", "d256"]
+_bf = {"win": M, "ew": M + 16, "w1": M + 16, "uw": M + 16, "zab": 14352, "gl": 3328, "gr": 3328, "gb": 3072, "tr": 3072,
+       "hb": 3072, "eo": 1024, "ta": 1024, "nb": M + 16, "dr": 2048, "dh": 2064, "dl": 2064, "msk": 2304, "nc0": 512, "nc1": 512,
        "it": 3072, "z": 144 * len(ZN), "z0": 432, "bo": 128, "ltm": 128, "nid": 128, "snf": 416, "krow": 256, "dm": 256,
-       "hi": 576, "lo": 576, "shi": 16, "slo": 16, "mh": 416, "ml": 416, "gs": 512, "x0": 256, "x1": 256, "x2": 256, "xa": 256, "gi": 256,
+       "hi": 576, "lo": 576, "meh": 208, "mel": 208, "nim": 128, "mh": 640, "ml": 224, "gs": 512, "x0": 256, "x1": 256, "x2": 256, "xa": 256, "gi": 256,
        "hot": 192, "m0": 256, "m1": 256, "m2": 256, "g1": 512, "gq": 512, "eg": 512, "gn": 512, "gsn": 512, "e2": 512, "dg": 512,
-       "ek": 576, "kh": 192, "tgh": 192, "tgl": 192, "m8": 192}
-_f32 = {"px0": 576, "px1": 672, "mc": 416, "me": 192, "me16": 192, "mme": 208, "lm": 208, "rm": 208, "dd": 416, "gt": 192, "thr": 192,
-        "cb": 224, "cw1": 224, "cw2": 200, "cs": 16, "tg": 256, "eq": 576, "ns": 192, "sp": 192, "pre": 576, "e1": 192, "e3": 192,
-        "wq": 576, "ci": 16, "mk": 16, "mk2": 8, "zc": 24, "i16": 16, "cc": 192, "sn": 16, "xs": 32, "bt": 80, "srf": 32, "ab": 16,
+       "ek": 224, "kh": 224, "tgh": 224, "tgl": 224, "m8": 224}
+_f32 = {"px0": 480, "px1": 576, "po": 672, "me": 192, "me16": 192, "idf": 128, "lm": 208, "rm": 208, "gt": 192, "thr": 192,
+        "cb": 224, "cw1": 224, "cw2": 200, "cs": 16, "tg": 256, "eq": 672, "pre": 672,
+        "ci": 16, "mk": 16, "mk2": 8, "zc": 24, "cc": 224, "sn": 16, "xs": 32, "bt": 80, "srf": 32, "ab": 16,
         "sw": 32, "kj": 32, "jj": 32, "nj": 64, "dj": 32, "inv": 64, "aj": 32, "pk": 64, "tq": 32, "dq": 64}
 _i32 = {"xin": 480, "sin": 32, "wti": 2, "pid": 4, "di": 64, "da": 64}
 _u16 = {"lv": 208, "rv": 208, "bv": 192, "lw": 208, "rw": 208, "sa": 32, "su": 16, "bes": 16, "bel0": 16, "bel1": 16,
@@ -71,7 +74,7 @@ def tracker(g, T):
                 ps = r[0][:2] == "ps"
                 for (x, k, tok) in acc.get(r[0], []):
                     if ps:
-                        if tok[2] == q and (q == "t" or wr or not k):
+                        if tok[2] == q and (q == "t" or not (k or wr) or not hit(r, x)):
                             continue
                     elif not (k or wr) or not hit(r, x) or (q == "t" and tok[2] == q):
                         continue
@@ -101,9 +104,9 @@ def tracker(g, T):
         snap[(sem, cnt[q])] = s
         note(q, reads, writes, (sem, cnt[q], q, False))
 
-    def dma(q, out, in_, oap, iap):
+    def dma(q, out, in_, oap, iap, after=()):
         rd, wr = ([in_] if in_ else []), ([out] if out else [])
-        deps(q, rd, wr)
+        deps(q, rd + list(after), wr)
         sem = "d%d" % nd[0]; nd[0] += 1
         Q[q].dma_start(out=oap, in_=iap).then_inc(T.sem[sem], 16)
         top[sem] = 16
@@ -137,6 +140,8 @@ def rank_program(g, core, T, topo):
         if n in AL:
             o, w = AL[n]
             return ("pf", o + a, o + (w if b is None else b), step, row)
+        if n in ("za", "zb"):
+            return ("zab", a + ZB * (n == "zb"), b + ZB * (n == "zb"), step, row)
         return (n, a, (SCRATCH[n][1][1] if b is None else b), step, row)
 
     def ap(r):
@@ -198,23 +203,41 @@ def rank_program(g, core, T, topo):
 
     def f2p(ps, c0, n, mode, terms, minus=(), first=True, last=True):
         mm, rd = [], []
-        for z, src, a0 in terms:
+        for z, src, a0, *lim in terms:
             k = {"d": 8, "q": 4}.get(mode, 16)
-            rd.append(R(src, a0, a0 + k * n))
+            lo, hi = lim or (0, k * n)
+            rd.append(R(src, a0, a0 + hi - lo))
             for i in range(k):
                 zi = z[i % 2] if isinstance(z, tuple) else z
                 o = 144 * ZN.index(zi) + 15 - (2 * i if mode == "d" else i)
                 rd.append(ZR(zi))
-                mm.append((T.z[:, o:o + 128], T[src][:, a0 + n * i:a0 + n * i + n] if mode == "c" else T[src][:, a0 + i:a0 + k * n:k]))
-        for r in minus:
-            rd += [r, R("nid")]
-            mm.append((T.nid[:, :], ap(r)))
-        op("t", rd, [R(ps)], [lambda e, k=k, l=l, x=x: e.matmul(T[ps][:, c0:c0 + n], l, x, first and k == 0, last and k == len(mm) - 1)
-                              for k, (l, x) in enumerate(mm)])
+                a, b = max(lo, n * i), min(hi, n * i + n)
+                if mode != "c":
+                    mm.append((T.z[:, o:o + 128], T[src][:, a0 + i:a0 + k * n:k], 0, n))
+                elif a < b:
+                    mm.append((T.z[:, o:o + 128], T[src][:, a0 + a - lo:a0 + b - lo], a - n * i, b - n * i))
+        for z, r, *c in minus:
+            rd += [r, R(z)]
+            mm.append((T[z][:, :], ap(r)) + (tuple(c) or (0, n)))
+        full = [x for x in mm if x[3] - x[2] == n]
+        mm = full[:1] + [x for x in mm if x[3] - x[2] < n] + full[1:]
+        op("t", rd, [R(ps)], [lambda e, k=k, x=x: e.matmul(T[ps][:, c0 + x[2]:c0 + x[3]], x[0], x[1], first and k == 0, last and k == len(mm) - 1)
+                              for k, x in enumerate(mm)])
 
-    def p2f(tab, row, col, src, c0, n):
+    def p2f(tab, row, col, src, c0, n, q="y"):
         out = R(tab, col, col + 16 * n, 1, row)
-        dma("y", out, R(src, c0, c0 + n), ap(out), T[src][:, c0:c0 + n])
+        dma(q, out, R(src, c0, c0 + n), ap(out), T[src][:, c0:c0 + n])
+
+    def copy(out, a, q="y"):
+        dma(q, out, a, ap(out), ap(a))
+
+    def unfold(tab, row, col, n, k, ps, c0, part=3):
+        h, l = R("hi", 192 * k, 192 * k + n), R("lo", 192 * k, 192 * k + n)
+        if part & 1:
+            copy(h, R(tab, col, col + 16 * n, 1, row))
+            copy(l, R(tab, col, col + 16 * n, 1, row + 1))
+        if part & 2:
+            f2p(ps, c0, n, "c", [], (("nid", h), ("nid", l)))
 
     def halves(src, a, b, h, l, ha, q="s"):
         if q == "s":
@@ -267,20 +290,36 @@ def rank_program(g, core, T, topo):
 
     op("g", [], [R("pid", 0, 1)], [lambda e: e.iota(T.pid[:, 0:1], [[1, 1]], 0, 1)])
     fill(R("bo"), 1.0)
-    iof("cc", 0, 192, [[1, 192]], 0)
-    fill(R("nid"), -1.0)
-    fill(R("win"), 0.25)
+    iof("cc", 0, 224, [[1, 224]], 0)
+    fill(R("win", 0, S0 + P0), 0.25)
+    act(R("win", S0 + P0, M), R("win", 0, M - S0 - P0))
     op("g", [R("bo")], [R("bo")], [lambda e: e.affine_select(T.bo[:, :], T.bo[:, :], [[-16, 8], [0, 16]], A.is_ge, 0.0, 0, 1)])
     op("g", [R("bo")], [R("bo")], [lambda e: e.affine_select(T.bo[:, :], T.bo[:, :], [[16, 8], [0, 16]], A.is_ge, 0.0, 15, -1)])
     iof("gi", 0, 256, [[0, 2], [-7, 16], [15, 8]], 0)
     iof("xs", 16, 32, [[128, 2], [1, 8]], S0)
+    fill(R("idf"), 1.0)
+    op("g", [R("idf")], [R("idf")], [lambda e: e.affine_select(T.idf[:, :], T.idf[:, :], [[-1, 128]], A.is_equal, 0.0, 0, 1)])
+    op("g", [R("bo")], [R("ltm")], [lambda e: e.affine_select(T.ltm[:, :], T.bo[:, :], [[1, 128]], A.is_ge, 0.0, 0, -1)])
+    iof("krow", 0, 256, [[1, 256]], 0)
+    iof("tg", 0, 256, [[0, 16], [1, 16]], 0)
     ts(R("pid", 1, 2), R("pid", 0, 1), 15, A.bitwise_and)
     fill(R("z0"), 0.0)
     ts(R("pid", 2, 3), R("pid", 1, 2), 1, A.logical_shift_right)
     cp(R("ci", 0, 1), R("pid", 1, 2))
     cp(R("ci", 1, 2), R("pid", 2, 3))
     I1, I2 = R("ci", 0, 1), R("ci", 1, 2)
+    ROW = {"l": 4, "r": 2, "b": 0}
+    XIN = (("b", 320), ("l", 0), ("r", 160))
+    for x, c in XIN:
+        cp(R("px0", c, c + 160), R("xin", c, c + 160))
+    for x, c in XIN:
+        halves("px0", c, c + 160, "hi", "lo", c)
+    for x, c in XIN:
+        for k, src in enumerate(("hi", "lo")):
+            p2f("win", ROW[x] + k, S0, src, c, 160, "sy"[k])
     fill(R("ew", 0, S0), 0.0)
+    ts(R("sa"), R("sin"), float(S0), A.add)
+    cp(R("su"), R("sa", 16, 32))
     ts(R("mk"), R("cc", 0, 16), I1, A.is_equal)
     ts(R("mk2"), R("cc", 0, 8), I2, A.is_equal)
     cp(R("z0", 15, 143, 16), R("bo", 0, 128, 16))
@@ -289,90 +328,79 @@ def rank_program(g, core, T, topo):
     cp(R("z0", 160, 288, 16), R("bo", 0, 128, 16))
     cp(R("z0", 303, 431, 4), R("bo", 0, 128, 4))
     ts(R("zc", 0, 5), R("mk2", 0, 5), R("ci", 6, 7), A.add)
-    ts(R("zc", 5, 7), R("mk2", 5, 7), 1.0 / KR, A.mult)
-    for k, (f, b) in enumerate(((160.0, 0.0), (64.0, float(P0)), (192.0, 0.0), (8.0, float(GH))), 2):
-        ts(R("ci", k, k + 1), I1, f, A.mult, b, A.add)
+    for k, f, b in ((11, 160.0, 0), (12, 192.0, 0), (13, 224.0, 0), (14, 64.0, P0), (5, 8.0, GH)):
+        ts(R("ci", k, k + 1), I1, f, A.mult, float(b), A.add)
     Z1, Z2, Z4 = R("z0", 0, 144), R("z0", 144, 288), R("z0", 288, 432)
 
     def zmat(z, col, src=Z1):
         act(ZR(z), src, col)
-    for z, k in (("zB16", 0), ("zL16", 2), ("zR16", 1), ("zT16", 4), ("zG0", 5), ("zG1", 6)):
-        zmat(z, R("zc", k, k + 1))
-    W0 = 192
-    ROW = {"l": 4, "r": 2, "b": 0}
-    for x, c, o in (("b", 320, 2), ("l", 0, 0), ("r", 160, 1)):
-        halves("xin", c, c + 160, "hi", "lo", W0 * o, "v")
-        for k, src in enumerate(("hi", "lo")):
-            p2f("win", ROW[x] + k, S0, src, W0 * o, 160)
-    ts(R("sa"), R("sin"), float(S0), A.add)
-    cp(R("su"), R("sa", 16, 32))
     gat("s", R("x0"), R("ew", 0, S0 + P0), R("su"))
     send("x0", 0, "x0", "ew", GC, 128)
-    for z, k in (("zL", 2), ("zR", 1), ("zB", 0), ("zE", 3), ("zN0", 5), ("zN1", 6)):
-        zmat(z, R("mk2", k, k + 1))
+    for z, k in (("zB16", 0), ("zL16", 2), ("zR16", 1)):
+        zmat(z, R("zc", k, k + 1))
     ts(R("ci", 7, 8), R("mk", 0, 1), 3840.0, A.mult)
     cp(R("sn"), R("sin", 16, 32))
     ts(R("snf"), R("win", M - 416, M), 0.0, A.mult, R("ci", 7, 8), A.add)
 
-    def slots():
-        halves("sn", 0, 16, "shi", "slo", 0, "v")
-        for k, src in enumerate(("shi", "slo")):
+    def numbers(a, b):
+        ts(R("meh", a, b), R("cc", a, b), 16.0, A.mult)
+        ts(R("mel", a, b), R("cc", a, b), 0.0, A.mult, I1, A.add)
+
+    def slots(c):
+        halves("sn", 0, 16, "meh", "mel", c, "v")
+        for k, src in enumerate(("meh", "mel")):
             for s in range(2):
-                p2f("snf", k, 16 + 144 * s, src, 8 * s, 8)
-    slots()
+                p2f("snf", k, 16 + 144 * s, src, c + 8 * s, 8)
+    slots(160)
     load("y", R("wti", 0, 1), T.wt[:, :])
     load("y", R("wti", 1, 2), T.th[:, :])
-    load("y", R("eo", 0, DA[0]), T.err[:, 0:DA[0]])
-    ts(R("me"), R("cc"), 16.0, A.mult, I1, A.add)
+    load("y", R("eo", 0, DA[0]), T.err[:, P0 - DA[0]:P0])
+    ts(R("me"), R("cc", 0, 192), 16.0, A.mult, I1, A.add)
     tt(R("zc", 8, 9), R("mk", 14, 15), R("mk", 15, 16), A.subtract)
-    ts(R("mme", 16, 208), R("me"), float(M), A.mult)
     ts(R("zc", 8, 9), R("mk2", 0, 1), float(M), A.mult, R("zc", 8, 9), A.add)
-    ts(R("mme", 0, 16), R("sn"), float(M), A.mult)
     ts(R("gi"), R("gi"), R("mk", 14, 15), A.mult)
-    zmat("zMB", R("zc", 8, 9))
-    act(R("me16"), R("me"), 1.0, float(S0))
-    ts(R("mc", 0, 160), R("cc", 0, 160), R("ci", 2, 3), A.add)
-    ts(R("mc", 160, 224), R("cc", 0, 64), R("ci", 3, 4), A.add)
-    ts(R("mc", 224, 416), R("cc"), R("ci", 4, 5), A.add)
+    numbers(0, 160)
 
     def early(k):
         if k == 0:
-            halves("mc", 0, 416, "mh", "ml", 0, "v")
+            zmat("zMB", R("zc", 8, 9))
+            act(R("me16"), R("me"), 1.0, float(S0))
+            cp(R("ml"), R("cc"))
+            for j, (a, b) in enumerate(((0, 160), (160, 352), (352, 576), (576, 640))):
+                act(R("mh", a, b), R("cc", 0, b - a), 0.0, R("ci", 11 + j, 12 + j), F.Identity)
             iof("msk", 0, 2304, [[0, 768], [256, 3]], 0)
-            op("g", [R("nid")], [R("nid")], [lambda e: e.affine_select(T.nid[:, :], T.nid[:, :], [[-1, 128]], A.is_equal, 0.0, 0, 1)])
-            op("g", [R("bo")], [R("ltm")], [lambda e: e.affine_select(T.ltm[:, :], T.bo[:, :], [[1, 128]], A.is_ge, 0.0, 0, -1)])
-            iof("krow", 0, 256, [[1, 256]], 0)
-            iof("tg", 0, 256, [[0, 16], [1, 16]], 0)
+            ts(R("nim"), R("idf"), -float(M), A.mult)
+            ts(R("nid"), R("idf"), -1.0, A.mult)
         if k == 1:
+            fill(R("ew", S0 + P0, GC), 0.0)
             for w in ("ew", "w1", "uw"):
-                fill(R(w, S0 + P0, GC), 0.0)
                 fill(R(w, M, M + 16), 0.0)
             for w in ("w1", "uw"):
                 fill(R(w, 0, S0), 0.0)
+                dma("y", R(w, S0 + P0, GC), R("ew", S0 + P0, GC), T[w][:, S0 + P0:GC], T.ew[:, S0 + P0:GC])
         if k == 2:
-            for o, c in enumerate((0, 160, 320)):
-                cp(R("px0", W0 * o, W0 * o + 160), R("xin", c, c + 160))
+            ts(R("zc", 5, 6), R("mk", 14, 15), 2.0 * KR, A.mult, R("zc", 1, 2), A.add)
             cp(R("ci", 8, 10), R("wti"))
+            ts(R("zc", 5, 6), R("mk", 10, 11), -0.5, A.mult, R("zc", 5, 6), A.add)
+            tt(R("zc", 4, 5), R("zc", 1, 2), R("mk", 8, 9), A.add)
             ts(R("ci", 10, 11), R("ci", 9, 10), -1.0, A.mult, 0.5, A.add)
+            for z, f, src in (("zz", 1.0, Z1), ("q1", 1.0, Z4), ("q16", 16.0, Z4), ("d1", 1.0, Z2), ("d16", 16.0, Z2), ("d256", 256.0, Z2)):
+                ts(ZR(z), src, f, A.mult)
 
     def later(k):
         if k == 0:
-            zmat("zz", 1.0)
-            for z, f, src in (("q1", 1.0, Z4), ("q16", 16.0, Z4), ("d1", 1.0, Z2), ("d16", 16.0, Z2), ("d256", 256.0, Z2)):
-                zmat(z, f, src)
-            for w in ("cb", "cw1", "cw2"):
-                act(R(w), R("mc", 0, SCRATCH[w][1][1]), 0.0, BIG)
-            act(R("cb", 0, 1), R("cc", 0, 1), 0.0)
+            for z, k in (("zL", 2), ("zR", 1), ("zB", 0), ("zE", 3), ("zN0", 5), ("zN1", 6)):
+                zmat(z, R("mk2", k, k + 1))
             act(R("kj"), R("cc", 0, 32), 8.0, I2, F.Identity)
-            act(R("inv"), R("cc", 0, 64), 0.0)
             act(R("xs", 0, 16), R("me", 0, 16), 1.0, float(GC))
             act(R("xs", 16, 32), R("xs", 16, 32), 1.0, R("ci", 5, 6), F.Identity)
             act(R("nj", 32, 64), R("me", 0, 32), 1.0, float(P0))
         else:
+            zmat("zT16", R("zc", 4, 5))
+            zmat("zX", R("zc", 5, 6))
             zmat("zh", R("ci", 8, 9))
             act(R("dj"), R("me", 0, 32), 1.0, float(M))
             act(R("dl", 2048, 2064), R("cc", 0, 16), 0.0, -128.0)
-            act(R("dh", 0, 2048), R("dr"), 0.5, 127.8)
             act(R("dl", 0, 2048), R("dh", 0, 2048), 1.0, -256.0)
 
     def newrows(t):
@@ -385,6 +413,9 @@ def rank_program(g, core, T, topo):
             iof("it", 0, 512, [[0, 16], [1, 32]], 0)
             iof("it", 512, 1024, [[0, 16], [2, 16]], 0, 2)
             iof("it", 513, 1024, [[0, 16], [-2, 16]], -1, 2)
+
+    def newrows2(t):
+        hi = 1024 + 1024 * t
         for row, c in ((10 + 2 * t, hi), (11 + 2 * t, 0), (2 * t, hi + 512), (2 * t + 1, 512)):
             out = R("nc%d" % t, 0, 512, 1, row)
             dma("y", out, R("it", c, c + 512), ap(out), T.it[0:8, c:c + 512])
@@ -398,94 +429,92 @@ def rank_program(g, core, T, topo):
         n, w = 16 * m, m + 32
         base, d, nsb = n, DA[t], m // 16
         px = "px%d" % t
-        PL, PR, PB = R(px, 0, m), R(px, w, w + m), R(px, 2 * w, 2 * w + m)
-        cut = [d // 16 + (m - d // 16) * k // CC[t] // 2 * 2 for k in range(CC[t] + 1)]
-        CH = list(zip(cut[:-1], cut[1:]))
-        PC = [0] + [16 + x for x in (cut[0], cut[PCK[t]], m)]
-        PC = list(zip(PC[:-1], PC[1:]))
+        PL, PR, PB = R(px, 0, m), R(px, m, 2 * m), R(px, 2 * m, 3 * m)
+        ca = m - d // 16
+        cut = [ca * k // 3 // 2 * 2 for k in range(3)] + [ca]
+        CH = [(cut[2], ca), (0, cut[1]), (cut[1], cut[2])]
+        PC = [(cut[2], m + 16), (0, cut[2])]
         EW, W1, UW = R("ew"), R("w1"), R("uw")
 
         def sl(buf, a, b, k):
-            return R(buf, 3 * (16 * a - d) + k, 3 * (16 * b - d), 3)
-
-        def L(x, a, b):
-            return R(x, 16 + a, 16 + b)
+            return R(buf, 48 * a + k, 48 * b, 3)
+        L = R
 
         def col(buf, a, b):
             return R(buf, S0 + 16 * a, S0 + 16 * b)
+
+        def own(k):
+            o, x = sl("za", *CH[k], 2), col("ew", *CH[k])
+            op("g", [x], [o], [lambda e: e.affine_select(ap(o), ap(x), [[0, x[2] - x[1]]], A.is_ge, 0.0, 0, 0)])
         if t == 0:
-            gat("s", R("gs", 0, 256), WIN, R("sa", 0, 16))
-            gat("s", R("gs", 256, 512), WIN, R("su"))
+            gat("s", R("gs", 0, 256), R("win", 0, S0 + n), R("sa", 0, 16))
+            gat("s", R("win", S0 + n, S0 + n + 256), R("win", 0, S0 + n), R("su"))
             f2p("ps3", 0, 16, "c", [("zB16", "gs", 0)])
-            cp(sl("za", d // 16, m, 2), col("ew", d // 16, m))
             sendbases(0, "ps3")
             cp(R("bt", 0, 16), R("ps3", 0, 16))
+            cp(sl("za", 0, ca, 2), col("ew", 0, ca))
             early(0)
-            for ps, z in (("ps0", "zL16"), ("ps1", "zR16")):
-                f2p(ps, 16, m, "i", [(z, "win", S0)])
-                f2p(ps, 0, 16, "i", [(z, "gs", 256)])
-            f2p("ps2", 0, m, "i", [("zB16", "win", S0)])
-            for k, z in enumerate(("zL16", "zR16")):
-                f2p("ps3", 32 + 16 * k, 16, "c", [(z, "gs", 0)])
             later(0)
-            load("y", R("dr"), T.det[:, :])
-        else:
-            for ps, z in (("ps0", "zL16"), ("ps1", "zR16")):
-                f2p(ps, 16, m, "i", [(z, "win", S0)])
-                f2p(ps, 0, 16, "i", [(z, "gs", 0)])
-            f2p("ps2", 0, m, "i", [("zB16", "win", S0)])
+        for k, (a, b) in enumerate(PC):
+            for j in range(2):
+                f2p("ps%d" % (2 * k + j), 0, b - a, "i", [((("zL16", "zR16"), ("zB", "zE"))[t][j], (TLR[j] if t else "win"), S0 + 16 * a)])
+        if t:
             gat("s", R("x0"), R("ew", 0, GC), R("su"))
             send("x0", 1, "x0", "ew", GC, 128)
-            newrows(1)
-            for k in (KL, KR, KB):
-                zero("rn", blk(k) + P0, blk(k) + P0 + 512)
-            act(R("eo", 0, d), col("ew", 0, d // 16))
+            copy(R("eo", 0, d), col("ew", ca, m))
+            newrows2(1)
+            for k in range(2):
+                own(k)
 
         def ghosts():
             arrived("be", t, "bel%d" % t, 0, 8)
             gat2(R("win", GC, M), R("snf"), R("bel%d" % t), R("gi"), A.add)
-        for ps, v, x in (("ps0", "lv", "lm"), ("ps1", "rv", "rm")):
-            cp(R(v, 0, 16 + m), R(ps, 0, 16 + m))
-            tt(R(x, 0, 16 + m), R(ps, 0, 16 + m), R("mme", 0, 16 + m), A.subtract)
-            if t == 0:
-                early(1 + (x == "rm"))
-            elif x == "lm":
-                ghosts()
-                cp(sl("za", d // 16, m, 2), col("ew", d // 16, m))
-        if t == 0:
-            zero("nb", 0, 1024)
-            ghosts()
         VB = ("ps4", "ps5", "ps6", "ps7")
+
+        def lists(k, j):
+            (a, b), x, ps = PC[k], "lr"[j], "ps%d" % (2 * k + j)
+            ts(R(x + "v", a, b), R(ps, 0, b - a), float(S0 * t), A.add)
+            act(R(x + "m", a, b), R(ps, 0, b - a), 1.0, float(S0 * t))
+            f2p(VB[2 * k + j], 0, b - a, "i", [], (("nim", R("meh", a, b)), ("nim", R("mel", a, b)), ("idf", R(x + "m", a, b))), last=False)
+        if t:
+            ghosts()
+        for k in range(2):
+            for j in range(2):
+                if t == 0 or k == 0:
+                    lists(k, j)
+            if t == 0:
+                early(1 + k)
+        if t == 0:
+            zero("nb", 0, 1536)
+            ghosts()
 
         def legs(k, x):
             a, b = PC[k]
-            ps = VB[(2 * k + (x == "r")) % 4]
-            f2p(ps, 0, b - a, "i", [("zMB", "g" + x, 16 * a)])
-            o = 208 * (x == "r")
-            tt(R("dd", o + a, o + b), R(ps, 0, b - a), R(x + "m", a, b), A.add)
-            ts(R(x + "w", a, b), R("dd", o + a, o + b), float(M), A.min)
+            ps = VB[2 * k + (x == "r")]
+            f2p(ps, 0, b - a, "i", [("zMB", "g" + x, 16 * a)], first=False)
+            ts(R(x + "w", a, b), R(ps, 0, b - a), float(M), A.min)
         for k, (a, b) in enumerate(PC):
             gat("v", R("gl", 16 * a, 16 * b), WIN, R("lv", a, b))
             gat("s", R("gr", 16 * a, 16 * b), WIN, R("rv", a, b))
-            if k == 0:
-                ts(R("bv", 0, m), R("ps2", 0, m), float(GC - 1), A.min)
-                tt(R("gt", 0, m), R("ps2", 0, m), R("me16", 0, m), A.is_gt)
-            if k:
-                legs(k - 1, "l")
-                legs(k - 1, "r")
-        XL, XR = R("lw", 0, 16), R("rw", 0, 16)
+            if k == 0 and t:
+                lists(1, 0)
+                lists(1, 1)
+        legs(0, "l")
+        legs(0, "r")
+        XL, XR = R("lw", m, m + 16), R("rw", m, m + 16)
 
         def three(win, own, slots_, out, dst, side):
             for k, (a, b) in enumerate(CH):
                 gat("s", sl(slots_, a, b, 0), win, L("lw", a, b))
                 gat("s", sl(slots_, a, b, 1), win, L("rw", a, b))
-            side(0)
-            gat2(R("ta", 0, d), win, L("lw", 0, d // 16), own, A.max)
-            side(1)
-            gat2(col(dst, 0, d // 16), win, L("rw", 0, d // 16), R("ta", 0, d), A.max)
+                if k == 0:
+                    side(0)
+                    gat2(R("ta", 0, d), win, L("lw", ca, m), own, A.max)
+                    side(1)
+            gat2(col(dst, ca, m), win, L("rw", ca, m), R("ta", 0, d), A.max)
             side(2)
             for k, (a, b) in enumerate(CH):
-                u, v = 3 * (16 * a - d), 3 * (16 * b - d)
+                u, v = 48 * a, 48 * b
                 scan(R(out, u, v), R("msk", 0, v - u), R(slots_, u, v), A.min, A.max)
                 cp(col(dst, a, b), sl(out, a, b, 2))
                 side(3 + k)
@@ -494,16 +523,22 @@ def rank_program(g, core, T, topo):
         gat2(R("xa"), EW, XL, R("x0"), A.max)
         gat2(R("x1"), EW, XR, R("xa"), A.max)
         send("x1", t, "x1", "w1", GC, 128)
-        legs(len(PC) - 1, "l")
-        legs(len(PC) - 1, "r")
         if t == 0:
-            zero("nb", 1024, M)
-        three(EW, R("eo", 0, d), "za", "zb", "w1", lambda k: None)
-        if t:
-            for k, z in enumerate(("zL", "zR", "zB")):
-                f2p("ps%d" % k, 0, m, "c", [(z, "win", S0)])
-                act(R(px, w * k, w * k + m), R("ps%d" % k, 0, m))
-        mh, ml = R("mh", 224 * t, 224 * t + m), R("ml", 224 * t, 224 * t + m)
+            zero("nb", 1536, M + 16)
+            load("y", R("dr"), T.det[:, :])
+        else:
+            own(2)
+
+        def side1(k):
+            if k < 2:
+                legs(1, "lr"[k])
+            if k == 2:
+                f2p("ps2", 0, m, "i", [("zB16", "win", S0)])
+            if k == 3:
+                ts(R("bv", 0, m), R("ps2", 0, m), float(GC - 1), A.min)
+                tt(R("gt", 0, m), R("ps2", 0, m), R("me16", 0, m), A.is_gt)
+        three(EW, R("eo", 0, d), "za", "zb", "w1", side1)
+        mh, ml = R("mh", 160 * t, 160 * t + m), R("ml", 0, m)
         g3 = (0,) + G3[t] + (m,)
 
         def bases(k):
@@ -511,20 +546,32 @@ def rank_program(g, core, T, topo):
                 gat("s", R("gb", 16 * g3[k], 16 * g3[k + 1]), WIN, R("bv", g3[k], g3[k + 1]))
         bases(0)
         for k, z in enumerate(("zL", "zR", "zB")):
-            f2p("ps%d" % (4 + k), 0, m, "c", [(z, "gr", 256)], (mh, ml))
+            f2p("ps%d" % (4 + k), 0, m, "c", [(z, "gr", 0)], (("nid", mh), ("nid", ml)))
+            if k == 0:
+                for j, x in enumerate("lrb"):
+                    if t:
+                        unfold("win", ROW[x], S0, m, j, "ps%d" % j, 0)
+                    elif j < 2:
+                        f2p("ps3", 32 + 16 * j, 16, "c", [(("zL16", "zR16")[j], "gs", 0)])
         arrived("x1", t, "w1", GC, 128)
         gat("v", R("xa"), W1, XL)
         gat2(R("x2"), W1, XR, R("xa"), A.max)
         send("x2", t, "x2", "uw", GC, 128)
         if t == 0:
+            for x, a in (("cb", 1), ("cw1", 0), ("cw2", 0)):
+                iof(x, a, SCRATCH[x][1][1], [[0, SCRATCH[x][1][1] - a]], int(BIG))
+            zero("cb", 0, 1)
+            zero("inv", 0, 32)
             newrows(0)
-            for k in (KL, KR, KB):
-                zero("rn", blk(k), blk(k) + P0)
-        c2 = [0, m // 8, 3 * m // 8, 11 * m // 16, m]
-        c2 = [x // 2 * 2 for x in c2]
+            zero("zab", ZB + 3 * (n - d), blk(KL) + 3072)
+            newrows(1)
+        c2 = (0,) + C2[t] + (m,)
         for k, (a, b) in enumerate(zip(c2[:-1], c2[1:])):
             gat("s", R("tr", 16 * a, 16 * b), W1, L("rw", a, b))
             gat2(col("uw", a, b), W1, L("lw", a, b), R("tr", 16 * a, 16 * b), A.max)
+        if t:
+            for k in range(3):
+                act(R(px, m * k, m * k + m), R("ps%d" % k, 0, m), -1.0)
         bases(1)
         pl, pr, pb = (R("ps%d" % j, 0, m) for j in (4, 5, 6))
         ts(R("ek", 0, m), pr, 0.0, A.is_equal, KR, A.mult)
@@ -532,19 +579,21 @@ def rank_program(g, core, T, topo):
         ts(pb, pb, 0.0, A.is_equal, KB, A.mult)
         tt(R("kh", 0, m), pl, R("ek", 0, m), A.max)
         if t == 0:
-            for k, src in enumerate(("mh", "ml")):
-                p2f("win", 6 + k, S0, src, 0, 160)
-                for row in (0, 2, 4, 6):
-                    p2f("win", row + k, S0 + P0, src, 160, 64)
+            for k, (src, a, b) in enumerate((("mh", 352, 576), ("ml", 0, 0))):
+                p2f("win", 6 + k, S0, src, a, 224)
+                for row in (0, 2, 4):
+                    p2f("win", row + k, S0 + P0, src, b, 64)
             ts(R("dm"), R("tg"), I1, A.is_le, BIG, A.mult)
             cp(R("bt", 32, 64), R("ps3", 32, 64))
-            cp(R("bt", 64, 80), R("rv", 0, 16))
-        tt(pb, pb, R("kh", 0, m), A.max)
+            cp(R("bt", 64, 80), R("rv", m, m + 16))
+        tt(R("kh", 0, m), pb, R("kh", 0, m), A.max)
         arrived("x2", t, "uw", GC, 128)
+        if t == 0:
+            newrows2(0)
 
         def side3(k):
-            if k == 1:
-                tt(pb, pb, PR, A.add)
+            if k == 2:
+                copy(R("eo", 0, d), col("w1", ca, m))
             if t == 0 and k == 1:
                 tt(R("srf"), R("bt", 48, 80), R("xs"), A.is_equal)
                 tt(R("ab"), R("bt", 48, 64), R("bt", 32, 48), A.subtract)
@@ -553,21 +602,18 @@ def rank_program(g, core, T, topo):
                 tt(R("ab"), R("ab"), R("srf", 0, 16), A.mult)
             if t == 0 and k == 3:
                 tt(R("ab"), R("ab"), R("bt", 32, 48), A.add)
-        three(UW, col("w1", 0, d // 16), "zb", "za", "w1", side3)
+        three(UW, col("w1", ca, m), "zb", "za", "w1", side3)
         bases(2)
-        act(R("tgh", 0, m), R("ps6", 0, m))
-        act(R("eo", 0, d), col("w1", 0, d // 16))
+        for row, src in ((8, "kh"), (10, "ek")):
+            p2f("win", row, S0, src, 0, m)
+        if t == 0:
+            act(R("dh", 0, 2048), R("dr"), 0.5, 127.8)
         f2p("ps3", 0, m, "i", [("zB", "gb", 0)])
-        e16 = d // 16 - HL
-        HC = CH + [(0, e16), (e16, d // 16)]
+        HC = CH + [(ca, m)]
         for k, (a, b) in enumerate(HC):
-            own = sl("za", a, b, 2) if k < len(CH) else R("eo", 16 * a, 16 * b)
             hb = R("hb", 16 * a, 16 * b)
-            gat2(hb, R("w1", 0, GC), R("bv", a, b), own, A.max)
+            gat2(hb, R("w1", 0, GC), R("bv", a, b), sl("za", a, b, 2) if k < len(CH) else R("eo", 0, d), A.max)
             if k == 0:
-                tt(R("tgl", 0, m), R("ps6", 0, m), R("tgh", 0, m), A.subtract)
-                for row, src in ((8, "tgh"), (9, "tgl"), (10 + 2 * t, "ek"), (11 + 2 * t, "ek")):
-                    p2f("win", row, S0, src, 0, m)
                 tt(R("ps3", 0, m), R("ps3", 0, m), R("me", 0, m), A.is_equal)
             if k < len(HC) - 1:
                 act(hb, hb, 1.0, R("ci", 10, 11), F.Sign)
@@ -576,8 +622,8 @@ def rank_program(g, core, T, topo):
             f2p(VB[k % 4], 0, b - a, "i", [("zz", "hb", 16 * a)])
             if k == 1:
                 tt(R("gt", 0, m), R("ps3", 0, m), R("gt", 0, m), A.mult)
-                act(R("thr", 0, m), R("gt", 0, m), -103.0, 99.0)
-                act(R("thr", e16, d // 16), R("gt", e16, d // 16), -87.0, 99.0)
+                act(R("thr", 0, ca), R("gt", 0, ca), -103.0, 99.0)
+                act(R("thr", ca, m), R("gt", ca, m), -87.0, 99.0)
             if k >= 2:
                 u, v = HC[k - 2]
                 tt(R("hot", u, v), R(VB[(k - 2) % 4], 0, v - u), R("thr", u, v), A.is_ge)
@@ -593,6 +639,10 @@ def rank_program(g, core, T, topo):
         f2p("ps3", 0, 64, "q", [("q16", "m0", 0)], last=False)
         f2p("ps4", 0, 32, "d", [("d256", "m0", 0)], last=False)
         scan(R("cw1", 1, m + 1), R("dm", 0, m), R("cb", 1, m + 1), A.add, A.min)
+        for k in (KL, KR, KB):
+            for row in (10 + 2 * t, 11 + 2 * t):
+                o = R("zab", blk(k), blk(k) + n, 1, row)
+                dma("ys"[row % 2], o, R("nb", 0, n, 1, 4), ap(o), T.nb[4::16, 0:n])
         act(R("pre", 192, 192 + m), PR, 1.0, -1.0)
         if t == 0:
             later(1)
@@ -615,123 +665,163 @@ def rank_program(g, core, T, topo):
         act(R("inv", 32, 64), R("inv", 32, 64), 4096.0)
         tt(R("tq"), R("ps4", 0, 32), R("aj"), A.add)
         ts(R("td"), R("tq"), float(S0), A.add)
-        gat("v", R("g1"), WIN, R("td"))
+        gat("s", R("g1"), WIN, R("td"))
         f2p("ps5", 0, 32, "i", [(("zE", "zB"), "g1", 0)])
-        tt(R("eq", 0, m), PL, PR, A.is_equal)
-        tt(R("eq", 192, 192 + m), PL, PB, A.is_equal)
+        EQ = [R("eq", 192 * k, 192 * k + m) for k in range(3)]
+        tt(EQ[0], PL, PR, A.is_equal)
+        tt(EQ[1], PL, PB, A.is_equal)
+        tt(EQ[2], PR, PB, A.is_equal)
+        if t == 0:
+            numbers(160, 192)
         ts(R("tu"), R("ps5", 0, 32), float(S0), A.add)
         nc, zn = R("nc%d" % t), "zN%d" % t
         gat("s", R("gq"), WIN, R("tu"))
         gat("s", R("eg"), R("ew", 0, GC), R("tu"))
         sca(R("nb"), R("tu"), nc)
+        for k in range(0 if t else 2, 3):
+            unfold("gq", (0, 6, 2)[k], 0, 32, k, None, 0, 1)
+        if t:
+            act(R("e2"), R("eg"), 0.5, 127.8)
+        else:
+            gat("s", R("gsn"), R("nb"), R("sa"))
+            for tab in TLR:
+                copy(R(tab, S0 + n, S0 + n + 512), R("gq"))
+            for row, src in ((4, 0), (5, 1), (2, 6), (3, 7)):
+                copy(R("win", S0 + n, S0 + n + 512, 1, row), R("gq", 0, 512, 1, src))
         f2p("ps6", 0, 32, "i", [("zT16", "gq", 0)])
-        f2p("ps6", 32, 32, "i", [("zR16", "gq", 0)])
         f2p("ps0", 0, m, "c", [(("zB", "zR")[t], "nb", S0)])
-        tt(R("eq", 384, 384 + m), PR, PB, A.is_equal)
+        f2p("ps7", 0, 32, "i", [("zX", "gq", 0)])
         cp(R("nj", 0, 32), R("ps5", 0, 32))
         tt(R("tq"), R("ps6", 0, 32), R("dj"), A.max)
         ts(R("ru"), R("tq"), -float(RN0), A.add)
-        cp(R("xu"), R("ps6", 32, 64))
-        if t == 0:
-            gat("s", R("gsn"), R("nb"), R("sa"))
-        sca(R("rn"), R("ru"), nc)
-        NS, SP, E1 = R("ps6", 64, 64 + m), R("ps6", 256, 256 + m), R("ps5", 64, 64 + m)
+        sca(R("zab"), R("ru"), nc)
+        NS, SP, E1 = R("ps6", 64, 64 + m), R("ps6", 288, 288 + m), R("ps5", 64, 64 + m)
         N0, NP = R("ps1", 0, m), R("ps1", 256, 256 + m)
         act(N0, R("ps0", 0, m), 1.0, 0.0, F.Abs)
         act(NS, N0, -1.0, 1.0, F.Relu)
         act(SP, N0, 1.0, 0.0, F.Sign)
         act(NP, R("ps0", 0, m), 1.0, 1.0, F.Abs)
         act(R("m8", 0, m), SP, 8192.0)
-        act(R("e2"), R("eg"), 0.5, 127.8)
-        M8 = (R("m8", 0, m),)
+        M8 = (("nid", R("m8", 0, m)),)
 
-        def child(k):
-            f2p(("ps7", "ps0")[k % 2], 32 * k, 32, "c", [(("zB", "zE", "zR")[k], "gq", 0)])
+        def new(k, a=0, b=m):
+            return R("po", w * k + a, w * k + b) if t else R("ps%d" % (2 + k), 256 + a, 256 + b)
+
+        def renamed(k, kb, z, minus):
+            f2p("ps%d" % (2 + k), 0, m, "c", [(zn, "zab", blk(kb))], minus)
+            if k < 2 and t:
+                unfold("gq", 0, 0, 32, k, "ps%d" % (2 + k), 256 + m, 2)
 
         def childto(k):
-            act(R(px, w * k + m, w * k + w), R(("ps7", "ps0")[k % 2], 32 * k, 32 * k + 32))
+            if t:
+                act(new(k, m, w), R("ps%d" % (2 + k), 256 + m, 256 + w), -1.0)
 
         def detlists():
-            f2p("ps7", 192, 32, "i", [("zh", "eg", 0)])
             for k in range(2):
                 tt(R("di", 32 * k, 32 * k + 32), R("ps7", 192, 224), R("nj", 32 * k, 32 * k + 32), A.add)
             ts(R("da"), R("di"), 2047, A.bitwise_and)
             tt(R("dq"), R("da"), R("inv"), A.add)
             ts(R("du"), R("dq"), 2048.0, A.min)
-            gat("s", R("dg"), R("dl"), R("du", 0, 32))
 
         def children():
             sca2(R("ew", 0, GC), R("tu"), R("e2"), R("dg"))
             if t:
                 dma("y", None, R("ew", S0, S0 + n), T.ye[:, 0:n], T.ew[:, S0:S0 + n])
-            gat2(R("ew", S0 + base, S0 + base + 512), R("dl"), R("du", 32, 64), R("e2"), A.add)
-            if t:
+
+        def right(k):
+            if k == 0:
+                gat("s", R("g1"), R("dl"), R("du", 32, 64))
+            if k == 1:
+                f2p("ps7", 0, 512, "c", [], (("nid", R("e2")), ("nid", R("g1"))))
+            if k == 2:
+                act(R("ew", S0 + n, S0 + n + 512), R("ps7"), -1.0)
+            if k == 2 and t:
                 dma("y", None, R("ew", S0 + n, GC), T.ye[:, n:GH], T.ew[:, S0 + n:GC])
+
         def border():
-            f2p("ps7", 160, 16, "c", [(zn, "gsn", 0)])
-            f2p("ps7", 176, 16, "i", [(zn, "gsn", 256)])
             ts(R("sw", 0, 16), R("ps7", 160, 176), 1.0, A.min)
             tt(R("sw", 16, 32), R("ps7", 176, 192), R("srf", 16, 32), A.mult)
             tt(R("ab"), R("ab"), R("sw", 0, 16), A.mult)
             tt(R("sn"), R("sn"), R("sw", 16, 32), A.max)
             tt(R("bt", 0, 16), R("bt", 0, 16), R("ab"), A.add)
+            slots(192)
             sendbases(1, "bt")
-            slots()
             ts(R("su"), R("sn"), float(S0), A.add)
-            act(R("mme", 0, 16), R("sn"), float(M))
         if t:
+            ts(R("xu"), R("ps7", 0, 32), float(M), A.min)
+            f2p("ps7", 192, 32, "i", [("zh", "eg", 0)])
             detlists()
-        child(0)
-        f2p("ps2", 0, m, "c", [(zn, "rn", blk(KL))])
-        childto(0)
-        child(1)
-        gat2(R("gn"), R("nb"), R("xu"), R("gq"), A.mult)
-        f2p("ps3", 0, m, "c", [(zn, "rn", blk(KR))], M8)
-        child(2)
-        f2p("ps7", 128, 32, "c", [("zG%d" % t, "gn", 0)])
-        f2p("ps4", 0, m, "c", [(zn, "rn", blk(KB))], M8)
+        else:
+            f2p("ps7", 160, 16, "c", [(zn, "gsn", 0)])
+            f2p("ps7", 176, 16, "i", [(zn, "gsn", 256)])
+            ts(R("xu"), R("ps7", 0, 32), float(M), A.min)
+            border()
+        renamed(0, KL, "zB", ())
+        if t:
+            gat("s", R("dg"), R("dl"), R("du", 0, 32))
+        gat("s", R("gn"), R("nb"), R("xu"))
+        if t == 0:
+            act(R("e2"), R("eg"), 0.5, 127.8)
+            f2p("ps7", 192, 32, "i", [("zh", "eg", 0)])
+        renamed(1, KR, "zE", M8)
+        unfold("gq", 0, 0, 32, 2, "ps0", 0, 2)
+        f2p("ps0", 32, 32, "c", [(zn, "gn", 0)])
+        renamed(2, KB, "zR", M8)
         q0, q1, q2 = (R("pre", 192 * k, 192 * k + m) for k in range(3))
         tt(q1, NS, q1, A.mult)
-        tt(q2, NS, PB, A.mult)
-        tt(E1, NS, R("eq", 0, m), A.mult)
-        tt(SP, SP, R("eq", 192, 192 + m), A.max)
-        tt(q1, NP, q1, A.add)
+        tt(E1, NS, EQ[0], A.mult)
         if t:
+            right(0)
+            right(1)
             children()
 
         def done(x, k):
             if t == 0:
-                halves(px, w * k, w * k + w, "hi", "lo", w * k)
-                for j, src in enumerate(("hi", "lo")):
-                    p2f("win", ROW[x] + j, S0, src, w * k, m)
-                    p2f("win", ROW[x] + j, S0 + n, src, w * k + m, 32)
+                halves("ps%d" % (2 + k), 256, 256 + (m if k < 2 else w), "hi", "lo", w * k, "v")
+                for tab, row in (((TLR[k], 6 * k), ("win", ROW[x])) if k < 2 else (("win", 0),)):
+                    for j, src in enumerate(("hi", "lo")):
+                        p2f(tab, row + j, S0, src, w * k, m, "sy"[j])
+                        if k == 2:
+                            p2f(tab, row + j, S0 + n, src, w * k + m, 32, "sy"[j])
             else:
                 y = {"l": T.yl, "r": T.yr, "b": T.yb}[x]
-                for a, b, c in ((0, n, 0), (n, GH, m)):
-                    src = R(px, w * k + c, w * k + c + (b - a) // 16)
-                    dma("y", None, src, y[:, a:b], ap(src))
+                for a, b, src in ((0, n, new(k)), (n, GH, new(k, m, w))):
+                    dma("s" if a else "y", None, src, y[:, a:b], ap(src))
         NL, NRm, NBm = R("ps2", 0, m), R("ps3", 0, m), R("ps4", 0, m)
         tt(PL, NL, PL, A.max)
+        childto(0)
+        tt(q1, NP, q1, A.add)
         tt(q0, NS, PL, A.mult)
         tt(E1, E1, PL, A.mult)
-        tt(SP, SP, PL, A.mult)
-        tt(PL, N0, q0, A.add)
+        tt(new(0), N0, q0, A.add)
         tt(q1, E1, q1, A.max)
-        tt(q2, SP, q2, A.max)
+        tt(SP, SP, EQ[1], A.max)
         done("l", 0)
+        if t == 0:
+            detlists()
+            act(R("tq"), R("ps0", 0, 32), -1.0)
+            gat("s", R("dg"), R("dl"), R("du", 0, 32))
+        tt(E1, NRm, EQ[2], A.mult)
+        tt(new(1), NRm, q1, A.max)
         childto(1)
-        tt(PR, NRm, q1, A.max)
-        tt(E1, NRm, R("eq", 384, 384 + m), A.mult)
+        tt(q2, NS, PB, A.mult)
+        tt(SP, SP, PL, A.mult)
         done("r", 1)
-        childto(2)
+        if t == 0:
+            right(0)
+            right(1)
+        else:
+            act(R("tq"), R("ps0", 0, 32), -1.0)
+            right(2)
         tt(q2, E1, q2, A.max)
-        BN = R(px, 2 * w + m, 3 * w)
-        tt(BN, R("ps7", 128, 160), BN, A.max)
-        tt(PB, NBm, q2, A.max)
+        tt(q2, SP, q2, A.max)
+        tt(new(2, m, w), R("ps0", 32, 64), R("tq"), A.max)
+        tt(new(2), NBm, q2, A.max)
         done("b", 2)
         if t == 0:
-            border()
-            detlists()
-            gat("s", R("gs", 0, 256), R("win", 0, GC), R("su"))
+            for tab in TLR:
+                e = S0 + 16 * w
+                gat("s", R(tab, e, e + 256), R(tab, 0, e), R("su"))
             children()
+            right(2)
     finish()

@@ -9,25 +9,22 @@ KB, KR, KL = 4352.0, 10368.0, 14336.0
 ZB = 6528
 TLR = ("w1", "uw")
 RN0 = 3840
-DA = (768, 1024)
-CC = (3, 3)
-PCK = (2, 2)
-G3 = ((70, 140), (80, 140))
-C2 = ((20, 60, 110), (24, 72, 132))
-HL = 24
+DA = (896, 1152)
+CUT = ((30, 66), (36, 76))
+G3 = ((50, 90), (60, 90))
 ZN = ["zz", "zB", "zR", "zL", "zE", "zB16", "zR16", "zL16", "zT16", "zMB", "zN0", "zN1", "zX", "zh", "q1", "q16", "d1", "d16", "d256"]
 _bf = {"win": M, "ew": M + 16, "w1": M + 16, "uw": M + 16, "zab": 14352, "gl": 3328, "gr": 3328, "gb": 3072, "tr": 3072,
-       "hb": 3072, "eo": 1024, "ta": 1024, "nb": M + 16, "dr": 2048, "dh": 2064, "dl": 2064, "msk": 2304, "nc0": 512, "nc1": 512,
+       "hb": 3072, "eo": 1280, "ta": 1280, "nb": M + 16, "dr": 2048, "dh": 2064, "dl": 2064, "msk": 2304, "nc0": 512, "nc1": 512,
        "it": 3072, "z": 144 * len(ZN), "z0": 432, "bo": 128, "ltm": 128, "nid": 128, "snf": 416, "krow": 256, "dm": 256,
-       "hi": 576, "lo": 576, "meh": 208, "mel": 208, "nim": 128, "mh": 640, "ml": 224, "gs": 512, "x0": 256, "x1": 256, "x2": 256, "xa": 256, "gi": 256,
+       "hi": 576, "lo": 576, "meh": 16, "mel": 16, "mh": 640, "ml": 224, "gs": 512, "x0": 256, "x1": 256, "x2": 256, "xa": 256, "gi": 256,
        "hot": 192, "m0": 256, "m1": 256, "m2": 256, "g1": 512, "gq": 512, "eg": 512, "gn": 512, "gsn": 512, "e2": 512, "dg": 512,
        "ek": 224, "kh": 224, "tgh": 224, "tgl": 224, "m8": 224}
-_f32 = {"px0": 480, "px1": 576, "po": 672, "me": 192, "me16": 192, "idf": 128, "lm": 208, "rm": 208, "gt": 192, "thr": 192,
+_f32 = {"px0": 480, "px1": 576, "po": 672, "me": 192, "me16": 192, "idf": 128, "mme": 208, "lm": 208, "rm": 208, "gt": 192, "thr": 192,
         "cb": 224, "cw1": 224, "cw2": 200, "cs": 16, "tg": 256, "eq": 672, "pre": 672,
         "ci": 16, "mk": 16, "mk2": 8, "zc": 24, "cc": 224, "sn": 16, "xs": 32, "bt": 80, "srf": 32, "ab": 16,
         "sw": 32, "kj": 32, "jj": 32, "nj": 64, "dj": 32, "inv": 64, "aj": 32, "pk": 64, "tq": 32, "dq": 64}
 _i32 = {"xin": 480, "sin": 32, "wti": 2, "pid": 4, "di": 64, "da": 64}
-_u16 = {"lv": 208, "rv": 208, "bv": 192, "lw": 208, "rw": 208, "sa": 32, "su": 16, "bes": 16, "bel0": 16, "bel1": 16,
+_u16 = {"lv": 208, "rv": 208, "bv": 192, "lw": 208, "rw": 208, "sa": 32, "sb": 32, "su": 16, "bes": 16, "bel0": 16, "bel1": 16,
         "l1": 16, "l2": 16, "td": 32, "tu": 32, "ru": 32, "xu": 32, "du": 64}
 SCRATCH, AL, _o = {}, {}, 0
 for _k in list(_f32):
@@ -198,6 +195,9 @@ def rank_program(g, core, T, topo):
     def zero(n, a, b):
         iof(n, a, b, [[0, b - a]], 0)
 
+    def gcp(out, a, n):
+        op("g", [a], [out], [lambda e: e.affine_select(ap(out), ap(a), [[0, n]], A.is_ge, 0.0, 0, 0)])
+
     def ZR(z):
         return R("z", 144 * ZN.index(z), 144 * ZN.index(z) + 144)
 
@@ -342,16 +342,13 @@ def rank_program(g, core, T, topo):
     cp(R("sn"), R("sin", 16, 32))
     ts(R("snf"), R("win", M - 416, M), 0.0, A.mult, R("ci", 7, 8), A.add)
 
-    def numbers(a, b):
-        ts(R("meh", a, b), R("cc", a, b), 16.0, A.mult)
-        ts(R("mel", a, b), R("cc", a, b), 0.0, A.mult, I1, A.add)
-
-    def slots(c):
-        halves("sn", 0, 16, "meh", "mel", c, "v")
+    def slots(t):
+        halves("sn", 0, 16, "meh", "mel", 0, "v")
         for k, src in enumerate(("meh", "mel")):
             for s in range(2):
-                p2f("snf", k, 16 + 144 * s, src, c + 8 * s, 8)
-    slots(160)
+                p2f("snf", k, 16 + 144 * s, src, 8 * s, 8)
+        act(R("mme", 160 + 32 * t, 176 + 32 * t), R("sn"), float(M), -float(S0 * t))
+    slots(0)
     load("y", R("wti", 0, 1), T.wt[:, :])
     load("y", R("wti", 1, 2), T.th[:, :])
     load("y", R("eo", 0, DA[0]), T.err[:, P0 - DA[0]:P0])
@@ -359,7 +356,9 @@ def rank_program(g, core, T, topo):
     tt(R("zc", 8, 9), R("mk", 14, 15), R("mk", 15, 16), A.subtract)
     ts(R("zc", 8, 9), R("mk2", 0, 1), float(M), A.mult, R("zc", 8, 9), A.add)
     ts(R("gi"), R("gi"), R("mk", 14, 15), A.mult)
-    numbers(0, 160)
+    ts(R("mme", 0, 160), R("me", 0, 160), float(M), A.mult)
+    for z, k in (("zL", 2), ("zR", 1), ("zB", 0), ("zE", 3), ("zN0", 5), ("zN1", 6)):
+        ts(ZR(z), Z1, R("mk2", k, k + 1), A.mult)
 
     def early(k):
         if k == 0:
@@ -369,7 +368,6 @@ def rank_program(g, core, T, topo):
             for j, (a, b) in enumerate(((0, 160), (160, 352), (352, 576), (576, 640))):
                 act(R("mh", a, b), R("cc", 0, b - a), 0.0, R("ci", 11 + j, 12 + j), F.Identity)
             iof("msk", 0, 2304, [[0, 768], [256, 3]], 0)
-            ts(R("nim"), R("idf"), -float(M), A.mult)
             ts(R("nid"), R("idf"), -1.0, A.mult)
         if k == 1:
             fill(R("ew", S0 + P0, GC), 0.0)
@@ -389,8 +387,6 @@ def rank_program(g, core, T, topo):
 
     def later(k):
         if k == 0:
-            for z, k in (("zL", 2), ("zR", 1), ("zB", 0), ("zE", 3), ("zN0", 5), ("zN1", 6)):
-                zmat(z, R("mk2", k, k + 1))
             act(R("kj"), R("cc", 0, 32), 8.0, I2, F.Identity)
             act(R("xs", 0, 16), R("me", 0, 16), 1.0, float(GC))
             act(R("xs", 16, 32), R("xs", 16, 32), 1.0, R("ci", 5, 6), F.Identity)
@@ -431,7 +427,7 @@ def rank_program(g, core, T, topo):
         px = "px%d" % t
         PL, PR, PB = R(px, 0, m), R(px, m, 2 * m), R(px, 2 * m, 3 * m)
         ca = m - d // 16
-        cut = [ca * k // 3 // 2 * 2 for k in range(3)] + [ca]
+        cut = [0, CUT[t][0], CUT[t][1], ca]
         CH = [(cut[2], ca), (0, cut[1]), (cut[1], cut[2])]
         PC = [(cut[2], m + 16), (0, cut[2])]
         EW, W1, UW = R("ew"), R("w1"), R("uw")
@@ -444,16 +440,16 @@ def rank_program(g, core, T, topo):
             return R(buf, S0 + 16 * a, S0 + 16 * b)
 
         def own(k):
-            o, x = sl("za", *CH[k], 2), col("ew", *CH[k])
-            op("g", [x], [o], [lambda e: e.affine_select(ap(o), ap(x), [[0, x[2] - x[1]]], A.is_ge, 0.0, 0, 0)])
+            gcp(sl("za", *CH[k], 2), col("ew", *CH[k]), 16 * (CH[k][1] - CH[k][0]))
         if t == 0:
             gat("s", R("gs", 0, 256), R("win", 0, S0 + n), R("sa", 0, 16))
             gat("s", R("win", S0 + n, S0 + n + 256), R("win", 0, S0 + n), R("su"))
             f2p("ps3", 0, 16, "c", [("zB16", "gs", 0)])
             sendbases(0, "ps3")
             cp(R("bt", 0, 16), R("ps3", 0, 16))
-            cp(sl("za", 0, ca, 2), col("ew", 0, ca))
             early(0)
+            for k in range(3):
+                own(k)
             later(0)
         for k, (a, b) in enumerate(PC):
             for j in range(2):
@@ -474,18 +470,15 @@ def rank_program(g, core, T, topo):
         def lists(k, j):
             (a, b), x, ps = PC[k], "lr"[j], "ps%d" % (2 * k + j)
             ts(R(x + "v", a, b), R(ps, 0, b - a), float(S0 * t), A.add)
-            act(R(x + "m", a, b), R(ps, 0, b - a), 1.0, float(S0 * t))
-            f2p(VB[2 * k + j], 0, b - a, "i", [], (("nim", R("meh", a, b)), ("nim", R("mel", a, b)), ("idf", R(x + "m", a, b))), last=False)
+            tt(R(x + "m", a, b), R(ps, 0, b - a), R("mme", a, b), A.subtract)
+            f2p(VB[2 * k + j], 0, b - a, "i", [], (("idf", R(x + "m", a, b)),), last=False)
         if t:
             ghosts()
-        for k in range(2):
-            for j in range(2):
-                if t == 0 or k == 0:
-                    lists(k, j)
-            if t == 0:
-                early(1 + k)
+        lists(0, 0)
         if t == 0:
-            zero("nb", 0, 1536)
+            early(1)
+            lists(0, 1)
+            early(2)
             ghosts()
 
         def legs(k, x):
@@ -494,9 +487,13 @@ def rank_program(g, core, T, topo):
             f2p(ps, 0, b - a, "i", [("zMB", "g" + x, 16 * a)], first=False)
             ts(R(x + "w", a, b), R(ps, 0, b - a), float(M), A.min)
         for k, (a, b) in enumerate(PC):
-            gat("v", R("gl", 16 * a, 16 * b), WIN, R("lv", a, b))
-            gat("s", R("gr", 16 * a, 16 * b), WIN, R("rv", a, b))
             if k == 0 and t:
+                gat("v", R("gl", 16 * a, 16 * a + 384), WIN, R("lv", a, a + 24))
+                lists(0, 1)
+            c = a + 24 * (k == 0 and t)
+            gat("v", R("gl", 16 * c, 16 * b), WIN, R("lv", c, b))
+            gat("s", R("gr", 16 * a, 16 * b), WIN, R("rv", a, b))
+            if k == 0:
                 lists(1, 0)
                 lists(1, 1)
         legs(0, "l")
@@ -511,12 +508,16 @@ def rank_program(g, core, T, topo):
                     side(0)
                     gat2(R("ta", 0, d), win, L("lw", ca, m), own, A.max)
                     side(1)
-            gat2(col(dst, ca, m), win, L("rw", ca, m), R("ta", 0, d), A.max)
-            side(2)
             for k, (a, b) in enumerate(CH):
                 u, v = 48 * a, 48 * b
                 scan(R(out, u, v), R("msk", 0, v - u), R(slots_, u, v), A.min, A.max)
-                cp(col(dst, a, b), sl(out, a, b, 2))
+                if k < 2:
+                    gcp(col(dst, a, b), sl(out, a, b, 2), 16 * (b - a))
+                else:
+                    cp(col(dst, a, b), sl(out, a, b, 2))
+                if k == 0:
+                    gat2(col(dst, ca, m), win, L("rw", ca, m), R("ta", 0, d), A.max)
+                    side(2)
                 side(3 + k)
 
         arrived("x0", t, "ew", GC, 128)
@@ -524,8 +525,11 @@ def rank_program(g, core, T, topo):
         gat2(R("x1"), EW, XR, R("xa"), A.max)
         send("x1", t, "x1", "w1", GC, 128)
         if t == 0:
-            zero("nb", 1536, M + 16)
             load("y", R("dr"), T.det[:, :])
+            for x, a, b in (("nb", 0, M + 16), ("zab", ZB + 3 * (n - d), blk(KL) + 3072)):
+                for c in range(a, b, 1024):
+                    e = min(1024, b - c)
+                    copy(R(x, c, c + e), R("ew", S0 + P0, S0 + P0 + e))
         else:
             own(2)
 
@@ -553,30 +557,25 @@ def rank_program(g, core, T, topo):
                         unfold("win", ROW[x], S0, m, j, "ps%d" % j, 0)
                     elif j < 2:
                         f2p("ps3", 32 + 16 * j, 16, "c", [(("zL16", "zR16")[j], "gs", 0)])
+                    else:
+                        o = 144 * ZN.index("zB") + 15
+                        op("t", [R("snf"), ZR("zB")], [R("ps3")],
+                           [lambda e, i=i, c=16 + 144 * (i // 8) + i % 8: e.matmul(T.ps3[:, 64:80], T.z[:, o - i:o - i + 128], T.snf[:, c:c + 128:8], i == 0, i == 15)
+                            for i in range(16)])
         arrived("x1", t, "w1", GC, 128)
         gat("v", R("xa"), W1, XL)
         gat2(R("x2"), W1, XR, R("xa"), A.max)
         send("x2", t, "x2", "uw", GC, 128)
         if t == 0:
-            for x, a in (("cb", 1), ("cw1", 0), ("cw2", 0)):
-                iof(x, a, SCRATCH[x][1][1], [[0, SCRATCH[x][1][1] - a]], int(BIG))
-            zero("cb", 0, 1)
-            zero("inv", 0, 32)
             newrows(0)
-            zero("zab", ZB + 3 * (n - d), blk(KL) + 3072)
-            newrows(1)
-        c2 = (0,) + C2[t] + (m,)
+        c2 = list(range(0, m + 1, 32))
         for k, (a, b) in enumerate(zip(c2[:-1], c2[1:])):
             gat("s", R("tr", 16 * a, 16 * b), W1, L("rw", a, b))
             gat2(col("uw", a, b), W1, L("lw", a, b), R("tr", 16 * a, 16 * b), A.max)
-        if t:
-            for k in range(3):
-                act(R(px, m * k, m * k + m), R("ps%d" % k, 0, m), -1.0)
         bases(1)
         pl, pr, pb = (R("ps%d" % j, 0, m) for j in (4, 5, 6))
         ts(R("ek", 0, m), pr, 0.0, A.is_equal, KR, A.mult)
         ts(pl, pl, 0.0, A.is_equal, KL, A.mult)
-        ts(pb, pb, 0.0, A.is_equal, KB, A.mult)
         tt(R("kh", 0, m), pl, R("ek", 0, m), A.max)
         if t == 0:
             for k, (src, a, b) in enumerate((("mh", 352, 576), ("ml", 0, 0))):
@@ -585,15 +584,18 @@ def rank_program(g, core, T, topo):
                     p2f("win", row + k, S0 + P0, src, b, 64)
             ts(R("dm"), R("tg"), I1, A.is_le, BIG, A.mult)
             cp(R("bt", 32, 64), R("ps3", 32, 64))
+            cp(R("sb", 0, 32, 2), R("sa", 0, 16))
+            ts(R("sb", 1, 32, 2), R("ps3", 64, 80), float(S0), A.add)
             cp(R("bt", 64, 80), R("rv", m, m + 16))
-        tt(R("kh", 0, m), pb, R("kh", 0, m), A.max)
+        f2p("ps3", 0, g3[2], "i", [("zB", "gb", 0)])
         arrived("x2", t, "uw", GC, 128)
-        if t == 0:
-            newrows2(0)
 
         def side3(k):
             if k == 2:
                 copy(R("eo", 0, d), col("w1", ca, m))
+                ts(pb, pb, 0.0, A.is_equal, KB, A.mult)
+            if k == 3:
+                tt(R("kh", 0, m), pb, R("kh", 0, m), A.max)
             if t == 0 and k == 1:
                 tt(R("srf"), R("bt", 48, 80), R("xs"), A.is_equal)
                 tt(R("ab"), R("bt", 48, 64), R("bt", 32, 48), A.subtract)
@@ -607,29 +609,34 @@ def rank_program(g, core, T, topo):
         for row, src in ((8, "kh"), (10, "ek")):
             p2f("win", row, S0, src, 0, m)
         if t == 0:
+            newrows2(0)
+            for x, a in (("cb", 1), ("cw1", 0), ("cw2", 0)):
+                iof(x, a, SCRATCH[x][1][1], [[0, SCRATCH[x][1][1] - a]], int(BIG))
+            zero("cb", 0, 1)
+            zero("inv", 0, 32)
+        if t == 0:
             act(R("dh", 0, 2048), R("dr"), 0.5, 127.8)
-        f2p("ps3", 0, m, "i", [("zB", "gb", 0)])
+        else:
+            for k in range(3):
+                act(R(px, m * k, m * k + m), R("ps%d" % k, 0, m), -1.0)
+        f2p("ps3", g3[2], m - g3[2], "i", [("zB", "gb", 16 * g3[2])])
         HC = CH + [(ca, m)]
         for k, (a, b) in enumerate(HC):
             hb = R("hb", 16 * a, 16 * b)
             gat2(hb, R("w1", 0, GC), R("bv", a, b), sl("za", a, b, 2) if k < len(CH) else R("eo", 0, d), A.max)
-            if k == 0:
+            if k == 1:
                 tt(R("ps3", 0, m), R("ps3", 0, m), R("me", 0, m), A.is_equal)
             if k < len(HC) - 1:
                 act(hb, hb, 1.0, R("ci", 10, 11), F.Sign)
             else:
                 ts(hb, hb, R("ci", 9, 10), A.is_ge, 2.0, A.mult)
-            f2p(VB[k % 4], 0, b - a, "i", [("zz", "hb", 16 * a)])
-            if k == 1:
+            f2p("ps4" if k < 3 else "ps5", a, b - a, "i", [("zz", "hb", 16 * a)])
+            if k == 2:
                 tt(R("gt", 0, m), R("ps3", 0, m), R("gt", 0, m), A.mult)
                 act(R("thr", 0, ca), R("gt", 0, ca), -103.0, 99.0)
                 act(R("thr", ca, m), R("gt", ca, m), -87.0, 99.0)
-            if k >= 2:
-                u, v = HC[k - 2]
-                tt(R("hot", u, v), R(VB[(k - 2) % 4], 0, v - u), R("thr", u, v), A.is_ge)
-        for k in (len(HC) - 2, len(HC) - 1):
-            u, v = HC[k]
-            tt(R("hot", u, v), R(VB[k % 4], 0, v - u), R("thr", u, v), A.is_ge)
+        for ps, u, v in (("ps4", 0, ca), ("ps5", ca, m)):
+            tt(R("hot", u, v), R(ps, u, v), R("thr", u, v), A.is_ge)
         op("t", [R("bo"), R("hot", 0, m)], [R("ps1")], [lambda e: e.matmul(T.ps1[:, 0:m], T.bo[:, :], T.hot[:, 0:m], True, True)])
         op("t", [R("ltm"), R("hot", 0, m)], [R("ps0")], [lambda e: e.matmul(T.ps0[:, 0:m], T.ltm[:, :], T.hot[:, 0:m], True, True)])
         scan(R("cb", 1, m + 1), R("ps1", 0, m), R("msk", 0, 3 * m, 3), A.add, A.max)
@@ -652,19 +659,18 @@ def rank_program(g, core, T, topo):
         def pick(lst, ps):
             scan(R("pk"), R("dm", 0, 256, 4), R(ps, 0, 64), A.add, A.min)
             cp(R(lst), R("pk", 3, 64, 4))
+        ts(R("inv", 32, 64), R("kj"), R("cb", m, m + 1), A.is_ge)
         pick("l1", "ps2")
         gat2(R("m1"), R("cw1", 16, 224), R("l1"), R("krow"), A.is_le)
         f2p("ps3", 0, 64, "q", [("q1", "m1", 0)], first=False)
-        f2p("ps4", 0, 32, "d", [("d16", "m1", 0)], first=False, last=False)
         tt(R("cw2", 0, m), R("ps0", 0, m), R("cb", 0, m), A.add)
-        ts(R("inv", 32, 64), R("kj"), R("cb", m, m + 1), A.is_ge)
+        tt(R("aj"), R("inv", 32, 64), R("me", 0, 32), A.mult)
+        f2p("ps4", 0, 32, "d", [("d16", "m1", 0)], (("idf", R("aj")),), first=False, last=False)
         pick("l2", "ps3")
         gat2(R("m2"), R("cw2"), R("l2"), R("krow"), A.is_le)
         f2p("ps4", 0, 32, "d", [("d1", "m2", 0)], first=False)
-        tt(R("aj"), R("inv", 32, 64), R("me", 0, 32), A.mult)
         act(R("inv", 32, 64), R("inv", 32, 64), 4096.0)
-        tt(R("tq"), R("ps4", 0, 32), R("aj"), A.add)
-        ts(R("td"), R("tq"), float(S0), A.add)
+        ts(R("td"), R("ps4", 0, 32), float(S0), A.add)
         gat("s", R("g1"), WIN, R("td"))
         f2p("ps5", 0, 32, "i", [(("zE", "zB"), "g1", 0)])
         EQ = [R("eq", 192 * k, 192 * k + m) for k in range(3)]
@@ -672,7 +678,7 @@ def rank_program(g, core, T, topo):
         tt(EQ[1], PL, PB, A.is_equal)
         tt(EQ[2], PR, PB, A.is_equal)
         if t == 0:
-            numbers(160, 192)
+            act(R("mme", 0, 192), R("me"), float(M), -float(S0))
         ts(R("tu"), R("ps5", 0, 32), float(S0), A.add)
         nc, zn = R("nc%d" % t), "zN%d" % t
         gat("s", R("gq"), WIN, R("tu"))
@@ -683,15 +689,14 @@ def rank_program(g, core, T, topo):
         if t:
             act(R("e2"), R("eg"), 0.5, 127.8)
         else:
-            gat("s", R("gsn"), R("nb"), R("sa"))
+            gat("s", R("gsn"), R("nb"), R("sb"))
             for tab in TLR:
                 copy(R(tab, S0 + n, S0 + n + 512), R("gq"))
             for row, src in ((4, 0), (5, 1), (2, 6), (3, 7)):
                 copy(R("win", S0 + n, S0 + n + 512, 1, row), R("gq", 0, 512, 1, src))
         f2p("ps6", 0, 32, "i", [("zT16", "gq", 0)])
         f2p("ps0", 0, m, "c", [(("zB", "zR")[t], "nb", S0)])
-        f2p("ps7", 0, 32, "i", [("zX", "gq", 0)])
-        cp(R("nj", 0, 32), R("ps5", 0, 32))
+        act(R("nj", 0, 32), R("ps5", 0, 32))
         tt(R("tq"), R("ps6", 0, 32), R("dj"), A.max)
         ts(R("ru"), R("tq"), -float(RN0), A.add)
         sca(R("zab"), R("ru"), nc)
@@ -718,7 +723,7 @@ def rank_program(g, core, T, topo):
 
         def detlists():
             for k in range(2):
-                tt(R("di", 32 * k, 32 * k + 32), R("ps7", 192, 224), R("nj", 32 * k, 32 * k + 32), A.add)
+                tt(R("di", 32 * k, 32 * k + 32), R("ps5" if t else "ps7", 320, 352), R("nj", 32 * k, 32 * k + 32), A.add)
             ts(R("da"), R("di"), 2047, A.bitwise_and)
             tt(R("dq"), R("da"), R("inv"), A.add)
             ts(R("du"), R("dq"), 2048.0, A.min)
@@ -736,7 +741,7 @@ def rank_program(g, core, T, topo):
             if k == 2:
                 act(R("ew", S0 + n, S0 + n + 512), R("ps7"), -1.0)
             if k == 2 and t:
-                dma("y", None, R("ew", S0 + n, GC), T.ye[:, n:GH], T.ew[:, S0 + n:GC])
+                dma("s", None, R("ew", S0 + n, GC), T.ye[:, n:GH], T.ew[:, S0 + n:GC])
 
         def border():
             ts(R("sw", 0, 16), R("ps7", 160, 176), 1.0, A.min)
@@ -744,43 +749,45 @@ def rank_program(g, core, T, topo):
             tt(R("ab"), R("ab"), R("sw", 0, 16), A.mult)
             tt(R("sn"), R("sn"), R("sw", 16, 32), A.max)
             tt(R("bt", 0, 16), R("bt", 0, 16), R("ab"), A.add)
-            slots(192)
+            slots(1)
             sendbases(1, "bt")
+            newrows(1)
             ts(R("su"), R("sn"), float(S0), A.add)
         if t:
-            ts(R("xu"), R("ps7", 0, 32), float(M), A.min)
-            f2p("ps7", 192, 32, "i", [("zh", "eg", 0)])
+            f2p("ps5", 320, 32, "i", [("zh", "eg", 0)])
             detlists()
         else:
-            f2p("ps7", 160, 16, "c", [(zn, "gsn", 0)])
-            f2p("ps7", 176, 16, "i", [(zn, "gsn", 256)])
-            ts(R("xu"), R("ps7", 0, 32), float(M), A.min)
+            f2p("ps7", 160, 32, "c", [(zn, "gsn", 0)])
             border()
         renamed(0, KL, "zB", ())
+        f2p("ps0", 64, 32, "i", [("zX", "gq", 0)])
         if t:
             gat("s", R("dg"), R("dl"), R("du", 0, 32))
-        gat("s", R("gn"), R("nb"), R("xu"))
-        if t == 0:
+            right(0)
+        else:
             act(R("e2"), R("eg"), 0.5, 127.8)
-            f2p("ps7", 192, 32, "i", [("zh", "eg", 0)])
+            f2p("ps7", 320, 32, "i", [("zh", "eg", 0)])
         renamed(1, KR, "zE", M8)
-        unfold("gq", 0, 0, 32, 2, "ps0", 0, 2)
-        f2p("ps0", 32, 32, "c", [(zn, "gn", 0)])
-        renamed(2, KB, "zR", M8)
         q0, q1, q2 = (R("pre", 192 * k, 192 * k + m) for k in range(3))
         tt(q1, NS, q1, A.mult)
         tt(E1, NS, EQ[0], A.mult)
-        if t:
-            right(0)
-            right(1)
-            children()
+
+        def lastbase(k):
+            if k == 0:
+                return ts(R("xu"), R("ps0", 64, 96), float(M), A.min)
+            gat("s", R("gn"), R("nb"), R("xu"))
+            if t:
+                right(1)
+            unfold("gq", 0, 0, 32, 2, "ps0", 0, 2)
+            f2p("ps0", 32, 32, "c", [(zn, "gn", 0)])
+            renamed(2, KB, "zR", M8)
 
         def done(x, k):
             if t == 0:
-                halves("ps%d" % (2 + k), 256, 256 + (m if k < 2 else w), "hi", "lo", w * k, "v")
+                halves("ps%d" % (2 + k), 256, 256 + (m if k < 2 else w), "hi", "lo", w * k, "svv"[k])
                 for tab, row in (((TLR[k], 6 * k), ("win", ROW[x])) if k < 2 else (("win", 0),)):
                     for j, src in enumerate(("hi", "lo")):
-                        p2f(tab, row + j, S0, src, w * k, m, "sy"[j])
+                        p2f(tab, row + j, S0, src, w * k, m, "sy"[j] if k < 2 else "y")
                         if k == 2:
                             p2f(tab, row + j, S0 + n, src, w * k + m, 32, "sy"[j])
             else:
@@ -791,28 +798,36 @@ def rank_program(g, core, T, topo):
         tt(PL, NL, PL, A.max)
         childto(0)
         tt(q1, NP, q1, A.add)
+        if t:
+            lastbase(0)
+            lastbase(1)
+        if t:
+            children()
+            right(2)
         tt(q0, NS, PL, A.mult)
         tt(E1, E1, PL, A.mult)
         tt(new(0), N0, q0, A.add)
         tt(q1, E1, q1, A.max)
         tt(SP, SP, EQ[1], A.max)
+        if t == 0:
+            lastbase(0)
         done("l", 0)
         if t == 0:
+            lastbase(1)
             detlists()
-            act(R("tq"), R("ps0", 0, 32), -1.0)
             gat("s", R("dg"), R("dl"), R("du", 0, 32))
+            act(R("tq"), R("ps0", 0, 32), -1.0)
         tt(E1, NRm, EQ[2], A.mult)
         tt(new(1), NRm, q1, A.max)
         childto(1)
+        if t:
+            act(R("tq"), R("ps0", 0, 32), -1.0)
         tt(q2, NS, PB, A.mult)
         tt(SP, SP, PL, A.mult)
         done("r", 1)
         if t == 0:
             right(0)
             right(1)
-        else:
-            act(R("tq"), R("ps0", 0, 32), -1.0)
-            right(2)
         tt(q2, E1, q2, A.max)
         tt(q2, SP, q2, A.max)
         tt(new(2, m, w), R("ps0", 32, 64), R("tq"), A.max)

from concourse.bass import DstId, RemoteDMATransfer
from concourse.mybir import AluOpType as A, ActivationFunctionType as F

NR, P0, GH = 8, 2560, 3584
S0 = 16
GC, M = GH + S0, 3856
BIG = 16384.0
KB, KR, KL = 4352.0, 10368.0, 14336.0
ZB = 6528
TLR = ("w1", "uw")
RN0 = 3840
DA = (896, 1152)
CUT = ((30, 66), (36, 76))
G3 = ((50, 90), (60, 90))
ZN = ["zz", "zB", "zR", "zL", "zE", "zB16", "zR16", "zL16", "zT16", "zMB", "zN0", "zN1", "zX", "zh", "q1", "q16", "d1", "d16", "d256"]
_bf = {"win": M, "ew": M + 16, "w1": M + 16, "uw": M + 16, "zab": 14352, "gl": 3328, "gr": 3328, "gb": 3072, "tr": 3072,
       "hb": 3072, "eo": 1280, "ta": 1280, "nb": M + 16, "dr": 2048, "dh": 2064, "dl": 2064, "msk": 2304, "nc0": 512, "nc1": 512,
       "it": 3072, "z": 144 * len(ZN), "z0": 432, "bo": 128, "ltm": 128, "nid": 128, "snf": 416, "krow": 256, "dm": 256,
       "hi": 576, "lo": 576, "meh": 16, "mel": 16, "mh": 640, "ml": 224, "gs": 512, "x0": 256, "x1": 256, "x2": 256, "xa": 256, "gi": 256,
       "hot": 192, "m0": 256, "m1": 256, "m2": 256, "g1": 512, "gq": 512, "eg": 512, "gn": 512, "gsn": 512, "e2": 512, "dg": 512,
       "ek": 224, "kh": 224, "tgh": 224, "tgl": 224, "m8": 224}
_f32 = {"px0": 480, "px1": 576, "po": 672, "me": 192, "me16": 192, "idf": 128, "mme": 208, "lm": 208, "rm": 208, "gt": 192, "thr": 192,
        "cb": 224, "cw1": 224, "cw2": 200, "cs": 16, "tg": 256, "eq": 672, "pre": 672,
        "ci": 16, "mk": 16, "mk2": 8, "zc": 24, "cc": 224, "sn": 16, "xs": 32, "bt": 80, "srf": 32, "ab": 16,
        "sw": 32, "kj": 32, "jj": 32, "nj": 64, "dj": 32, "inv": 64, "aj": 32, "pk": 64, "tq": 32, "dq": 64}
_i32 = {"xin": 480, "sin": 32, "wti": 2, "pid": 4, "di": 64, "da": 64}
_u16 = {"lv": 208, "rv": 208, "bv": 192, "lw": 208, "rw": 208, "sa": 32, "sb": 32, "su": 16, "bes": 16, "bel0": 16, "bel1": 16,
        "l1": 16, "l2": 16, "td": 32, "tu": 32, "ru": 32, "xu": 32, "du": 64}
SCRATCH, AL, _o = {}, {}, 0
for _k in list(_f32):
    if _f32[_k] <= 80 and _k != "xs":
        AL[_k] = (_o, _f32[_k])
        _o += (_f32.pop(_k) + 7) // 8 * 8
_f32["pf"] = _o
for _s, _d in ((_bf, "bfloat16"), (_f32, "float32"), (_i32, "int32"), (_u16, "uint16")):
    for _k in _s:
        SCRATCH[_k] = ("sbuf", [128, _s[_k]], _d)
for _k in range(8):
    SCRATCH["ps%d" % _k] = ("psum", [128, 512], "float32")
_KINDS = ["be", "x0", "x1", "x2"]
NDMA = 110
SEMAPHORES = ["qv", "qs", "qt", "qg"] + ["a%s%d" % (k, t) for k in _KINDS for t in range(2)] + \
             ["l%s%d" % (k, t) for k in _KINDS for t in range(2)] + ["d%d" % k for k in range(NDMA)]


def tracker(g, T):
    Q = {"v": g.vector, "s": g.scalar, "t": g.tensor, "g": g, "y": g.sync}
    acc, known, snap, cnt, top = {}, {q: {} for q in Q}, {}, {q: 0 for q in Q}, {}
    nd = [0]

    def hit(x, y):
        if x[1] >= y[2] or y[1] >= x[2]:
            return False
        if x[3] > 1 and x[3] == y[3] and (x[1] - y[1]) % x[3]:
            return False
        return x[4] is None or y[4] is None or x[4] == y[4]

    def wait(q, sem, val):
        if known[q].get(sem, 0) >= val:
            return
        Q[q].wait_ge(T.sem[sem], val)
        for s, v in snap.get((sem, val), {}).items():
            if known[q].get(s, 0) < v:
                known[q][s] = v
        known[q][sem] = val

    def deps(q, reads, writes):
        need = {}
        for wr, refs in ((False, reads), (True, writes)):
            for r in refs:
                ps = r[0][:2] == "ps"
                for (x, k, tok) in acc.get(r[0], []):
                    if ps:
                        if tok[2] == q and (q == "t" or not (k or wr) or not hit(r, x)):
                            continue
                    elif not (k or wr) or not hit(r, x) or (q == "t" and tok[2] == q):
                        continue
                    need[tok[0]] = max(need.get(tok[0], 0), tok[1])
        for sem, val in sorted(need.items(), key=lambda z: (z[0][0] == "q", -z[1])):
            wait(q, sem, val)

    def note(q, reads, writes, tok):
        for wr, refs in ((False, reads), (True, writes)):
            for r in refs:
                old = acc.get(r[0], [])
                if wr:
                    old = [o for o in old if not (r[3] == 1 and r[1] <= o[0][1] and o[0][2] <= r[2] and (r[4] is None or r[4] == o[0][4]))]
                else:
                    old = [o for o in old if not (not o[1] and o[0] == r and o[2][2] == tok[2] and not tok[3] and not o[2][3])]
                acc[r[0]] = old + [(r, wr, tok)]

    def op(q, reads, writes, fns):
        deps(q, reads, writes)
        for f in fns[:-1]:
            f(Q[q])
        cnt[q] += 1
        sem = "q" + q
        fns[-1](Q[q]).then_inc(T.sem[sem], 1)
        top[sem] = cnt[q]
        s = dict(known[q]); s[sem] = cnt[q]
        snap[(sem, cnt[q])] = s
        note(q, reads, writes, (sem, cnt[q], q, False))

    def dma(q, out, in_, oap, iap, after=()):
        rd, wr = ([in_] if in_ else []), ([out] if out else [])
        deps(q, rd + list(after), wr)
        sem = "d%d" % nd[0]; nd[0] += 1
        Q[q].dma_start(out=oap, in_=iap).then_inc(T.sem[sem], 16)
        top[sem] = 16
        snap[(sem, 16)] = dict(known[q])
        note(q, rd, wr, (sem, 16, q, True))

    def remote(src, lsem, lval, call):
        deps("g", [src], [])
        call()
        top[lsem] = lval
        note("g", [src], [], (lsem, lval, "g", True))

    def land(refs, sem, val):
        top[sem] = val
        for r in refs:
            acc[r[0]] = [o for o in acc.get(r[0], []) if not hit(r, o[0])] + [(r, True, (sem, val, "-", True))]

    def finish():
        for sem, val in sorted(top.items()):
            wait("g", sem, val)
    return op, dma, remote, land, finish


def rank_program(g, core, T, topo):
    rank = T.rank_of(core)
    if rank is None:
        return
    op, dma, remote, land, finish = tracker(g, T)

    def R(n, a=0, b=None, step=1, row=None):
        if n in AL:
            o, w = AL[n]
            return ("pf", o + a, o + (w if b is None else b), step, row)
        if n in ("za", "zb"):
            return ("zab", a + ZB * (n == "zb"), b + ZB * (n == "zb"), step, row)
        return (n, a, (SCRATCH[n][1][1] if b is None else b), step, row)

    def ap(r):
        if r[4] is not None:
            return T[r[0]][r[4]::16, r[1]:r[2]]
        return T[r[0]][:, r[1]:r[2]] if r[3] == 1 else T[r[0]][:, r[1]:r[2]:r[3]]

    def ts(out, a, s1, o1, s2=None, o2=None):
        rd = [a] + [s for s in (s1, s2) if isinstance(s, tuple)]
        f1 = ap(s1) if isinstance(s1, tuple) else s1
        f2 = ap(s2) if isinstance(s2, tuple) else s2
        if o2 is None:
            op("v", rd, [out], [lambda e: e.tensor_scalar(out=ap(out), in0=ap(a), scalar1=f1, scalar2=None, op0=o1)])
        else:
            op("v", rd, [out], [lambda e: e.tensor_scalar(out=ap(out), in0=ap(a), scalar1=f1, scalar2=f2, op0=o1, op1=o2)])

    def tt(out, a, b, o):
        op("v", [a, b], [out], [lambda e: e.tensor_tensor(out=ap(out), in0=ap(a), in1=ap(b), op=o)])

    def cp(out, a):
        op("v", [a], [out], [lambda e: e.tensor_copy(out=ap(out), in_=ap(a))])

    def act(out, a, scale=1.0, bias=0.0, func=F.Copy):
        rd = [a] + [s for s in (scale, bias) if isinstance(s, tuple)]
        sc = ap(scale) if isinstance(scale, tuple) else scale
        bi = ap(bias) if isinstance(bias, tuple) else bias
        op("s", rd, [out], [lambda e: e.activation(out=ap(out), in_=ap(a), func=func, bias=bi, scale=sc)])

    def fill(r, c):
        op("v", [], [r], [lambda e: e.memset(ap(r), c)])

    def scan(out, d0, d1, o0, o1):
        op("v", [d0, d1], [out], [lambda e: e.tensor_tensor_scan(ap(out), ap(d0), ap(d1), 0.0, o0, o1)])

    def gat(q, out, win, off):
        if q == "v":
            op("v", [win, off], [out], [lambda e: e.tensor_copy(out=ap(out), in_=ap(win).indirect(ap(off)))])
        else:
            op("s", [win, off], [out], [lambda e: e.activation(out=ap(out), in_=ap(win).indirect(ap(off)), func=F.Copy)])

    def gat2(out, win, off, b, o):
        op("v", [win, off, b], [out], [lambda e: e.tensor_tensor(out=ap(out), in0=ap(win).indirect(ap(off)), in1=ap(b), op=o)])

    def sca(win, off, a):
        op("v", [a, off], [win], [lambda e: e.tensor_copy(out=ap(win).indirect(ap(off)), in_=ap(a))])

    def sca2(win, off, a, b):
        op("v", [a, b, off], [win], [lambda e: e.tensor_tensor(out=ap(win).indirect(ap(off)), in0=ap(a), in1=ap(b), op=A.add)])

    def iof(n, a, b, pat, base, step=1):
        r = R(n, a, b, step)
        op("g", [], [r], [lambda e: e.iota(ap(r), pat, base, 0, allow_small_or_imprecise_dtypes=True)])

    def zero(n, a, b):
        iof(n, a, b, [[0, b - a]], 0)

    def gcp(out, a, n):
        op("g", [a], [out], [lambda e: e.affine_select(ap(out), ap(a), [[0, n]], A.is_ge, 0.0, 0, 0)])

    def ZR(z):
        return R("z", 144 * ZN.index(z), 144 * ZN.index(z) + 144)

    def f2p(ps, c0, n, mode, terms, minus=(), first=True, last=True):
        mm, rd = [], []
        for z, src, a0, *lim in terms:
            k = {"d": 8, "q": 4}.get(mode, 16)
            lo, hi = lim or (0, k * n)
            rd.append(R(src, a0, a0 + hi - lo))
            for i in range(k):
                zi = z[i % 2] if isinstance(z, tuple) else z
                o = 144 * ZN.index(zi) + 15 - (2 * i if mode == "d" else i)
                rd.append(ZR(zi))
                a, b = max(lo, n * i), min(hi, n * i + n)
                if mode != "c":
                    mm.append((T.z[:, o:o + 128], T[src][:, a0 + i:a0 + k * n:k], 0, n))
                elif a < b:
                    mm.append((T.z[:, o:o + 128], T[src][:, a0 + a - lo:a0 + b - lo], a - n * i, b - n * i))
        for z, r, *c in minus:
            rd += [r, R(z)]
            mm.append((T[z][:, :], ap(r)) + (tuple(c) or (0, n)))
        full = [x for x in mm if x[3] - x[2] == n]
        mm = full[:1] + [x for x in mm if x[3] - x[2] < n] + full[1:]
        op("t", rd, [R(ps)], [lambda e, k=k, x=x: e.matmul(T[ps][:, c0 + x[2]:c0 + x[3]], x[0], x[1], first and k == 0, last and k == len(mm) - 1)
                              for k, x in enumerate(mm)])

    def p2f(tab, row, col, src, c0, n, q="y"):
        out = R(tab, col, col + 16 * n, 1, row)
        dma(q, out, R(src, c0, c0 + n), ap(out), T[src][:, c0:c0 + n])

    def copy(out, a, q="y"):
        dma(q, out, a, ap(out), ap(a))

    def unfold(tab, row, col, n, k, ps, c0, part=3):
        h, l = R("hi", 192 * k, 192 * k + n), R("lo", 192 * k, 192 * k + n)
        if part & 1:
            copy(h, R(tab, col, col + 16 * n, 1, row))
            copy(l, R(tab, col, col + 16 * n, 1, row + 1))
        if part & 2:
            f2p(ps, c0, n, "c", [], (("nid", h), ("nid", l)))

    def halves(src, a, b, h, l, ha, q="s"):
        if q == "s":
            act(R(h, ha, ha + b - a), R(src, a, b))
        else:
            cp(R(h, ha, ha + b - a), R(src, a, b))
        tt(R(l, ha, ha + b - a), R(src, a, b), R(h, ha, ha + b - a), A.subtract)

    def route(c):
        r = T.rank_of(c)
        nb = [T.cores[(r - 1) % NR], T.cores[(r + 1) % NR]]
        e = [topo.engines(c, d) for d in nb]
        first = 0 if len(e[0]) <= len(e[1]) else 1
        for k in (8, 4, 2, 1):
            x = e[first][:k]
            y = [z for z in e[1 - first] if z not in x][-k:]
            if len(x) == k and len(y) == k:
                return nb, ([x, y] if first == 0 else [y, x]), k

    nbr, eng, kk = route(core)
    arrive = route(nbr[0])[2] + route(nbr[1])[2]

    def send(kind, t, src, dst, d0, w):
        tr = []
        for s in range(2):
            rid, pid, _se = topo.addr(nbr[s])
            tr.append(RemoteDMATransfer(dst_ids=[DstId(rid=rid, pnc=pid)], dma_engine_mask=sum(1 << z for z in eng[s]),
                                        remote_sem=T.sem["a%s%d" % (kind, t)], src=T[src][:, s * w:s * w + w],
                                        dst=T[dst][:, d0 + (1 - s) * w:d0 + (2 - s) * w]))
        ls = "l%s%d" % (kind, t)
        remote(R(src), ls, 2 * kk, lambda: g.remote_dma_fused(tr, local_sem=T.sem[ls]))

    def arrived(kind, t, dst, d0, w):
        land([R(dst, d0, d0 + 2 * w)], "a%s%d" % (kind, t), arrive)

    def sendbases(t, src):
        ts(R("bes", 0, 8), R(src, 0, 8), -3440.0, A.add, 144.0, A.max)
        ts(R("bes", 8, 16), R(src, 8, 16), -3712.0, A.add)
        send("be", t, "bes", "bel%d" % t, 0, 8)

    def load(q, out, src):
        dma(q, out, None, ap(out), src)
    load("y", R("xin", 320, 480), T.bs[:, :])
    load("s", R("xin", 0, 160), T.lt[:, :])
    load("y", R("xin", 160, 320), T.rt[:, :])
    for s in range(2):
        load("s", R("sin", 16 + 8 * s, 24 + 8 * s), T.snd[:, 128 * s:128 * s + 128])
    load("y", R("sin", 0, 16), T.snd[:, :])
    load("y", R("ew", S0, S0 + P0), T.err[:, :])

    op("g", [], [R("pid", 0, 1)], [lambda e: e.iota(T.pid[:, 0:1], [[1, 1]], 0, 1)])
    fill(R("bo"), 1.0)
    iof("cc", 0, 224, [[1, 224]], 0)
    fill(R("win", 0, S0 + P0), 0.25)
    act(R("win", S0 + P0, M), R("win", 0, M - S0 - P0))
    op("g", [R("bo")], [R("bo")], [lambda e: e.affine_select(T.bo[:, :], T.bo[:, :], [[-16, 8], [0, 16]], A.is_ge, 0.0, 0, 1)])
    op("g", [R("bo")], [R("bo")], [lambda e: e.affine_select(T.bo[:, :], T.bo[:, :], [[16, 8], [0, 16]], A.is_ge, 0.0, 15, -1)])
    iof("gi", 0, 256, [[0, 2], [-7, 16], [15, 8]], 0)
    iof("xs", 16, 32, [[128, 2], [1, 8]], S0)
    fill(R("idf"), 1.0)
    op("g", [R("idf")], [R("idf")], [lambda e: e.affine_select(T.idf[:, :], T.idf[:, :], [[-1, 128]], A.is_equal, 0.0, 0, 1)])
    op("g", [R("bo")], [R("ltm")], [lambda e: e.affine_select(T.ltm[:, :], T.bo[:, :], [[1, 128]], A.is_ge, 0.0, 0, -1)])
    iof("krow", 0, 256, [[1, 256]], 0)
    iof("tg", 0, 256, [[0, 16], [1, 16]], 0)
    ts(R("pid", 1, 2), R("pid", 0, 1), 15, A.bitwise_and)
    fill(R("z0"), 0.0)
    ts(R("pid", 2, 3), R("pid", 1, 2), 1, A.logical_shift_right)
    cp(R("ci", 0, 1), R("pid", 1, 2))
    cp(R("ci", 1, 2), R("pid", 2, 3))
    I1, I2 = R("ci", 0, 1), R("ci", 1, 2)
    ROW = {"l": 4, "r": 2, "b": 0}
    XIN = (("b", 320), ("l", 0), ("r", 160))
    for x, c in XIN:
        cp(R("px0", c, c + 160), R("xin", c, c + 160))
    for x, c in XIN:
        halves("px0", c, c + 160, "hi", "lo", c)
    for x, c in XIN:
        for k, src in enumerate(("hi", "lo")):
            p2f("win", ROW[x] + k, S0, src, c, 160, "sy"[k])
    fill(R("ew", 0, S0), 0.0)
    ts(R("sa"), R("sin"), float(S0), A.add)
    cp(R("su"), R("sa", 16, 32))
    ts(R("mk"), R("cc", 0, 16), I1, A.is_equal)
    ts(R("mk2"), R("cc", 0, 8), I2, A.is_equal)
    cp(R("z0", 15, 143, 16), R("bo", 0, 128, 16))
    ts(R("ci", 6, 7), R("mk", 15, 16), 4.0 * S0, A.mult)
    cp(R("z0", 159, 287, 16), R("bo", 0, 128, 16))
    cp(R("z0", 160, 288, 16), R("bo", 0, 128, 16))
    cp(R("z0", 303, 431, 4), R("bo", 0, 128, 4))
    ts(R("zc", 0, 5), R("mk2", 0, 5), R("ci", 6, 7), A.add)
    for k, f, b in ((11, 160.0, 0), (12, 192.0, 0), (13, 224.0, 0), (14, 64.0, P0), (5, 8.0, GH)):
        ts(R("ci", k, k + 1), I1, f, A.mult, float(b), A.add)
    Z1, Z2, Z4 = R("z0", 0, 144), R("z0", 144, 288), R("z0", 288, 432)

    def zmat(z, col, src=Z1):
        act(ZR(z), src, col)
    gat("s", R("x0"), R("ew", 0, S0 + P0), R("su"))
    send("x0", 0, "x0", "ew", GC, 128)
    for z, k in (("zB16", 0), ("zL16", 2), ("zR16", 1)):
        zmat(z, R("zc", k, k + 1))
    ts(R("ci", 7, 8), R("mk", 0, 1), 3840.0, A.mult)
    cp(R("sn"), R("sin", 16, 32))
    ts(R("snf"), R("win", M - 416, M), 0.0, A.mult, R("ci", 7, 8), A.add)

    def slots(t):
        halves("sn", 0, 16, "meh", "mel", 0, "v")
        for k, src in enumerate(("meh", "mel")):
            for s in range(2):
                p2f("snf", k, 16 + 144 * s, src, 8 * s, 8)
        act(R("mme", 160 + 32 * t, 176 + 32 * t), R("sn"), float(M), -float(S0 * t))
    slots(0)
    load("y", R("wti", 0, 1), T.wt[:, :])
    load("y", R("wti", 1, 2), T.th[:, :])
    load("y", R("eo", 0, DA[0]), T.err[:, P0 - DA[0]:P0])
    ts(R("me"), R("cc", 0, 192), 16.0, A.mult, I1, A.add)
    tt(R("zc", 8, 9), R("mk", 14, 15), R("mk", 15, 16), A.subtract)
    ts(R("zc", 8, 9), R("mk2", 0, 1), float(M), A.mult, R("zc", 8, 9), A.add)
    ts(R("gi"), R("gi"), R("mk", 14, 15), A.mult)
    ts(R("mme", 0, 160), R("me", 0, 160), float(M), A.mult)
    for z, k in (("zL", 2), ("zR", 1), ("zB", 0), ("zE", 3), ("zN0", 5), ("zN1", 6)):
        ts(ZR(z), Z1, R("mk2", k, k + 1), A.mult)

    def early(k):
        if k == 0:
            zmat("zMB", R("zc", 8, 9))
            act(R("me16"), R("me"), 1.0, float(S0))
            cp(R("ml"), R("cc"))
            for j, (a, b) in enumerate(((0, 160), (160, 352), (352, 576), (576, 640))):
                act(R("mh", a, b), R("cc", 0, b - a), 0.0, R("ci", 11 + j, 12 + j), F.Identity)
            iof("msk", 0, 2304, [[0, 768], [256, 3]], 0)
            ts(R("nid"), R("idf"), -1.0, A.mult)
        if k == 1:
            fill(R("ew", S0 + P0, GC), 0.0)
            for w in ("ew", "w1", "uw"):
                fill(R(w, M, M + 16), 0.0)
            for w in ("w1", "uw"):
                fill(R(w, 0, S0), 0.0)
                dma("y", R(w, S0 + P0, GC), R("ew", S0 + P0, GC), T[w][:, S0 + P0:GC], T.ew[:, S0 + P0:GC])
        if k == 2:
            ts(R("zc", 5, 6), R("mk", 14, 15), 2.0 * KR, A.mult, R("zc", 1, 2), A.add)
            cp(R("ci", 8, 10), R("wti"))
            ts(R("zc", 5, 6), R("mk", 10, 11), -0.5, A.mult, R("zc", 5, 6), A.add)
            tt(R("zc", 4, 5), R("zc", 1, 2), R("mk", 8, 9), A.add)
            ts(R("ci", 10, 11), R("ci", 9, 10), -1.0, A.mult, 0.5, A.add)
            for z, f, src in (("zz", 1.0, Z1), ("q1", 1.0, Z4), ("q16", 16.0, Z4), ("d1", 1.0, Z2), ("d16", 16.0, Z2), ("d256", 256.0, Z2)):
                ts(ZR(z), src, f, A.mult)

    def later(k):
        if k == 0:
            act(R("kj"), R("cc", 0, 32), 8.0, I2, F.Identity)
            act(R("xs", 0, 16), R("me", 0, 16), 1.0, float(GC))
            act(R("xs", 16, 32), R("xs", 16, 32), 1.0, R("ci", 5, 6), F.Identity)
            act(R("nj", 32, 64), R("me", 0, 32), 1.0, float(P0))
        else:
            zmat("zT16", R("zc", 4, 5))
            zmat("zX", R("zc", 5, 6))
            zmat("zh", R("ci", 8, 9))
            act(R("dj"), R("me", 0, 32), 1.0, float(M))
            act(R("dl", 2048, 2064), R("cc", 0, 16), 0.0, -128.0)
            act(R("dl", 0, 2048), R("dh", 0, 2048), 1.0, -256.0)

    def newrows(t):
        zero("nc%d" % t, 0, 512)
        hi, b = 1024 + 1024 * t, P0 + 512 * t
        iof("it", hi, hi + 512, [[32, 16], [0, 32]], b)
        iof("it", hi + 512, hi + 1024, [[32, 16], [0, 16]], b, 2)
        iof("it", hi + 513, hi + 1024, [[-32, 16], [0, 16]], -b, 2)
        if t == 0:
            iof("it", 0, 512, [[0, 16], [1, 32]], 0)
            iof("it", 512, 1024, [[0, 16], [2, 16]], 0, 2)
            iof("it", 513, 1024, [[0, 16], [-2, 16]], -1, 2)

    def newrows2(t):
        hi = 1024 + 1024 * t
        for row, c in ((10 + 2 * t, hi), (11 + 2 * t, 0), (2 * t, hi + 512), (2 * t + 1, 512)):
            out = R("nc%d" % t, 0, 512, 1, row)
            dma("y", out, R("it", c, c + 512), ap(out), T.it[0:8, c:c + 512])

    def blk(k):
        return int(k) - RN0 + S0

    WIN = R("win")
    for t in range(2):
        m = 160 + 32 * t
        n, w = 16 * m, m + 32
        base, d, nsb = n, DA[t], m // 16
        px = "px%d" % t
        PL, PR, PB = R(px, 0, m), R(px, m, 2 * m), R(px, 2 * m, 3 * m)
        ca = m - d // 16
        cut = [0, CUT[t][0], CUT[t][1], ca]
        CH = [(cut[2], ca), (0, cut[1]), (cut[1], cut[2])]
        PC = [(cut[2], m + 16), (0, cut[2])]
        EW, W1, UW = R("ew"), R("w1"), R("uw")

        def sl(buf, a, b, k):
            return R(buf, 48 * a + k, 48 * b, 3)
        L = R

        def col(buf, a, b):
            return R(buf, S0 + 16 * a, S0 + 16 * b)

        def own(k):
            gcp(sl("za", *CH[k], 2), col("ew", *CH[k]), 16 * (CH[k][1] - CH[k][0]))
        if t == 0:
            gat("s", R("gs", 0, 256), R("win", 0, S0 + n), R("sa", 0, 16))
            gat("s", R("win", S0 + n, S0 + n + 256), R("win", 0, S0 + n), R("su"))
            f2p("ps3", 0, 16, "c", [("zB16", "gs", 0)])
            sendbases(0, "ps3")
            cp(R("bt", 0, 16), R("ps3", 0, 16))
            early(0)
            for k in range(3):
                own(k)
            later(0)
        for k, (a, b) in enumerate(PC):
            for j in range(2):
                f2p("ps%d" % (2 * k + j), 0, b - a, "i", [((("zL16", "zR16"), ("zB", "zE"))[t][j], (TLR[j] if t else "win"), S0 + 16 * a)])
        if t:
            gat("s", R("x0"), R("ew", 0, GC), R("su"))
            send("x0", 1, "x0", "ew", GC, 128)
            copy(R("eo", 0, d), col("ew", ca, m))
            newrows2(1)
            for k in range(2):
                own(k)

        def ghosts():
            arrived("be", t, "bel%d" % t, 0, 8)
            gat2(R("win", GC, M), R("snf"), R("bel%d" % t), R("gi"), A.add)
        VB = ("ps4", "ps5", "ps6", "ps7")

        def lists(k, j):
            (a, b), x, ps = PC[k], "lr"[j], "ps%d" % (2 * k + j)
            ts(R(x + "v", a, b), R(ps, 0, b - a), float(S0 * t), A.add)
            tt(R(x + "m", a, b), R(ps, 0, b - a), R("mme", a, b), A.subtract)
            f2p(VB[2 * k + j], 0, b - a, "i", [], (("idf", R(x + "m", a, b)),), last=False)
        if t:
            ghosts()
        lists(0, 0)
        if t == 0:
            early(1)
            lists(0, 1)
            early(2)
            ghosts()

        def legs(k, x):
            a, b = PC[k]
            ps = VB[2 * k + (x == "r")]
            f2p(ps, 0, b - a, "i", [("zMB", "g" + x, 16 * a)], first=False)
            ts(R(x + "w", a, b), R(ps, 0, b - a), float(M), A.min)
        for k, (a, b) in enumerate(PC):
            if k == 0 and t:
                gat("v", R("gl", 16 * a, 16 * a + 384), WIN, R("lv", a, a + 24))
                lists(0, 1)
            c = a + 24 * (k == 0 and t)
            gat("v", R("gl", 16 * c, 16 * b), WIN, R("lv", c, b))
            gat("s", R("gr", 16 * a, 16 * b), WIN, R("rv", a, b))
            if k == 0:
                lists(1, 0)
                lists(1, 1)
        legs(0, "l")
        legs(0, "r")
        XL, XR = R("lw", m, m + 16), R("rw", m, m + 16)

        def three(win, own, slots_, out, dst, side):
            for k, (a, b) in enumerate(CH):
                gat("s", sl(slots_, a, b, 0), win, L("lw", a, b))
                gat("s", sl(slots_, a, b, 1), win, L("rw", a, b))
                if k == 0:
                    side(0)
                    gat2(R("ta", 0, d), win, L("lw", ca, m), own, A.max)
                    side(1)
            for k, (a, b) in enumerate(CH):
                u, v = 48 * a, 48 * b
                scan(R(out, u, v), R("msk", 0, v - u), R(slots_, u, v), A.min, A.max)
                if k < 2:
                    gcp(col(dst, a, b), sl(out, a, b, 2), 16 * (b - a))
                else:
                    cp(col(dst, a, b), sl(out, a, b, 2))
                if k == 0:
                    gat2(col(dst, ca, m), win, L("rw", ca, m), R("ta", 0, d), A.max)
                    side(2)
                side(3 + k)

        arrived("x0", t, "ew", GC, 128)
        gat2(R("xa"), EW, XL, R("x0"), A.max)
        gat2(R("x1"), EW, XR, R("xa"), A.max)
        send("x1", t, "x1", "w1", GC, 128)
        if t == 0:
            load("y", R("dr"), T.det[:, :])
            for x, a, b in (("nb", 0, M + 16), ("zab", ZB + 3 * (n - d), blk(KL) + 3072)):
                for c in range(a, b, 1024):
                    e = min(1024, b - c)
                    copy(R(x, c, c + e), R("ew", S0 + P0, S0 + P0 + e))
        else:
            own(2)

        def side1(k):
            if k < 2:
                legs(1, "lr"[k])
            if k == 2:
                f2p("ps2", 0, m, "i", [("zB16", "win", S0)])
            if k == 3:
                ts(R("bv", 0, m), R("ps2", 0, m), float(GC - 1), A.min)
                tt(R("gt", 0, m), R("ps2", 0, m), R("me16", 0, m), A.is_gt)
        three(EW, R("eo", 0, d), "za", "zb", "w1", side1)
        mh, ml = R("mh", 160 * t, 160 * t + m), R("ml", 0, m)
        g3 = (0,) + G3[t] + (m,)

        def bases(k):
            if g3[k] < g3[k + 1]:
                gat("s", R("gb", 16 * g3[k], 16 * g3[k + 1]), WIN, R("bv", g3[k], g3[k + 1]))
        bases(0)
        for k, z in enumerate(("zL", "zR", "zB")):
            f2p("ps%d" % (4 + k), 0, m, "c", [(z, "gr", 0)], (("nid", mh), ("nid", ml)))
            if k == 0:
                for j, x in enumerate("lrb"):
                    if t:
                        unfold("win", ROW[x], S0, m, j, "ps%d" % j, 0)
                    elif j < 2:
                        f2p("ps3", 32 + 16 * j, 16, "c", [(("zL16", "zR16")[j], "gs", 0)])
                    else:
                        o = 144 * ZN.index("zB") + 15
                        op("t", [R("snf"), ZR("zB")], [R("ps3")],
                           [lambda e, i=i, c=16 + 144 * (i // 8) + i % 8: e.matmul(T.ps3[:, 64:80], T.z[:, o - i:o - i + 128], T.snf[:, c:c + 128:8], i == 0, i == 15)
                            for i in range(16)])
        arrived("x1", t, "w1", GC, 128)
        gat("v", R("xa"), W1, XL)
        gat2(R("x2"), W1, XR, R("xa"), A.max)
        send("x2", t, "x2", "uw", GC, 128)
        if t == 0:
            newrows(0)
        c2 = list(range(0, m + 1, 32))
        for k, (a, b) in enumerate(zip(c2[:-1], c2[1:])):
            gat("s", R("tr", 16 * a, 16 * b), W1, L("rw", a, b))
            gat2(col("uw", a, b), W1, L("lw", a, b), R("tr", 16 * a, 16 * b), A.max)
        bases(1)
        pl, pr, pb = (R("ps%d" % j, 0, m) for j in (4, 5, 6))
        ts(R("ek", 0, m), pr, 0.0, A.is_equal, KR, A.mult)
        ts(pl, pl, 0.0, A.is_equal, KL, A.mult)
        tt(R("kh", 0, m), pl, R("ek", 0, m), A.max)
        if t == 0:
            for k, (src, a, b) in enumerate((("mh", 352, 576), ("ml", 0, 0))):
                p2f("win", 6 + k, S0, src, a, 224)
                for row in (0, 2, 4):
                    p2f("win", row + k, S0 + P0, src, b, 64)
            ts(R("dm"), R("tg"), I1, A.is_le, BIG, A.mult)
            cp(R("bt", 32, 64), R("ps3", 32, 64))
            cp(R("sb", 0, 32, 2), R("sa", 0, 16))
            ts(R("sb", 1, 32, 2), R("ps3", 64, 80), float(S0), A.add)
            cp(R("bt", 64, 80), R("rv", m, m + 16))
        f2p("ps3", 0, g3[2], "i", [("zB", "gb", 0)])
        arrived("x2", t, "uw", GC, 128)

        def side3(k):
            if k == 2:
                copy(R("eo", 0, d), col("w1", ca, m))
                ts(pb, pb, 0.0, A.is_equal, KB, A.mult)
            if k == 3:
                tt(R("kh", 0, m), pb, R("kh", 0, m), A.max)
            if t == 0 and k == 1:
                tt(R("srf"), R("bt", 48, 80), R("xs"), A.is_equal)
                tt(R("ab"), R("bt", 48, 64), R("bt", 32, 48), A.subtract)
                tt(R("bt", 32, 48), R("bt", 32, 48), R("bt", 0, 16), A.subtract)
            if t == 0 and k == 2:
                tt(R("ab"), R("ab"), R("srf", 0, 16), A.mult)
            if t == 0 and k == 3:
                tt(R("ab"), R("ab"), R("bt", 32, 48), A.add)
        three(UW, col("w1", ca, m), "zb", "za", "w1", side3)
        bases(2)
        for row, src in ((8, "kh"), (10, "ek")):
            p2f("win", row, S0, src, 0, m)
        if t == 0:
            newrows2(0)
            for x, a in (("cb", 1), ("cw1", 0), ("cw2", 0)):
                iof(x, a, SCRATCH[x][1][1], [[0, SCRATCH[x][1][1] - a]], int(BIG))
            zero("cb", 0, 1)
            zero("inv", 0, 32)
        if t == 0:
            act(R("dh", 0, 2048), R("dr"), 0.5, 127.8)
        else:
            for k in range(3):
                act(R(px, m * k, m * k + m), R("ps%d" % k, 0, m), -1.0)
        f2p("ps3", g3[2], m - g3[2], "i", [("zB", "gb", 16 * g3[2])])
        HC = CH + [(ca, m)]
        for k, (a, b) in enumerate(HC):
            hb = R("hb", 16 * a, 16 * b)
            gat2(hb, R("w1", 0, GC), R("bv", a, b), sl("za", a, b, 2) if k < len(CH) else R("eo", 0, d), A.max)
            if k == 1:
                tt(R("ps3", 0, m), R("ps3", 0, m), R("me", 0, m), A.is_equal)
            if k < len(HC) - 1:
                act(hb, hb, 1.0, R("ci", 10, 11), F.Sign)
            else:
                ts(hb, hb, R("ci", 9, 10), A.is_ge, 2.0, A.mult)
            f2p("ps4" if k < 3 else "ps5", a, b - a, "i", [("zz", "hb", 16 * a)])
            if k == 2:
                tt(R("gt", 0, m), R("ps3", 0, m), R("gt", 0, m), A.mult)
                act(R("thr", 0, ca), R("gt", 0, ca), -103.0, 99.0)
                act(R("thr", ca, m), R("gt", ca, m), -87.0, 99.0)
        for ps, u, v in (("ps4", 0, ca), ("ps5", ca, m)):
            tt(R("hot", u, v), R(ps, u, v), R("thr", u, v), A.is_ge)
        op("t", [R("bo"), R("hot", 0, m)], [R("ps1")], [lambda e: e.matmul(T.ps1[:, 0:m], T.bo[:, :], T.hot[:, 0:m], True, True)])
        op("t", [R("ltm"), R("hot", 0, m)], [R("ps0")], [lambda e: e.matmul(T.ps0[:, 0:m], T.ltm[:, :], T.hot[:, 0:m], True, True)])
        scan(R("cb", 1, m + 1), R("ps1", 0, m), R("msk", 0, 3 * m, 3), A.add, A.max)
        scan(R("cs", 0, nsb + 1), R("dm", 0, nsb + 1), R("cb", 16, m + 17, 16), A.add, A.min)
        ts(R("m0"), R("krow"), R("cs", nsb, nsb + 1), A.is_ge)
        f2p("ps2", 0, 64, "q", [("q16", "m0", 0)])
        f2p("ps3", 0, 64, "q", [("q16", "m0", 0)], last=False)
        f2p("ps4", 0, 32, "d", [("d256", "m0", 0)], last=False)
        scan(R("cw1", 1, m + 1), R("dm", 0, m), R("cb", 1, m + 1), A.add, A.min)
        for k in (KL, KR, KB):
            for row in (10 + 2 * t, 11 + 2 * t):
                o = R("zab", blk(k), blk(k) + n, 1, row)
                dma("ys"[row % 2], o, R("nb", 0, n, 1, 4), ap(o), T.nb[4::16, 0:n])
        act(R("pre", 192, 192 + m), PR, 1.0, -1.0)
        if t == 0:
            later(1)
        else:
            act(R("nj", 32, 64), R("me", 0, 32), 1.0, float(base))

        def pick(lst, ps):
            scan(R("pk"), R("dm", 0, 256, 4), R(ps, 0, 64), A.add, A.min)
            cp(R(lst), R("pk", 3, 64, 4))
        ts(R("inv", 32, 64), R("kj"), R("cb", m, m + 1), A.is_ge)
        pick("l1", "ps2")
        gat2(R("m1"), R("cw1", 16, 224), R("l1"), R("krow"), A.is_le)
        f2p("ps3", 0, 64, "q", [("q1", "m1", 0)], first=False)
        tt(R("cw2", 0, m), R("ps0", 0, m), R("cb", 0, m), A.add)
        tt(R("aj"), R("inv", 32, 64), R("me", 0, 32), A.mult)
        f2p("ps4", 0, 32, "d", [("d16", "m1", 0)], (("idf", R("aj")),), first=False, last=False)
        pick("l2", "ps3")
        gat2(R("m2"), R("cw2"), R("l2"), R("krow"), A.is_le)
        f2p("ps4", 0, 32, "d", [("d1", "m2", 0)], first=False)
        act(R("inv", 32, 64), R("inv", 32, 64), 4096.0)
        ts(R("td"), R("ps4", 0, 32), float(S0), A.add)
        gat("s", R("g1"), WIN, R("td"))
        f2p("ps5", 0, 32, "i", [(("zE", "zB"), "g1", 0)])
        EQ = [R("eq", 192 * k, 192 * k + m) for k in range(3)]
        tt(EQ[0], PL, PR, A.is_equal)
        tt(EQ[1], PL, PB, A.is_equal)
        tt(EQ[2], PR, PB, A.is_equal)
        if t == 0:
            act(R("mme", 0, 192), R("me"), float(M), -float(S0))
        ts(R("tu"), R("ps5", 0, 32), float(S0), A.add)
        nc, zn = R("nc%d" % t), "zN%d" % t
        gat("s", R("gq"), WIN, R("tu"))
        gat("s", R("eg"), R("ew", 0, GC), R("tu"))
        sca(R("nb"), R("tu"), nc)
        for k in range(0 if t else 2, 3):
            unfold("gq", (0, 6, 2)[k], 0, 32, k, None, 0, 1)
        if t:
            act(R("e2"), R("eg"), 0.5, 127.8)
        else:
            gat("s", R("gsn"), R("nb"), R("sb"))
            for tab in TLR:
                copy(R(tab, S0 + n, S0 + n + 512), R("gq"))
            for row, src in ((4, 0), (5, 1), (2, 6), (3, 7)):
                copy(R("win", S0 + n, S0 + n + 512, 1, row), R("gq", 0, 512, 1, src))
        f2p("ps6", 0, 32, "i", [("zT16", "gq", 0)])
        f2p("ps0", 0, m, "c", [(("zB", "zR")[t], "nb", S0)])
        act(R("nj", 0, 32), R("ps5", 0, 32))
        tt(R("tq"), R("ps6", 0, 32), R("dj"), A.max)
        ts(R("ru"), R("tq"), -float(RN0), A.add)
        sca(R("zab"), R("ru"), nc)
        NS, SP, E1 = R("ps6", 64, 64 + m), R("ps6", 288, 288 + m), R("ps5", 64, 64 + m)
        N0, NP = R("ps1", 0, m), R("ps1", 256, 256 + m)
        act(N0, R("ps0", 0, m), 1.0, 0.0, F.Abs)
        act(NS, N0, -1.0, 1.0, F.Relu)
        act(SP, N0, 1.0, 0.0, F.Sign)
        act(NP, R("ps0", 0, m), 1.0, 1.0, F.Abs)
        act(R("m8", 0, m), SP, 8192.0)
        M8 = (("nid", R("m8", 0, m)),)

        def new(k, a=0, b=m):
            return R("po", w * k + a, w * k + b) if t else R("ps%d" % (2 + k), 256 + a, 256 + b)

        def renamed(k, kb, z, minus):
            f2p("ps%d" % (2 + k), 0, m, "c", [(zn, "zab", blk(kb))], minus)
            if k < 2 and t:
                unfold("gq", 0, 0, 32, k, "ps%d" % (2 + k), 256 + m, 2)

        def childto(k):
            if t:
                act(new(k, m, w), R("ps%d" % (2 + k), 256 + m, 256 + w), -1.0)

        def detlists():
            for k in range(2):
                tt(R("di", 32 * k, 32 * k + 32), R("ps5" if t else "ps7", 320, 352), R("nj", 32 * k, 32 * k + 32), A.add)
            ts(R("da"), R("di"), 2047, A.bitwise_and)
            tt(R("dq"), R("da"), R("inv"), A.add)
            ts(R("du"), R("dq"), 2048.0, A.min)

        def children():
            sca2(R("ew", 0, GC), R("tu"), R("e2"), R("dg"))
            if t:
                dma("y", None, R("ew", S0, S0 + n), T.ye[:, 0:n], T.ew[:, S0:S0 + n])

        def right(k):
            if k == 0:
                gat("s", R("g1"), R("dl"), R("du", 32, 64))
            if k == 1:
                f2p("ps7", 0, 512, "c", [], (("nid", R("e2")), ("nid", R("g1"))))
            if k == 2:
                act(R("ew", S0 + n, S0 + n + 512), R("ps7"), -1.0)
            if k == 2 and t:
                dma("s", None, R("ew", S0 + n, GC), T.ye[:, n:GH], T.ew[:, S0 + n:GC])

        def border():
            ts(R("sw", 0, 16), R("ps7", 160, 176), 1.0, A.min)
            tt(R("sw", 16, 32), R("ps7", 176, 192), R("srf", 16, 32), A.mult)
            tt(R("ab"), R("ab"), R("sw", 0, 16), A.mult)
            tt(R("sn"), R("sn"), R("sw", 16, 32), A.max)
            tt(R("bt", 0, 16), R("bt", 0, 16), R("ab"), A.add)
            slots(1)
            sendbases(1, "bt")
            newrows(1)
            ts(R("su"), R("sn"), float(S0), A.add)
        if t:
            f2p("ps5", 320, 32, "i", [("zh", "eg", 0)])
            detlists()
        else:
            f2p("ps7", 160, 32, "c", [(zn, "gsn", 0)])
            border()
        renamed(0, KL, "zB", ())
        f2p("ps0", 64, 32, "i", [("zX", "gq", 0)])
        if t:
            gat("s", R("dg"), R("dl"), R("du", 0, 32))
            right(0)
        else:
            act(R("e2"), R("eg"), 0.5, 127.8)
            f2p("ps7", 320, 32, "i", [("zh", "eg", 0)])
        renamed(1, KR, "zE", M8)
        q0, q1, q2 = (R("pre", 192 * k, 192 * k + m) for k in range(3))
        tt(q1, NS, q1, A.mult)
        tt(E1, NS, EQ[0], A.mult)

        def lastbase(k):
            if k == 0:
                return ts(R("xu"), R("ps0", 64, 96), float(M), A.min)
            gat("s", R("gn"), R("nb"), R("xu"))
            if t:
                right(1)
            unfold("gq", 0, 0, 32, 2, "ps0", 0, 2)
            f2p("ps0", 32, 32, "c", [(zn, "gn", 0)])
            renamed(2, KB, "zR", M8)

        def done(x, k):
            if t == 0:
                halves("ps%d" % (2 + k), 256, 256 + (m if k < 2 else w), "hi", "lo", w * k, "svv"[k])
                for tab, row in (((TLR[k], 6 * k), ("win", ROW[x])) if k < 2 else (("win", 0),)):
                    for j, src in enumerate(("hi", "lo")):
                        p2f(tab, row + j, S0, src, w * k, m, "sy"[j] if k < 2 else "y")
                        if k == 2:
                            p2f(tab, row + j, S0 + n, src, w * k + m, 32, "sy"[j])
            else:
                y = {"l": T.yl, "r": T.yr, "b": T.yb}[x]
                for a, b, src in ((0, n, new(k)), (n, GH, new(k, m, w))):
                    dma("s" if a else "y", None, src, y[:, a:b], ap(src))
        NL, NRm, NBm = R("ps2", 0, m), R("ps3", 0, m), R("ps4", 0, m)
        tt(PL, NL, PL, A.max)
        childto(0)
        tt(q1, NP, q1, A.add)
        if t:
            lastbase(0)
            lastbase(1)
        if t:
            children()
            right(2)
        tt(q0, NS, PL, A.mult)
        tt(E1, E1, PL, A.mult)
        tt(new(0), N0, q0, A.add)
        tt(q1, E1, q1, A.max)
        tt(SP, SP, EQ[1], A.max)
        if t == 0:
            lastbase(0)
        done("l", 0)
        if t == 0:
            lastbase(1)
            detlists()
            gat("s", R("dg"), R("dl"), R("du", 0, 32))
            act(R("tq"), R("ps0", 0, 32), -1.0)
        tt(E1, NRm, EQ[2], A.mult)
        tt(new(1), NRm, q1, A.max)
        childto(1)
        if t:
            act(R("tq"), R("ps0", 0, 32), -1.0)
        tt(q2, NS, PB, A.mult)
        tt(SP, SP, PL, A.mult)
        done("r", 1)
        if t == 0:
            right(0)
            right(1)
        tt(q2, E1, q2, A.max)
        tt(q2, SP, q2, A.max)
        tt(new(2, m, w), R("ps0", 32, 64), R("tq"), A.max)
        tt(new(2), NBm, q2, A.max)
        done("b", 2)
        if t == 0:
            for tab in TLR:
                e = S0 + 16 * w
                gat("s", R(tab, e, e + 256), R(tab, 0, e), R("su"))
            children()
            right(2)
    finish()
